import numpy as np
import ml_dtypes


def mxq(x, axis, fmt="e4m3"):
    dtype, down = {"e4m3": (ml_dtypes.float8_e4m3fn, 7), "e5m2": (ml_dtypes.float8_e5m2, 14)}[fmt]
    v = np.moveaxis(np.asarray(x, np.float32).astype(ml_dtypes.bfloat16).astype(np.float64), axis, -1)
    blocks = v.reshape(v.shape[:-1] + (-1, 32))
    amax = np.abs(blocks).max(-1, keepdims=True)
    byte = np.maximum(np.where(amax > 0, np.frexp(amax)[1] - 1 + 127, 0) - down, 1)
    scale = np.exp2(byte - 127.0)
    codes = (blocks / scale).astype(np.float32).astype(dtype).astype(np.float64)
    return np.moveaxis((codes * scale).reshape(v.shape), -1, axis)


WIDE = False


def mx_kscale(k):
    if not WIDE:
        return np.ones(k)
    levels = np.array([24, -24, 12, -12, 0])
    if k % 512:
        return np.exp2(np.random.permutation(np.resize(levels, k // 32))).repeat(32)
    a = np.empty((k // 512, 16))
    for p in range(k // 512):
        a[p, :8] = np.random.permutation(np.resize(levels, 8))
        for g in range(8):
            far = levels[np.abs(levels - a[p, g]) >= 10]
            a[p, g + 8] = far[np.random.randint(len(far))]
    return np.exp2(a.ravel()).repeat(32)


def f64(x):
    return np.asarray(x).astype(np.float64)


def striped(idx):
    return np.tile(idx.reshape(-1, 16).T, (8, 1)).astype(np.uint16)


def unstriped(offs):
    return offs[:16].T.reshape(-1).astype(np.int64)


E2M1 = np.array([0.0, 0.5, 1.0, 1.5, 2.0, 3.0, 4.0, 6.0, -0.0, -0.5, -1.0, -1.5, -2.0, -3.0, -4.0, -6.0])


def pack_weight(w, fmt):
    k, n = w.shape
    w = f64(np.asarray(w, np.float32).astype(ml_dtypes.bfloat16)).reshape(k // 32, 32, n)
    amax = np.abs(w).max(1)
    if fmt == "e4m3":
        byte = np.frexp(amax)[1] - 1 + 127 - 7
    else:
        mant, ex = np.frexp(amax / 6.0)
        byte = np.where(mant > 0.5, ex, ex - 1) + 127
    byte = np.clip(np.where(amax > 0, byte, 1), 1, 254)
    scaled = (w * np.exp2(127.0 - byte)[:, None, :]).reshape(k, n).astype(np.float32)
    by_word = np.ascontiguousarray(scaled.reshape(k // 512, 128, 4, n).transpose(0, 1, 3, 2))
    if fmt == "e4m3":
        words = by_word.astype(ml_dtypes.float8_e4m3fn).view(np.uint8)
    else:
        c = by_word.astype(ml_dtypes.float4_e2m1fn).view(np.uint8) & 0xF
        words = (c[..., 0::2] | (c[..., 1::2] << 4)).reshape(k // 512, 128, 2 * n)
    return np.ascontiguousarray(words), np.ascontiguousarray(byte.astype(np.uint8).reshape(k // 512, 16, n))


def unpack_weight(words, scales, fmt):
    g, _, n = scales.shape
    words = np.ascontiguousarray(words).reshape(g, 128, n, -1)
    if fmt == "e4m3":
        vals = words.view(ml_dtypes.float8_e4m3fn).astype(np.float64)
    else:
        nib = np.empty((g, 128, n, 4), np.uint8)
        nib[..., 0::2] = words & 0xF
        nib[..., 1::2] = words >> 4
        vals = E2M1[nib]
    vals = vals * np.repeat(np.exp2(scales.astype(np.float64) - 127.0), 8, axis=1)[..., None]
    return vals.transpose(0, 1, 3, 2).reshape(g * 512, n)


def pack_table4(v):
    words, scales = pack_weight(v, "e2m1")
    g, t = words.shape[0] // 2, v.shape[1]
    return np.ascontiguousarray(words.reshape(g, 2, 128, t, 2).transpose(0, 2, 3, 1, 4).reshape(g, 128, t, 4)), scales


def unpack_table4(words, scales):
    g, _, t, _ = words.shape
    return unpack_weight(words.reshape(g, 128, t, 2, 2).transpose(0, 3, 1, 2, 4).reshape(2 * g, 128, 2 * t), scales, "e2m1")


K, L, N, T, J = 1024, 512, 1024, 4096, 2048


def setup_inputs():
    n = np.random.standard_normal
    s = mx_kscale(K)[:, None]
    s2 = mx_kscale(L)[:, None]
    p_tab = pack_table4(n((K, T)) * s)
    p_wx = pack_weight(n((L, N)) / np.sqrt(L) / s2, "e2m1")
    return {
        "tab_words": p_tab[0],
        "tab_scales": p_tab[1],
        "wt": (n((K, N)) / np.sqrt(K) / s).astype(np.float32),
        "x": (n((L, J)) * s2).astype(np.float32),
        "wx_words": p_wx[0],
        "wx_scales": p_wx[1],
        "b": (0.3 * n(N)).astype(np.float32),
        "offs": striped(np.random.permutation(T)[:J]),
    }


def reference(tab_words, tab_scales, wt, x, wx_words, wx_scales, b, offs):
    idx = unstriped(offs)
    tab_ = unpack_table4(tab_words, tab_scales)[:, idx]
    wt_ = mxq(f64(wt), 0, "e4m3")
    x_q_ = mxq(f64(x), 0, "e4m3")
    x_r_ = mxq(f64(x) - x_q_, 0, "e4m3")
    wx_ = unpack_weight(wx_words, wx_scales, "e2m1")
    y = wt_.T @ tab_ + wx_.T @ x_q_ + wx_.T @ x_r_
    return y + f64(b)[:, None]

@@ -1,0 +1,354 @@
+from contextlib import ExitStack
+
+import concourse.mybir as mybir
+
+K, L, N, T, J = 1024, 512, 1024, 4096, 2048
+FLOPS = 2 * K * N * J + 2 * 2 * L * N * J + 2 * L * L * J
+
+F32 = mybir.dt.float32
+BF16 = mybir.dt.bfloat16
+I32 = mybir.dt.int32
+U32 = mybir.dt.uint32
+U16 = mybir.dt.uint16
+U8 = mybir.dt.uint8
+FP8X4 = mybir.dt.float8_e4m3fn_x4
+FP4X4 = mybir.dt.float4_e2m1fn_x4
+IDENT = mybir.ActivationFunctionType.Identity
+SUB = mybir.AluOpType.subtract
+
+P = 128
+PACK = 4
+W = 512
+RUN = 4
+CHUNKS = J // W
+SUBS = W // P
+KIB = 1024
+
+V_SHARE = {'x0': 256, 'w00': 0, 'w10': 192, 'w01': 0, 'w11': 192, 'x1': 128, 'x2': 256, 'x3': 0}
+
+
+def tile_list_tiert_bias_kernel(
+    tc, tab_words, tab_scales, wt, x, wx_words, wx_scales, b, offs, out
+):
+    nc = tc.nc
+    with ExitStack() as ctx:
+        keep = ctx.enter_context(tc.tile_pool(name="keep", bufs=1))
+        outp = ctx.enter_context(tc.tile_pool(name="outp", bufs=3))
+        psum = ctx.enter_context(tc.psum_pool(name="psum", bufs=8))
+
+        def kept(shape, dtype, name):
+            return keep.tile(shape, dtype, name=name, align_bytes=64)
+
+        offsets = keep.tile([P, J // 16], U16, name="offsets")
+        tab_s = kept([P, 2, T // 4], I32, "tab_s")
+        wx_w = kept([P, N // 2], I32, "wx_w")
+        ident = kept([P, P], F32, "ident")
+        bias = kept([P, N // P], F32, "bias")
+        sel_c = kept([P, W], U32, "sel_c")
+        sel_s = kept([P, W], U8, "sel_s")
+        raw = {"x0": kept([P, PACK, W], F32, "x_raw0")}
+        halves = [(a, h) for a in range(2) for h in range(2)]
+        w_c = {k: kept([P, W], U32, "w_c%d%d" % k) for k in halves}
+        w_s = {k: kept([P, W], U8, "w_s%d%d" % k) for k in halves}
+        xq_c = [kept([P, W], U32, "xq_c%d" % c) for c in range(CHUNKS)]
+        xq_s = [kept([P, W], U8, "xq_s%d" % c) for c in range(CHUNKS)]
+        xr_c = [kept([P, W], U32, "xr_c%d" % c) for c in range(CHUNKS)]
+        xr_s = [kept([P, W], U8, "xr_s%d" % c) for c in range(CHUNKS)]
+        t_c = [kept([P, 2, 2 * W], U8, "t_c%d" % c) for c in range(CHUNKS)]
+
+        def load_x(c):
+            nc.sync.dma_start(raw["x%d" % c][:], x[:, c * W : (c + 1) * W].rearrange("(p i) j -> p i j", i=PACK))
+
+        def load_w(a, h):
+            rows = wt[a * W : (a + 1) * W, h * W : (h + 1) * W]
+            nc.sync.dma_start(raw["w%d%d" % (a, h)][:], rows.rearrange("(p i) n -> p i n", i=PACK))
+
+        def load(key, make):
+            if key == "tab":
+                raw[key] = make([P, T], I32, "tab_w", 16 * KIB)
+                nc.sync.dma_start(raw[key][:], tab_words[0].rearrange("p t y -> p (t y)").bitcast(I32))
+            else:
+                raw[key] = make([P, PACK, W], F32, "raw_" + key, 8 * KIB)
+                if key[0] == "w":
+                    load_w(int(key[1]), int(key[2]))
+                else:
+                    load_x(int(key[1]))
+
+        nc.vector.memset(tab_s[:], 0)
+        load_x(0)
+        nc.sync.dma_start(offsets[:], offs)
+        nc.sync.dma_start(wx_w[:], wx_words[0].bitcast(I32))
+        for q in (0, 2, 1, 3):
+            nc.sync.dma_start(
+                tab_s[32 * q : 32 * q + 4, :, :],
+                tab_scales[:, 4 * q : 4 * q + 4, :].bitcast(I32).rearrange("a r t -> r a t"),
+            )
+        with tc.tile_pool(name="zeros", bufs=1) as zeros:
+            blank = zeros.tile([P, P], F32, name="blank")
+            nc.vector.memset(blank[:], 0.0)
+            nc.gpsimd.affine_select(
+                out=ident[:], in_=blank[:], pattern=[[-1, P]], compare_op=mybir.AluOpType.not_equal,
+                fill=1.0, base=0, channel_multiplier=1,
+            )
+
+        second = ctx.enter_context(tc.tile_pool(name="second", bufs=1))
+        b_rows = second.tile([P, P], F32, name="b_rows", align_bytes=64)
+        wx_s = second.tile([P, N // 4], I32, name="wx_s", align_bytes=64)
+        nc.gpsimd.memset(b_rows[:], 0.0)
+        nc.gpsimd.memset(wx_s[:], 0)
+        for key in ('tab',):
+            load(key, lambda shape, dtype, name, room: second.tile(shape, dtype, name=name, align_bytes=64))
+        nc.sync.dma_start(b_rows[0 : N // P, :], b.rearrange("(c p) -> c p", p=P))
+        for q in (0, 2, 1, 3):
+            nc.sync.dma_start(wx_s[32 * q : 32 * q + 4, :], wx_scales[0, 4 * q : 4 * q + 4, :].bitcast(I32))
+
+        with tc.tile_pool(name="setup", bufs=1) as setup:
+            sel_in = setup.tile([P, PACK, P, PACK], BF16, name="sel_in", align_bytes=64)
+            nc.vector.memset(sel_in[:].rearrange("p t m i -> p (t m i)").bitcast(I32), 0)
+            for t in range(PACK):
+                nc.vector.tensor_copy(sel_in[:, t, :, t], ident[:])
+            nc.vector.quantize_mx(sel_c[:].bitcast(FP8X4), sel_s[:], sel_in[:].rearrange("p t m i -> p (t m i)"))
+
+        late = ctx.enter_context(tc.tile_pool(name="late", bufs=1))
+        place = {}
+        top = [0]
+
+        def placed(shape, dtype, name, room):
+            if name in AFTER:
+                prior, shift = AFTER[name]
+                place[name] = place[prior] + shift
+            else:
+                place[name] = top[0]
+                top[0] = top[0] + room
+            return late.tile(shape, dtype, name=name, align_bytes=64, offset=place[name])
+
+        AFTER = {'t_s10': ('rest0', 0), 't_s11': ('grp_w01', 0), 'g_w1': ('grp_w10', 0), 'res00': ('raw_w01', 0), 'res01': ('grp_x1', 0), 'res10': ('grp_x2', 0), 'res21': ('grp_x3', 0), 'g_w2': ('rest1', 0), 't_s20': ('rest1', 2048), 't_s21': ('rest1', 2560), 'g_w3': ('rest2', 0), 't_s30': ('rest2', 2048), 't_s31': ('rest2', 2560)}
+        for key in ('w00', 'w10', 'w01', 'w11', 'x1', 'x2', 'x3'):
+            load(key, placed)
+
+        def runs_out(tile, lo, hi):
+            return tile[:, lo:hi, :].rearrange("p (c r) i -> p c i r", r=RUN)
+
+        def runs_in(ap):
+            return ap.rearrange("p i (c r) -> p c i r", r=RUN)
+
+        def interleave(key):
+            if key == "x0":
+                grouped = kept([P, W, PACK], BF16, "grp_x0")
+            else:
+                grouped = placed([P, W, PACK], BF16, "grp_" + key, 8 * KIB)
+            v = V_SHARE[key]
+            if v > 0:
+                nc.vector.tensor_copy(runs_out(grouped, 0, v), runs_in(raw[key][:, :, 0:v]))
+            if v < W:
+                nc.scalar.activation(runs_out(grouped, v, W), runs_in(raw[key][:, :, v:W]), IDENT)
+            return grouped
+
+        def quantize(grouped, codes, scales):
+            nc.vector.quantize_mx(codes[:].bitcast(FP8X4), scales[:], grouped[:].rearrange("p j i -> p (j i)"))
+
+        def listed(c):
+            return offsets[:, c * (W // 16) : (c + 1) * (W // 16)]
+
+        g_w = {}
+        t_s = {}
+
+        def gather_scales(c, a):
+            t_s[c, a] = placed([P, W], U8, "t_s%d%d" % (c, a), W)
+            nc.vector.tensor_copy(t_s[c, a][:], tab_s[:, a, :].bitcast(U8).indirect(listed(c)))
+
+        def gather_words(c):
+            g_w[c] = placed([P, W], U32, "g_w%d" % c, 4 * W)
+            nc.vector.tensor_copy(g_w[c][:], raw["tab"][:].bitcast(U32).indirect(listed(c)))
+
+        def part_words(c):
+            nc.vector.tensor_copy(
+                t_c[c][:].bitcast(U16), g_w[c][:].bitcast(U16).rearrange("p (j d) -> p d j", d=2)
+            )
+
+        rests = {}
+
+        def residual(c, subs):
+            if c not in rests:
+                rests[c] = placed([P, W, PACK], BF16, "rest%d" % c, 4 * KIB)
+            rest = rests[c]
+            for s in subs:
+                cols = slice(s * P, (s + 1) * P)
+                dq = psum.tile([P, PACK, P], F32, name="bank")
+                for t in range(PACK):
+                    sel = slice(t * P, (t + 1) * P)
+                    nc.tensor.matmul_mx(
+                        dq[:, t, :],
+                        lhsT=sel_c[:, sel].bitcast(FP8X4),
+                        lhsT_scale=sel_s[:, sel],
+                        rhs=xq_c[c][:, cols].bitcast(FP8X4),
+                        rhs_scale=xq_s[c][:, cols],
+                        start=True,
+                        stop=True,
+                    )
+                nc.vector.tensor_tensor(
+                    runs_out(rest, s * P, (s + 1) * P), runs_in(raw["x%d" % c][:, :, cols]), runs_in(dq[:]), SUB
+                )
+
+        acc = {}
+        done = {}
+        stage = {}
+
+        def mm(kind, c, m):
+            if (c, m) not in acc:
+                acc[c, m] = psum.tile([P, W], F32, name="bank")
+                done[c, m] = 0
+            first, last = done[c, m] == 0, done[c, m] == 3
+            done[c, m] = done[c, m] + 1
+            if kind in ("q", "r"):
+                codes, scales = (xq_c, xq_s) if kind == "q" else (xr_c, xr_s)
+                lhsT = wx_w[:, 64 * m : 64 * (m + 1)].bitcast(FP4X4)
+                lhsT_s = wx_s[:, 32 * m : 32 * (m + 1)].bitcast(U8)
+                rhs, rhs_s = codes[c][:].bitcast(FP8X4), scales[c][:]
+            else:
+                h, cols = m // SUBS, slice((m % SUBS) * P, (m % SUBS + 1) * P)
+                lhsT, lhsT_s = w_c[kind, h][:, cols].bitcast(FP8X4), w_s[kind, h][:, cols]
+                rhs, rhs_s = t_c[c][:, kind, :].bitcast(FP4X4), t_s[c, kind][:]
+            nc.tensor.matmul_mx(
+                acc[c, m][:], lhsT=lhsT, lhsT_scale=lhsT_s, rhs=rhs, rhs_scale=rhs_s, start=first, stop=last
+            )
+            if last:
+                h = m // SUBS
+                if (c, h) not in stage:
+                    name = "res%d%d" % (c, h)
+                    if name in AFTER:
+                        stage[c, h] = placed([P, SUBS, W], F32, name, 8 * KIB)
+                    else:
+                        stage[c, h] = outp.tile([P, SUBS, W], F32, name="res")
+                res = stage[c, h][:, m % SUBS, :]
+                if (c, m) in ((3, 0), (3, 2), (3, 4), (3, 6), (0, 1), (0, 0), (0, 5), (3, 1), (1, 4), (2, 6)):
+                    nc.vector.tensor_scalar_add(res, acc[c, m][:], bias[:, m : m + 1])
+                else:
+                    nc.scalar.activation(res, acc[c, m][:], IDENT, bias=bias[:, m : m + 1])
+                nc.sync.dma_start(out[m * P : (m + 1) * P, c * W : (c + 1) * W], res)
+
+        def mms(kinds, c, ms):
+            for kind in kinds:
+                for m in ms:
+                    mm(kind, c, m)
+
+        def groups(kinds, c, ms):
+            for m in ms:
+                for kind in kinds:
+                    mm(kind, c, m)
+
+        def prep_w(a, h):
+            quantize(interleave("w%d%d" % (a, h)), w_c[a, h], w_s[a, h])
+
+        def first_tier(c):
+            quantize(interleave("x%d" % c), xq_c[c], xq_s[c])
+
+        def second_tier(c):
+            quantize(rests[c], xr_c[c], xr_s[c])
+
+        def make_bias():
+            b_ps = psum.tile([P, P], F32, name="bank")
+            nc.tensor.transpose(b_ps[:], b_rows[:], ident[:])
+            nc.scalar.activation(bias[:], b_ps[:, 0 : N // P], IDENT)
+
+        first_tier(0)
+        gather_scales(0, 0)
+        residual(0, (0, 1))
+        residual(0, (2, 3))
+        make_bias()
+        mms(('q',), 0, range(0, 2))
+        second_tier(0)
+        mms(('q',), 0, range(2, 4))
+        mms(('q',), 0, range(4, 6))
+        gather_scales(0, 1)
+        prep_w(1, 0)
+        mms(('r',), 0, range(0, 2))
+        mms(('r',), 0, range(2, 4))
+        mms(('r',), 0, range(4, 6))
+        gather_scales(1, 0)
+        prep_w(0, 0)
+        gather_words(0)
+        part_words(0)
+        gather_words(1)
+        mms((0,), 0, range(2, 4))
+        mms(('q',), 0, range(6, 8))
+        mms(('r',), 0, range(6, 8))
+        mms((0,), 0, range(0, 2))
+        prep_w(0, 1)
+        mms((1,), 0, range(2, 4))
+        prep_w(1, 1)
+        part_words(1)
+        mms((1,), 0, range(0, 2))
+        gather_scales(1, 1)
+        mms((0,), 0, range(4, 6))
+        first_tier(1)
+        mms((1,), 0, range(4, 6))
+        mms((0,), 1, range(0, 2))
+        mms((0,), 0, range(6, 8))
+        residual(1, (0, 1))
+        residual(1, (2, 3))
+        second_tier(1)
+        mms((1,), 0, range(6, 8))
+        mms((1,), 1, range(0, 2))
+        gather_words(2)
+        gather_scales(2, 1)
+        gather_scales(2, 0)
+        mms((1,), 1, range(2, 4))
+        first_tier(2)
+        part_words(2)
+        mms((0,), 1, range(2, 4))
+        mms(('r',), 1, range(0, 2))
+        mms(('q',), 1, range(0, 2))
+        mms(('q',), 1, range(2, 4))
+        mms(('r',), 1, range(2, 4))
+        mms((0,), 1, range(6, 8))
+        mms((0,), 1, range(4, 6))
+        mms((1,), 1, range(4, 6))
+        mms(('q',), 1, range(4, 6))
+        mms(('r',), 1, range(4, 6))
+        mms(('q',), 1, range(6, 8))
+        residual(2, (0, 1))
+        residual(2, (2, 3))
+        mms((1,), 1, range(6, 8))
+        mms(('r',), 1, range(6, 8))
+        second_tier(2)
+        mms((1,), 2, range(0, 2))
+        gather_words(3)
+        mms((0,), 2, range(0, 2))
+        mms((1,), 2, range(2, 4))
+        gather_scales(3, 0)
+        mms((0,), 2, range(2, 4))
+        gather_scales(3, 1)
+        part_words(3)
+        mms(('q',), 2, range(0, 2))
+        first_tier(3)
+        mms(('q',), 2, range(2, 4))
+        mms(('r',), 2, range(0, 2))
+        mms(('r',), 2, range(2, 4))
+        residual(3, (0, 1))
+        mms((0,), 2, range(4, 6))
+        mms(('r',), 2, range(4, 6))
+        residual(3, (2, 3))
+        mms((1,), 2, range(4, 6))
+        mms(('q',), 2, range(4, 6))
+        mms((1,), 3, range(0, 2))
+        second_tier(3)
+        mms((1,), 3, range(2, 4))
+        mms((1,), 2, range(6, 8))
+        mms(('q',), 2, range(6, 8))
+        mms((0,), 2, range(6, 8))
+        mms(('r',), 2, range(6, 8))
+        mms(('r',), 3, range(2, 4))
+        mms(('r',), 3, range(0, 2))
+        mms((1,), 3, range(4, 6))
+        mms((0,), 3, range(0, 2))
+        mms((0,), 3, range(2, 4))
+        mms(('q',), 3, range(0, 2))
+        mms((0,), 3, range(4, 6))
+        mms(('q',), 3, range(4, 6))
+        mms(('q',), 3, range(2, 4))
+        mms((0,), 3, range(6, 8))
+        mms((1,), 3, range(6, 8))
+        mms(('r',), 3, range(4, 6))
+        mms(('q',), 3, range(6, 8))
+        mms(('r',), 3, range(6, 8))

@@ -24,7 +24,8 @@ CHUNKS = J // W
 SUBS = W // P
 KIB = 1024
 
-V_SHARE = {'x0': 256, 'w00': 0, 'w10': 192, 'w01': 0, 'w11': 192, 'x1': 128, 'x2': 256, 'x3': 0}
+V_SHARE = {'x0': 320, 'w00': 128, 'w10': 0, 'w01': 192, 'w11': 512, 'x1': 512, 'x2': 128, 'x3': 384}
+RUNS = ((0, 1), (2, 3))
 
 
 def tile_list_tiert_bias_kernel(
@@ -39,14 +40,29 @@ def tile_list_tiert_bias_kernel(
         def kept(shape, dtype, name):
             return keep.tile(shape, dtype, name=name, align_bytes=64)
 
+        late = ctx.enter_context(tc.tile_pool(name="late", bufs=1))
+        place = dict({'raw_w00': 0, 'sel_in': 6144, 'raw_w10': 8192, 'raw_w11': 16384, 'rest0': 22528, 'raw_w01': 24576, 'tab_s': 32768})
+        top = [36864]
+
+        def placed(shape, dtype, name, room):
+            if name in AFTER:
+                prior, shift = AFTER[name]
+                place[name] = place[prior] + shift
+            elif name not in place:
+                place[name] = top[0]
+                top[0] = top[0] + room
+            return late.tile(shape, dtype, name=name, align_bytes=64, offset=place[name])
+
+        AFTER = {'t_s1': ('rest1', 0), 'res01': ('raw_w11', 0), 'res21': ('grp_x3', 0), 'grp_x2': ('grp_w11', 0), 'grp_x3': ('raw_x2', 0), 'g_w2': ('rest1', 1024), 'g_w3': ('rest2', 0), 'raw_x1': ('raw_w00', 0), 'raw_x2': ('raw_w10', 0), 'raw_x3': ('grp_w10', 0)}
         offsets = keep.tile([P, J // 16], U16, name="offsets")
-        tab_s = kept([P, 2, T // 4], I32, "tab_s")
+        tab_s = placed([P, T // 4], I32, "tab_s", 0)
+        low_s = [kept([P, len(cs) * W // 4], I32, "low_s%d" % g) for g, cs in enumerate(RUNS)]
         wx_w = kept([P, N // 2], I32, "wx_w")
         ident = kept([P, P], F32, "ident")
         bias = kept([P, N // P], F32, "bias")
         sel_c = kept([P, W], U32, "sel_c")
         sel_s = kept([P, W], U8, "sel_s")
-        raw = {"x0": kept([P, PACK, W], F32, "x_raw0")}
+        raw = {}
         halves = [(a, h) for a in range(2) for h in range(2)]
         w_c = {k: kept([P, W], U32, "w_c%d%d" % k) for k in halves}
         w_s = {k: kept([P, W], U8, "w_s%d%d" % k) for k in halves}
@@ -65,7 +81,7 @@ def tile_list_tiert_bias_kernel(
 
         def load(key, make):
             if key == "tab":
-                raw[key] = make([P, T], I32, "tab_w", 16 * KIB)
+                raw[key] = make([P, T], I32, "raw_tab", 16 * KIB)
                 nc.sync.dma_start(raw[key][:], tab_words[0].rearrange("p t y -> p (t y)").bitcast(I32))
             else:
                 raw[key] = make([P, PACK, W], F32, "raw_" + key, 8 * KIB)
@@ -75,13 +91,11 @@ def tile_list_tiert_bias_kernel(
                     load_x(int(key[1]))
 
         nc.vector.memset(tab_s[:], 0)
-        load_x(0)
         nc.sync.dma_start(offsets[:], offs)
         nc.sync.dma_start(wx_w[:], wx_words[0].bitcast(I32))
-        for q in (0, 2, 1, 3):
+        for r in range(4):
             nc.sync.dma_start(
-                tab_s[32 * q : 32 * q + 4, :, :],
-                tab_scales[:, 4 * q : 4 * q + 4, :].bitcast(I32).rearrange("a r t -> r a t"),
+                tab_s[r:P:16, :], tab_scales[:, r:16:4, :].bitcast(I32).rearrange("a q t -> q a t")
             )
         with tc.tile_pool(name="zeros", bufs=1) as zeros:
             blank = zeros.tile([P, P], F32, name="blank")
@@ -96,35 +110,19 @@ def tile_list_tiert_bias_kernel(
         wx_s = second.tile([P, N // 4], I32, name="wx_s", align_bytes=64)
         nc.gpsimd.memset(b_rows[:], 0.0)
         nc.gpsimd.memset(wx_s[:], 0)
-        for key in ('tab',):
+        for key in ('x0', 'tab'):
             load(key, lambda shape, dtype, name, room: second.tile(shape, dtype, name=name, align_bytes=64))
         nc.sync.dma_start(b_rows[0 : N // P, :], b.rearrange("(c p) -> c p", p=P))
-        for q in (0, 2, 1, 3):
-            nc.sync.dma_start(wx_s[32 * q : 32 * q + 4, :], wx_scales[0, 4 * q : 4 * q + 4, :].bitcast(I32))
+        for r in range(4):
+            nc.sync.dma_start(wx_s[r:P:32, :], wx_scales[0, r:16:4, :].bitcast(I32))
+        for low in low_s:
+            nc.gpsimd.memset(low[96:P, :], 0)
 
-        with tc.tile_pool(name="setup", bufs=1) as setup:
-            sel_in = setup.tile([P, PACK, P, PACK], BF16, name="sel_in", align_bytes=64)
-            nc.vector.memset(sel_in[:].rearrange("p t m i -> p (t m i)").bitcast(I32), 0)
-            for t in range(PACK):
-                nc.vector.tensor_copy(sel_in[:, t, :, t], ident[:])
-            nc.vector.quantize_mx(sel_c[:].bitcast(FP8X4), sel_s[:], sel_in[:].rearrange("p t m i -> p (t m i)"))
-
-        late = ctx.enter_context(tc.tile_pool(name="late", bufs=1))
-        place = {}
-        top = [0]
-
-        def placed(shape, dtype, name, room):
-            if name in AFTER:
-                prior, shift = AFTER[name]
-                place[name] = place[prior] + shift
-            else:
-                place[name] = top[0]
-                top[0] = top[0] + room
-            return late.tile(shape, dtype, name=name, align_bytes=64, offset=place[name])
-
-        AFTER = {'t_s10': ('rest0', 0), 't_s11': ('grp_w01', 0), 'g_w1': ('grp_w10', 0), 'res00': ('raw_w01', 0), 'res01': ('grp_x1', 0), 'res10': ('grp_x2', 0), 'res21': ('grp_x3', 0), 'g_w2': ('rest1', 0), 't_s20': ('rest1', 2048), 't_s21': ('rest1', 2560), 'g_w3': ('rest2', 0), 't_s30': ('rest2', 2048), 't_s31': ('rest2', 2560)}
-        for key in ('w00', 'w10', 'w01', 'w11', 'x1', 'x2', 'x3'):
-            load(key, placed)
+        sel_in = placed([P, PACK, P, PACK], BF16, "sel_in", 0)
+        nc.vector.memset(sel_in[:].rearrange("p t m i -> p (t m i)").bitcast(I32), 0)
+        for t in range(PACK):
+            nc.vector.tensor_copy(sel_in[:, t, :, t], ident[:])
+        nc.vector.quantize_mx(sel_c[:].bitcast(FP8X4), sel_s[:], sel_in[:].rearrange("p t m i -> p (t m i)"))
 
         def runs_out(tile, lo, hi):
             return tile[:, lo:hi, :].rearrange("p (c r) i -> p c i r", r=RUN)
@@ -153,9 +151,15 @@ def tile_list_tiert_bias_kernel(
         g_w = {}
         t_s = {}
 
-        def gather_scales(c, a):
-            t_s[c, a] = placed([P, W], U8, "t_s%d%d" % (c, a), W)
-            nc.vector.tensor_copy(t_s[c, a][:], tab_s[:, a, :].bitcast(U8).indirect(listed(c)))
+        def gather_scales(g):
+            cs = RUNS[g]
+            both = placed([P, len(cs) * W], U8, "t_s%d" % g, len(cs) * W)
+            lst = offsets[:, cs[0] * (W // 16) : (cs[-1] + 1) * (W // 16)]
+            nc.vector.tensor_copy(both[:], tab_s[:].bitcast(U8).indirect(lst))
+            nc.sync.dma_start(low_s[g][0:112, :], both[16:P, :].bitcast(I32))
+            for d, c in enumerate(cs):
+                t_s[c, 0] = both[:, d * W : (d + 1) * W]
+                t_s[c, 1] = low_s[g][:].bitcast(U8)[:, d * W : (d + 1) * W]
 
         def gather_words(c):
             g_w[c] = placed([P, W], U32, "g_w%d" % c, 4 * W)
@@ -170,7 +174,7 @@ def tile_list_tiert_bias_kernel(
 
         def residual(c, subs):
             if c not in rests:
-                rests[c] = placed([P, W, PACK], BF16, "rest%d" % c, 4 * KIB)
+                rests[c] = placed([P, W, PACK], BF16, "rest%d" % c, 8 * KIB)
             rest = rests[c]
             for s in subs:
                 cols = slice(s * P, (s + 1) * P)
@@ -208,7 +212,7 @@ def tile_list_tiert_bias_kernel(
             else:
                 h, cols = m // SUBS, slice((m % SUBS) * P, (m % SUBS + 1) * P)
                 lhsT, lhsT_s = w_c[kind, h][:, cols].bitcast(FP8X4), w_s[kind, h][:, cols]
-                rhs, rhs_s = t_c[c][:, kind, :].bitcast(FP4X4), t_s[c, kind][:]
+                rhs, rhs_s = t_c[c][:, kind, :].bitcast(FP4X4), t_s[c, kind]
             nc.tensor.matmul_mx(
                 acc[c, m][:], lhsT=lhsT, lhsT_scale=lhsT_s, rhs=rhs, rhs_scale=rhs_s, start=first, stop=last
             )
@@ -221,7 +225,7 @@ def tile_list_tiert_bias_kernel(
                     else:
                         stage[c, h] = outp.tile([P, SUBS, W], F32, name="res")
                 res = stage[c, h][:, m % SUBS, :]
-                if (c, m) in ((3, 0), (3, 2), (3, 4), (3, 6), (0, 1), (0, 0), (0, 5), (3, 1), (1, 4), (2, 6)):
+                if (c, m) in ((2, 0), (2, 2), (3, 1), (3, 5), (3, 7)):
                     nc.vector.tensor_scalar_add(res, acc[c, m][:], bias[:, m : m + 1])
                 else:
                     nc.scalar.activation(res, acc[c, m][:], IDENT, bias=bias[:, m : m + 1])
@@ -251,104 +255,102 @@ def tile_list_tiert_bias_kernel(
             nc.tensor.transpose(b_ps[:], b_rows[:], ident[:])
             nc.scalar.activation(bias[:], b_ps[:, 0 : N // P], IDENT)
 
+        gather_scales(0)
+        load("w00", placed)
+        load("w10", placed)
         first_tier(0)
-        gather_scales(0, 0)
         residual(0, (0, 1))
         residual(0, (2, 3))
-        make_bias()
-        mms(('q',), 0, range(0, 2))
         second_tier(0)
+        make_bias()
+        load("w01", placed)
+        load("w11", placed)
+        mms(('q',), 0, range(0, 2))
         mms(('q',), 0, range(2, 4))
         mms(('q',), 0, range(4, 6))
-        gather_scales(0, 1)
-        prep_w(1, 0)
+        mms(('q',), 0, range(6, 8))
         mms(('r',), 0, range(0, 2))
         mms(('r',), 0, range(2, 4))
         mms(('r',), 0, range(4, 6))
-        gather_scales(1, 0)
-        prep_w(0, 0)
+        mms(('r',), 0, range(6, 8))
         gather_words(0)
         part_words(0)
-        gather_words(1)
-        mms((0,), 0, range(2, 4))
-        mms(('q',), 0, range(6, 8))
-        mms(('r',), 0, range(6, 8))
+        prep_w(0, 0)
+        load("x1", placed)
         mms((0,), 0, range(0, 2))
-        prep_w(0, 1)
-        mms((1,), 0, range(2, 4))
-        prep_w(1, 1)
+        mms((0,), 0, range(2, 4))
+        gather_words(1)
+        prep_w(1, 0)
+        load("x2", placed)
         part_words(1)
+        prep_w(0, 1)
+        load("x3", placed)
         mms((1,), 0, range(0, 2))
-        gather_scales(1, 1)
+        mms((1,), 0, range(2, 4))
         mms((0,), 0, range(4, 6))
-        first_tier(1)
-        mms((1,), 0, range(4, 6))
-        mms((0,), 1, range(0, 2))
         mms((0,), 0, range(6, 8))
+        prep_w(1, 1)
+        first_tier(1)
+        mms((0,), 1, range(0, 2))
+        mms((1,), 1, range(0, 2))
+        mms((1,), 0, range(4, 6))
+        mms((1,), 0, range(6, 8))
+        mms((0,), 1, range(2, 4))
+        mms((1,), 1, range(2, 4))
         residual(1, (0, 1))
         residual(1, (2, 3))
         second_tier(1)
-        mms((1,), 0, range(6, 8))
-        mms((1,), 1, range(0, 2))
+        gather_scales(1)
         gather_words(2)
-        gather_scales(2, 1)
-        gather_scales(2, 0)
-        mms((1,), 1, range(2, 4))
-        first_tier(2)
         part_words(2)
-        mms((0,), 1, range(2, 4))
-        mms(('r',), 1, range(0, 2))
+        first_tier(2)
         mms(('q',), 1, range(0, 2))
         mms(('q',), 1, range(2, 4))
+        mms(('r',), 1, range(0, 2))
         mms(('r',), 1, range(2, 4))
-        mms((0,), 1, range(6, 8))
         mms((0,), 1, range(4, 6))
         mms((1,), 1, range(4, 6))
         mms(('q',), 1, range(4, 6))
         mms(('r',), 1, range(4, 6))
-        mms(('q',), 1, range(6, 8))
         residual(2, (0, 1))
         residual(2, (2, 3))
-        mms((1,), 1, range(6, 8))
-        mms(('r',), 1, range(6, 8))
         second_tier(2)
-        mms((1,), 2, range(0, 2))
-        gather_words(3)
+        mms((0,), 1, range(6, 8))
+        mms((1,), 1, range(6, 8))
+        mms(('q',), 1, range(6, 8))
+        mms(('r',), 1, range(6, 8))
         mms((0,), 2, range(0, 2))
-        mms((1,), 2, range(2, 4))
-        gather_scales(3, 0)
         mms((0,), 2, range(2, 4))
-        gather_scales(3, 1)
+        mms((1,), 2, range(0, 2))
+        mms((1,), 2, range(2, 4))
+        gather_words(3)
         part_words(3)
-        mms(('q',), 2, range(0, 2))
         first_tier(3)
+        mms(('q',), 2, range(0, 2))
         mms(('q',), 2, range(2, 4))
         mms(('r',), 2, range(0, 2))
         mms(('r',), 2, range(2, 4))
-        residual(3, (0, 1))
         mms((0,), 2, range(4, 6))
-        mms(('r',), 2, range(4, 6))
-        residual(3, (2, 3))
         mms((1,), 2, range(4, 6))
         mms(('q',), 2, range(4, 6))
-        mms((1,), 3, range(0, 2))
+        mms(('r',), 2, range(4, 6))
+        residual(3, (0, 1))
+        residual(3, (2, 3))
         second_tier(3)
-        mms((1,), 3, range(2, 4))
+        mms((0,), 2, range(6, 8))
         mms((1,), 2, range(6, 8))
         mms(('q',), 2, range(6, 8))
-        mms((0,), 2, range(6, 8))
         mms(('r',), 2, range(6, 8))
-        mms(('r',), 3, range(2, 4))
-        mms(('r',), 3, range(0, 2))
-        mms((1,), 3, range(4, 6))
         mms((0,), 3, range(0, 2))
         mms((0,), 3, range(2, 4))
+        mms((1,), 3, range(0, 2))
+        mms((1,), 3, range(2, 4))
         mms(('q',), 3, range(0, 2))
-        mms((0,), 3, range(4, 6))
-        mms(('q',), 3, range(4, 6))
         mms(('q',), 3, range(2, 4))
-        mms((0,), 3, range(6, 8))
-        mms((1,), 3, range(6, 8))
+        mms(('r',), 3, range(0, 2))
+        mms(('r',), 3, range(2, 4))
+        mms((0,), 3, range(4, 6))
+        mms((1,), 3, range(4, 6))
+        mms(('q',), 3, range(4, 6))
         mms(('r',), 3, range(4, 6))
-        mms(('q',), 3, range(6, 8))
-        mms(('r',), 3, range(6, 8))
+        groups((0, 1, 'q', 'r'), 3, range(6, 8))

@@ -1,6 +1,7 @@
 from contextlib import ExitStack
 
 import concourse.mybir as mybir
+from concourse.masks import make_identity
 
 K, L, N, T, J = 1024, 512, 1024, 4096, 2048
 FLOPS = 2 * K * N * J + 2 * 2 * L * N * J + 2 * L * L * J
@@ -24,7 +25,7 @@ CHUNKS = J // W
 SUBS = W // P
 KIB = 1024
 
-V_SHARE = {'x0': 320, 'w00': 128, 'w10': 0, 'w01': 192, 'w11': 512, 'x1': 512, 'x2': 128, 'x3': 384}
+V_SHARE = {'x0': 320, 'w00': 0, 'w10': 128, 'w01': 512, 'w11': 512, 'x1': 512, 'x2': 128, 'x3': 320}
 RUNS = ((0, 1), (2, 3))
 
 
@@ -41,8 +42,8 @@ def tile_list_tiert_bias_kernel(
             return keep.tile(shape, dtype, name=name, align_bytes=64)
 
         late = ctx.enter_context(tc.tile_pool(name="late", bufs=1))
-        place = dict({'raw_w00': 0, 'sel_in': 6144, 'raw_w10': 8192, 'raw_w11': 16384, 'rest0': 22528, 'raw_w01': 24576, 'tab_s': 32768})
-        top = [36864]
+        place = dict({'raw_w00': 0, 'sel_in': 7680, 't_s0': 8192, 'low_s': 9216, 'grp_x0': 11264, 'raw_w10': 11264, 'raw_w11': 19456, 'rest0': 25600, 'raw_w01': 27648, 'tab_s': 35840, 'raw_x0': 39936, 'blank': 39936, 'raw_tab': 48128, 'ident': 64256, 'wx_s': 64512})
+        top = [65536]
 
         def placed(shape, dtype, name, room):
             if name in AFTER:
@@ -53,12 +54,12 @@ def tile_list_tiert_bias_kernel(
                 top[0] = top[0] + room
             return late.tile(shape, dtype, name=name, align_bytes=64, offset=place[name])
 
-        AFTER = {'t_s1': ('rest1', 0), 'res01': ('raw_w11', 0), 'res21': ('grp_x3', 0), 'grp_x2': ('grp_w11', 0), 'grp_x3': ('raw_x2', 0), 'g_w2': ('rest1', 1024), 'g_w3': ('rest2', 0), 'raw_x1': ('raw_w00', 0), 'raw_x2': ('raw_w10', 0), 'raw_x3': ('grp_w10', 0)}
+        AFTER = {'t_s1': ('rest1', 0), 'res20': ('grp_x3', 0), 'grp_x2': ('raw_x1', 0), 'grp_x3': ('raw_x2', 0), 'g_w2': ('rest1', 1024), 'g_w3': ('rest2', 0), 'raw_x1': ('raw_w00', 0), 'raw_x2': ('raw_w10', 0), 'raw_x3': ('grp_w10', 0)}
         offsets = keep.tile([P, J // 16], U16, name="offsets")
         tab_s = placed([P, T // 4], I32, "tab_s", 0)
-        low_s = [kept([P, len(cs) * W // 4], I32, "low_s%d" % g) for g, cs in enumerate(RUNS)]
         wx_w = kept([P, N // 2], I32, "wx_w")
-        ident = kept([P, P], F32, "ident")
+        b_rows = kept([P, P], F32, "b_rows")
+        ident_pe = kept([P, P], F32, "ident_pe")
         bias = kept([P, N // P], F32, "bias")
         sel_c = kept([P, W], U32, "sel_c")
         sel_s = kept([P, W], U8, "sel_s")
@@ -93,36 +94,29 @@ def tile_list_tiert_bias_kernel(
         nc.vector.memset(tab_s[:], 0)
         nc.sync.dma_start(offsets[:], offs)
         nc.sync.dma_start(wx_w[:], wx_words[0].bitcast(I32))
-        for r in range(4):
-            nc.sync.dma_start(
-                tab_s[r:P:16, :], tab_scales[:, r:16:4, :].bitcast(I32).rearrange("a q t -> q a t")
-            )
-        with tc.tile_pool(name="zeros", bufs=1) as zeros:
-            blank = zeros.tile([P, P], F32, name="blank")
-            nc.vector.memset(blank[:], 0.0)
-            nc.gpsimd.affine_select(
-                out=ident[:], in_=blank[:], pattern=[[-1, P]], compare_op=mybir.AluOpType.not_equal,
-                fill=1.0, base=0, channel_multiplier=1,
-            )
-
-        second = ctx.enter_context(tc.tile_pool(name="second", bufs=1))
-        b_rows = second.tile([P, P], F32, name="b_rows", align_bytes=64)
-        wx_s = second.tile([P, N // 4], I32, name="wx_s", align_bytes=64)
-        nc.gpsimd.memset(b_rows[:], 0.0)
-        nc.gpsimd.memset(wx_s[:], 0)
-        for key in ('x0', 'tab'):
-            load(key, lambda shape, dtype, name, room: second.tile(shape, dtype, name=name, align_bytes=64))
+        for q in (0, 2, 1, 3):
+            nc.sync.dma_start(tab_s[32 * q : 32 * q + 8, :], tab_scales[:, 4 * q : 4 * q + 4, :].bitcast(I32))
+        blank = placed([P, P], F32, "blank", 0)
+        ident = placed([P, P], F32, "ident", 0)
+        nc.gpsimd.memset(blank[:], 0.0)
+        make_identity(nc, ident[:])
+        nc.vector.tensor_copy(b_rows[:], blank[:])
+        nc.scalar.activation(ident_pe[:], ident[:], IDENT)
+        load("x0", placed)
         nc.sync.dma_start(b_rows[0 : N // P, :], b.rearrange("(c p) -> c p", p=P))
-        for r in range(4):
-            nc.sync.dma_start(wx_s[r:P:32, :], wx_scales[0, r:16:4, :].bitcast(I32))
-        for low in low_s:
-            nc.gpsimd.memset(low[96:P, :], 0)
 
         sel_in = placed([P, PACK, P, PACK], BF16, "sel_in", 0)
         nc.vector.memset(sel_in[:].rearrange("p t m i -> p (t m i)").bitcast(I32), 0)
         for t in range(PACK):
             nc.vector.tensor_copy(sel_in[:, t, :, t], ident[:])
+        load("tab", placed)
+        wx_s = placed([P, N // 4], I32, "wx_s", 0)
+        nc.vector.memset(wx_s[:], 0)
+        for r in range(4):
+            nc.sync.dma_start(wx_s[r:P:32, :], wx_scales[0, r:16:4, :].bitcast(I32))
         nc.vector.quantize_mx(sel_c[:].bitcast(FP8X4), sel_s[:], sel_in[:].rearrange("p t m i -> p (t m i)"))
+        low_s = placed([P, 2, 2 * W // 4], I32, "low_s", 0)
+        nc.gpsimd.memset(low_s[96:P, :, :], 0)
 
         def runs_out(tile, lo, hi):
             return tile[:, lo:hi, :].rearrange("p (c r) i -> p c i r", r=RUN)
@@ -131,10 +125,7 @@ def tile_list_tiert_bias_kernel(
             return ap.rearrange("p i (c r) -> p c i r", r=RUN)
 
         def interleave(key):
-            if key == "x0":
-                grouped = kept([P, W, PACK], BF16, "grp_x0")
-            else:
-                grouped = placed([P, W, PACK], BF16, "grp_" + key, 8 * KIB)
+            grouped = placed([P, W, PACK], BF16, "grp_" + key, 8 * KIB)
             v = V_SHARE[key]
             if v > 0:
                 nc.vector.tensor_copy(runs_out(grouped, 0, v), runs_in(raw[key][:, :, 0:v]))
@@ -156,10 +147,10 @@ def tile_list_tiert_bias_kernel(
             both = placed([P, len(cs) * W], U8, "t_s%d" % g, len(cs) * W)
             lst = offsets[:, cs[0] * (W // 16) : (cs[-1] + 1) * (W // 16)]
             nc.vector.tensor_copy(both[:], tab_s[:].bitcast(U8).indirect(lst))
-            nc.sync.dma_start(low_s[g][0:112, :], both[16:P, :].bitcast(I32))
+            nc.sync.dma_start(low_s[0:112, g, :], both[4:116, :].bitcast(I32))
             for d, c in enumerate(cs):
                 t_s[c, 0] = both[:, d * W : (d + 1) * W]
-                t_s[c, 1] = low_s[g][:].bitcast(U8)[:, d * W : (d + 1) * W]
+                t_s[c, 1] = low_s[:, g, :].bitcast(U8)[:, d * W : (d + 1) * W]
 
         def gather_words(c):
             g_w[c] = placed([P, W], U32, "g_w%d" % c, 4 * W)
@@ -225,7 +216,7 @@ def tile_list_tiert_bias_kernel(
                     else:
                         stage[c, h] = outp.tile([P, SUBS, W], F32, name="res")
                 res = stage[c, h][:, m % SUBS, :]
-                if (c, m) in ((2, 0), (2, 2), (3, 1), (3, 5), (3, 7)):
+                if (c, m) in ((2, 1), (2, 3), (2, 5), (2, 7), (3, 2), (3, 6)):
                     nc.vector.tensor_scalar_add(res, acc[c, m][:], bias[:, m : m + 1])
                 else:
                     nc.scalar.activation(res, acc[c, m][:], IDENT, bias=bias[:, m : m + 1])
@@ -252,13 +243,13 @@ def tile_list_tiert_bias_kernel(
 
         def make_bias():
             b_ps = psum.tile([P, P], F32, name="bank")
-            nc.tensor.transpose(b_ps[:], b_rows[:], ident[:])
+            nc.tensor.transpose(b_ps[:], b_rows[:], ident_pe[:])
             nc.scalar.activation(bias[:], b_ps[:, 0 : N // P], IDENT)
 
-        gather_scales(0)
         load("w00", placed)
-        load("w10", placed)
+        gather_scales(0)
         first_tier(0)
+        load("w10", placed)
         residual(0, (0, 1))
         residual(0, (2, 3))
         second_tier(0)

@@ -20,13 +20,68 @@ SUB = mybir.AluOpType.subtract
 P = 128
 PACK = 4
 W = 512
-RUN = 4
 CHUNKS = J // W
-SUBS = W // P
+TILES = N // P
+HALF = W // P
+RUN = 4
+LIST_ROWS = 16
+QUADRANT = 32
+SCALE_ROWS = 4
+BLOCKS = 16
+LIFT = 16
+PAIR = 2
+BANKS = 8
+STAGES = 4
+ALIGN = 64
 KIB = 1024
 
-V_SHARE = {'x0': 320, 'w00': 0, 'w10': 128, 'w01': 512, 'w11': 512, 'x1': 512, 'x2': 128, 'x3': 320}
-RUNS = ((0, 1), (2, 3))
+V_SHARE = {"x0": 384, "w00": 192, "w10": 128, "w01": 320, "w11": 512, "x1": 320, "x2": 256, "x3": 320}
+
+V_EMPTIES = ((2, 0), (2, 2), (2, 4), (2, 6), (3, 2), (3, 6))
+
+FIRST_HOME = {
+    "raw_w00": 0,
+    "sel_in": 7 * KIB + KIB // 2,
+    "scales0": 8 * KIB,
+    "low_s": 9 * KIB,
+    "staged_x0": 11 * KIB,
+    "raw_w10": 11 * KIB,
+    "raw_w11": 19 * KIB,
+    "rest0": 25 * KIB,
+    "raw_w01": 27 * KIB,
+    "tab_s": 35 * KIB,
+    "raw_x0": 39 * KIB,
+    "blank": 39 * KIB,
+    "raw_tab": 47 * KIB,
+    "ident": 63 * KIB - KIB // 4,
+    "wx_s": 63 * KIB,
+    "words0": 64 * KIB,
+    "staged_w00": 66 * KIB,
+    "staged_w10": 70 * KIB,
+    "staged_w01": 74 * KIB,
+    "staged_w11": 82 * KIB,
+    "staged_x1": 86 * KIB,
+    "rest1": 90 * KIB,
+    "rest2": 94 * KIB,
+    "rest3": 98 * KIB,
+}
+
+TAKES_OVER = {
+    "raw_x1": "raw_w00",
+    "raw_x2": "raw_w10",
+    "raw_x3": "staged_w01",
+    "staged_x2": "raw_x1",
+    "staged_x3": "raw_x2",
+    "words1": "staged_w00",
+    "words2": "staged_x2",
+    "words3": "rest2",
+    "scales1": "rest1",
+    "done21": "staged_x3",
+}
+
+
+def home(name):
+    return home(TAKES_OVER[name]) if name in TAKES_OVER else FIRST_HOME[name]
 
 
 def tile_list_tiert_bias_kernel(
@@ -35,35 +90,24 @@ def tile_list_tiert_bias_kernel(
     nc = tc.nc
     with ExitStack() as ctx:
         keep = ctx.enter_context(tc.tile_pool(name="keep", bufs=1))
-        outp = ctx.enter_context(tc.tile_pool(name="outp", bufs=3))
-        psum = ctx.enter_context(tc.psum_pool(name="psum", bufs=8))
+        outp = ctx.enter_context(tc.tile_pool(name="outp", bufs=STAGES))
+        psum = ctx.enter_context(tc.psum_pool(name="psum", bufs=BANKS))
+        shared = ctx.enter_context(tc.tile_pool(name="shared", bufs=1))
 
         def kept(shape, dtype, name):
-            return keep.tile(shape, dtype, name=name, align_bytes=64)
+            return keep.tile(shape, dtype, name=name, align_bytes=ALIGN)
 
-        late = ctx.enter_context(tc.tile_pool(name="late", bufs=1))
-        place = dict({'raw_w00': 0, 'sel_in': 7680, 't_s0': 8192, 'low_s': 9216, 'grp_x0': 11264, 'raw_w10': 11264, 'raw_w11': 19456, 'rest0': 25600, 'raw_w01': 27648, 'tab_s': 35840, 'raw_x0': 39936, 'blank': 39936, 'raw_tab': 48128, 'ident': 64256, 'wx_s': 64512})
-        top = [65536]
+        def placed(shape, dtype, name):
+            return shared.tile(shape, dtype, name=name, align_bytes=ALIGN, offset=home(name))
 
-        def placed(shape, dtype, name, room):
-            if name in AFTER:
-                prior, shift = AFTER[name]
-                place[name] = place[prior] + shift
-            elif name not in place:
-                place[name] = top[0]
-                top[0] = top[0] + room
-            return late.tile(shape, dtype, name=name, align_bytes=64, offset=place[name])
-
-        AFTER = {'t_s1': ('rest1', 0), 'res20': ('grp_x3', 0), 'grp_x2': ('raw_x1', 0), 'grp_x3': ('raw_x2', 0), 'g_w2': ('rest1', 1024), 'g_w3': ('rest2', 0), 'raw_x1': ('raw_w00', 0), 'raw_x2': ('raw_w10', 0), 'raw_x3': ('grp_w10', 0)}
-        offsets = keep.tile([P, J // 16], U16, name="offsets")
-        tab_s = placed([P, T // 4], I32, "tab_s", 0)
+        offsets = keep.tile([P, J // LIST_ROWS], U16, name="offsets")
+        tab_s = placed([P, T // 4], I32, "tab_s")
         wx_w = kept([P, N // 2], I32, "wx_w")
         b_rows = kept([P, P], F32, "b_rows")
         ident_pe = kept([P, P], F32, "ident_pe")
-        bias = kept([P, N // P], F32, "bias")
-        sel_c = kept([P, W], U32, "sel_c")
-        sel_s = kept([P, W], U8, "sel_s")
-        raw = {}
+        bias = kept([P, TILES], F32, "bias")
+        sel_c = kept([P, PACK * P], U32, "sel_c")
+        sel_s = kept([P, PACK * P], U8, "sel_s")
         halves = [(a, h) for a in range(2) for h in range(2)]
         w_c = {k: kept([P, W], U32, "w_c%d%d" % k) for k in halves}
         w_s = {k: kept([P, W], U8, "w_s%d%d" % k) for k in halves}
@@ -72,108 +116,105 @@ def tile_list_tiert_bias_kernel(
         xr_c = [kept([P, W], U32, "xr_c%d" % c) for c in range(CHUNKS)]
         xr_s = [kept([P, W], U8, "xr_s%d" % c) for c in range(CHUNKS)]
         t_c = [kept([P, 2, 2 * W], U8, "t_c%d" % c) for c in range(CHUNKS)]
+        raw = {}
+
+        def load_block(key, rows):
+            raw[key] = placed([P, PACK, W], F32, "raw_" + key)
+            nc.sync.dma_start(raw[key][:], rows.rearrange("(p i) j -> p i j", i=PACK))
 
         def load_x(c):
-            nc.sync.dma_start(raw["x%d" % c][:], x[:, c * W : (c + 1) * W].rearrange("(p i) j -> p i j", i=PACK))
+            load_block("x%d" % c, x[:, c * W : (c + 1) * W])
 
         def load_w(a, h):
-            rows = wt[a * W : (a + 1) * W, h * W : (h + 1) * W]
-            nc.sync.dma_start(raw["w%d%d" % (a, h)][:], rows.rearrange("(p i) n -> p i n", i=PACK))
-
-        def load(key, make):
-            if key == "tab":
-                raw[key] = make([P, T], I32, "raw_tab", 16 * KIB)
-                nc.sync.dma_start(raw[key][:], tab_words[0].rearrange("p t y -> p (t y)").bitcast(I32))
-            else:
-                raw[key] = make([P, PACK, W], F32, "raw_" + key, 8 * KIB)
-                if key[0] == "w":
-                    load_w(int(key[1]), int(key[2]))
-                else:
-                    load_x(int(key[1]))
+            load_block("w%d%d" % (a, h), wt[a * W : (a + 1) * W, h * W : (h + 1) * W])
 
         nc.vector.memset(tab_s[:], 0)
         nc.sync.dma_start(offsets[:], offs)
         nc.sync.dma_start(wx_w[:], wx_words[0].bitcast(I32))
-        for q in (0, 2, 1, 3):
-            nc.sync.dma_start(tab_s[32 * q : 32 * q + 8, :], tab_scales[:, 4 * q : 4 * q + 4, :].bitcast(I32))
-        blank = placed([P, P], F32, "blank", 0)
-        ident = placed([P, P], F32, "ident", 0)
+        for r in range(SCALE_ROWS):
+            rows = tab_scales[:, r:BLOCKS:SCALE_ROWS, :].bitcast(I32).rearrange("a q t -> q a t")
+            nc.sync.dma_start(tab_s[r:P:LIFT, :], rows)
+
+        blank = placed([P, P], F32, "blank")
+        ident = placed([P, P], F32, "ident")
         nc.gpsimd.memset(blank[:], 0.0)
         make_identity(nc, ident[:])
         nc.vector.tensor_copy(b_rows[:], blank[:])
         nc.scalar.activation(ident_pe[:], ident[:], IDENT)
-        load("x0", placed)
-        nc.sync.dma_start(b_rows[0 : N // P, :], b.rearrange("(c p) -> c p", p=P))
+        load_x(0)
+        nc.sync.dma_start(b_rows[0:TILES, :], b.rearrange("(m p) -> m p", p=P))
 
-        sel_in = placed([P, PACK, P, PACK], BF16, "sel_in", 0)
-        nc.vector.memset(sel_in[:].rearrange("p t m i -> p (t m i)").bitcast(I32), 0)
+        sel_in = placed([P, PACK, P, PACK], BF16, "sel_in")
+        sel_flat = sel_in[:].rearrange("p t m i -> p (t m i)")
+        nc.vector.memset(sel_flat.bitcast(I32), 0)
         for t in range(PACK):
             nc.vector.tensor_copy(sel_in[:, t, :, t], ident[:])
-        load("tab", placed)
-        wx_s = placed([P, N // 4], I32, "wx_s", 0)
+        raw_tab = placed([P, T], I32, "raw_tab")
+        nc.sync.dma_start(raw_tab[:], tab_words[0].rearrange("p t y -> p (t y)").bitcast(I32))
+        wx_s = placed([P, N // 4], I32, "wx_s")
         nc.vector.memset(wx_s[:], 0)
-        for r in range(4):
-            nc.sync.dma_start(wx_s[r:P:32, :], wx_scales[0, r:16:4, :].bitcast(I32))
-        nc.vector.quantize_mx(sel_c[:].bitcast(FP8X4), sel_s[:], sel_in[:].rearrange("p t m i -> p (t m i)"))
-        low_s = placed([P, 2, 2 * W // 4], I32, "low_s", 0)
-        nc.gpsimd.memset(low_s[96:P, :, :], 0)
+        for r in range(SCALE_ROWS):
+            nc.sync.dma_start(wx_s[r:P:QUADRANT, :], wx_scales[0, r:BLOCKS:SCALE_ROWS, :].bitcast(I32))
+        nc.vector.quantize_mx(sel_c[:].bitcast(FP8X4), sel_s[:], sel_flat)
 
-        def runs_out(tile, lo, hi):
-            return tile[:, lo:hi, :].rearrange("p (c r) i -> p c i r", r=RUN)
+        low_s = placed([P, CHUNKS // PAIR, PAIR * W // 4], I32, "low_s")
+        nc.gpsimd.memset(low_s[P - QUADRANT : P, :, :], 0)
+
+        def runs_out(staged, lo, hi):
+            return staged[:, lo:hi, :].rearrange("p (c r) i -> p c i r", r=RUN)
 
         def runs_in(ap):
             return ap.rearrange("p i (c r) -> p c i r", r=RUN)
 
-        def interleave(key):
-            grouped = placed([P, W, PACK], BF16, "grp_" + key, 8 * KIB)
+        def stage(key):
+            staged = placed([P, W, PACK], BF16, "staged_" + key)
             v = V_SHARE[key]
-            if v > 0:
-                nc.vector.tensor_copy(runs_out(grouped, 0, v), runs_in(raw[key][:, :, 0:v]))
+            nc.vector.tensor_copy(runs_out(staged, 0, v), runs_in(raw[key][:, :, 0:v]))
             if v < W:
-                nc.scalar.activation(runs_out(grouped, v, W), runs_in(raw[key][:, :, v:W]), IDENT)
-            return grouped
+                nc.scalar.activation(runs_out(staged, v, W), runs_in(raw[key][:, :, v:W]), IDENT)
+            return staged
 
-        def quantize(grouped, codes, scales):
-            nc.vector.quantize_mx(codes[:].bitcast(FP8X4), scales[:], grouped[:].rearrange("p j i -> p (j i)"))
+        def quantize(staged, codes, scales):
+            nc.vector.quantize_mx(codes[:].bitcast(FP8X4), scales[:], staged[:].rearrange("p j i -> p (j i)"))
 
-        def listed(c):
-            return offsets[:, c * (W // 16) : (c + 1) * (W // 16)]
+        def listed(first, count):
+            return offsets[:, first * W // LIST_ROWS : (first + count) * W // LIST_ROWS]
 
-        g_w = {}
+        words = {}
         t_s = {}
 
         def gather_scales(g):
-            cs = RUNS[g]
-            both = placed([P, len(cs) * W], U8, "t_s%d" % g, len(cs) * W)
-            lst = offsets[:, cs[0] * (W // 16) : (cs[-1] + 1) * (W // 16)]
-            nc.vector.tensor_copy(both[:], tab_s[:].bitcast(U8).indirect(lst))
-            nc.sync.dma_start(low_s[0:112, g, :], both[4:116, :].bitcast(I32))
-            for d, c in enumerate(cs):
-                t_s[c, 0] = both[:, d * W : (d + 1) * W]
-                t_s[c, 1] = low_s[:, g, :].bitcast(U8)[:, d * W : (d + 1) * W]
+            both = placed([P, PAIR * W], U8, "scales%d" % g)
+            nc.vector.tensor_copy(both[:], tab_s[:].bitcast(U8).indirect(listed(PAIR * g, PAIR)))
+            nc.sync.dma_start(low_s[0 : P - LIFT, g, :], both[LIFT:P, :].bitcast(I32))
+            for d in range(PAIR):
+                t_s[PAIR * g + d, 0] = both[:, d * W : (d + 1) * W]
+                t_s[PAIR * g + d, 1] = low_s[:, g, :].bitcast(U8)[:, d * W : (d + 1) * W]
 
         def gather_words(c):
-            g_w[c] = placed([P, W], U32, "g_w%d" % c, 4 * W)
-            nc.vector.tensor_copy(g_w[c][:], raw["tab"][:].bitcast(U32).indirect(listed(c)))
+            words[c] = placed([P, W], U32, "words%d" % c)
+            nc.vector.tensor_copy(words[c][:], raw_tab[:].bitcast(U32).indirect(listed(c, 1)))
 
         def part_words(c):
             nc.vector.tensor_copy(
-                t_c[c][:].bitcast(U16), g_w[c][:].bitcast(U16).rearrange("p (j d) -> p d j", d=2)
+                t_c[c][:].bitcast(U16), words[c][:].bitcast(U16).rearrange("p (j a) -> p a j", a=2)
             )
 
-        rests = {}
+        def quantize_w(a, h):
+            quantize(stage("w%d%d" % (a, h)), w_c[a, h], w_s[a, h])
 
-        def residual(c, subs):
-            if c not in rests:
-                rests[c] = placed([P, W, PACK], BF16, "rest%d" % c, 8 * KIB)
-            rest = rests[c]
-            for s in subs:
+        def first_tier(c):
+            quantize(stage("x%d" % c), xq_c[c], xq_s[c])
+
+        def second_tier(c):
+            rest = placed([P, W, PACK], BF16, "rest%d" % c)
+            for s in range(HALF):
                 cols = slice(s * P, (s + 1) * P)
-                dq = psum.tile([P, PACK, P], F32, name="bank")
+                values = psum.tile([P, PACK, P], F32, name="bank")
                 for t in range(PACK):
                     sel = slice(t * P, (t + 1) * P)
                     nc.tensor.matmul_mx(
-                        dq[:, t, :],
+                        values[:, t, :],
                         lhsT=sel_c[:, sel].bitcast(FP8X4),
                         lhsT_scale=sel_s[:, sel],
                         rhs=xq_c[c][:, cols].bitcast(FP8X4),
@@ -182,166 +223,104 @@ def tile_list_tiert_bias_kernel(
                         stop=True,
                     )
                 nc.vector.tensor_tensor(
-                    runs_out(rest, s * P, (s + 1) * P), runs_in(raw["x%d" % c][:, :, cols]), runs_in(dq[:]), SUB
+                    runs_out(rest, s * P, (s + 1) * P), runs_in(raw["x%d" % c][:, :, cols]), runs_in(values[:]), SUB
                 )
+            quantize(rest, xr_c[c], xr_s[c])
 
         acc = {}
+        passes_done = {}
         done = {}
-        stage = {}
+        all_kinds = (0, 1, "q", "r")
 
-        def mm(kind, c, m):
+        def finish(c, m):
+            h = m // HALF
+            if (c, h) not in done:
+                name = "done%d%d" % (c, h)
+                if name in TAKES_OVER:
+                    done[c, h] = placed([P, HALF, W], F32, name)
+                else:
+                    done[c, h] = outp.tile([P, HALF, W], F32, name="done")
+            res = done[c, h][:, m % HALF, :]
+            if (c, m) in V_EMPTIES:
+                nc.vector.tensor_scalar_add(res, acc[c, m][:], bias[:, m : m + 1])
+            else:
+                nc.scalar.activation(res, acc[c, m][:], IDENT, bias=bias[:, m : m + 1])
+            nc.sync.dma_start(out[m * P : (m + 1) * P, c * W : (c + 1) * W], res)
+
+        def one_pass(kind, c, m):
             if (c, m) not in acc:
                 acc[c, m] = psum.tile([P, W], F32, name="bank")
-                done[c, m] = 0
-            first, last = done[c, m] == 0, done[c, m] == 3
-            done[c, m] = done[c, m] + 1
+                passes_done[c, m] = 0
+            first, last = passes_done[c, m] == 0, passes_done[c, m] == len(all_kinds) - 1
+            passes_done[c, m] = passes_done[c, m] + 1
             if kind in ("q", "r"):
                 codes, scales = (xq_c, xq_s) if kind == "q" else (xr_c, xr_s)
-                lhsT = wx_w[:, 64 * m : 64 * (m + 1)].bitcast(FP4X4)
-                lhsT_s = wx_s[:, 32 * m : 32 * (m + 1)].bitcast(U8)
+                lhsT = wx_w[:, m * P // 2 : (m + 1) * P // 2].bitcast(FP4X4)
+                lhsT_s = wx_s[:, m * P // 4 : (m + 1) * P // 4].bitcast(U8)
                 rhs, rhs_s = codes[c][:].bitcast(FP8X4), scales[c][:]
             else:
-                h, cols = m // SUBS, slice((m % SUBS) * P, (m % SUBS + 1) * P)
+                h, cols = m // HALF, slice((m % HALF) * P, (m % HALF + 1) * P)
                 lhsT, lhsT_s = w_c[kind, h][:, cols].bitcast(FP8X4), w_s[kind, h][:, cols]
                 rhs, rhs_s = t_c[c][:, kind, :].bitcast(FP4X4), t_s[c, kind]
             nc.tensor.matmul_mx(
                 acc[c, m][:], lhsT=lhsT, lhsT_scale=lhsT_s, rhs=rhs, rhs_scale=rhs_s, start=first, stop=last
             )
             if last:
-                h = m // SUBS
-                if (c, h) not in stage:
-                    name = "res%d%d" % (c, h)
-                    if name in AFTER:
-                        stage[c, h] = placed([P, SUBS, W], F32, name, 8 * KIB)
-                    else:
-                        stage[c, h] = outp.tile([P, SUBS, W], F32, name="res")
-                res = stage[c, h][:, m % SUBS, :]
-                if (c, m) in ((2, 1), (2, 3), (2, 5), (2, 7), (3, 2), (3, 6)):
-                    nc.vector.tensor_scalar_add(res, acc[c, m][:], bias[:, m : m + 1])
-                else:
-                    nc.scalar.activation(res, acc[c, m][:], IDENT, bias=bias[:, m : m + 1])
-                nc.sync.dma_start(out[m * P : (m + 1) * P, c * W : (c + 1) * W], res)
+                finish(c, m)
 
-        def mms(kinds, c, ms):
+        def by_kind(kinds, c, tiles):
             for kind in kinds:
-                for m in ms:
-                    mm(kind, c, m)
+                for m in tiles:
+                    one_pass(kind, c, m)
 
-        def groups(kinds, c, ms):
-            for m in ms:
-                for kind in kinds:
-                    mm(kind, c, m)
+        lower, upper = range(0, HALF), range(HALF, TILES)
+        third_pair, last_pair = upper[:2], upper[2:]
 
-        def prep_w(a, h):
-            quantize(interleave("w%d%d" % (a, h)), w_c[a, h], w_s[a, h])
-
-        def first_tier(c):
-            quantize(interleave("x%d" % c), xq_c[c], xq_s[c])
-
-        def second_tier(c):
-            quantize(rests[c], xr_c[c], xr_s[c])
-
-        def make_bias():
-            b_ps = psum.tile([P, P], F32, name="bank")
-            nc.tensor.transpose(b_ps[:], b_rows[:], ident_pe[:])
-            nc.scalar.activation(bias[:], b_ps[:, 0 : N // P], IDENT)
-
-        load("w00", placed)
+        load_w(0, 0)
         gather_scales(0)
         first_tier(0)
-        load("w10", placed)
-        residual(0, (0, 1))
-        residual(0, (2, 3))
+        load_w(1, 0)
         second_tier(0)
-        make_bias()
-        load("w01", placed)
-        load("w11", placed)
-        mms(('q',), 0, range(0, 2))
-        mms(('q',), 0, range(2, 4))
-        mms(('q',), 0, range(4, 6))
-        mms(('q',), 0, range(6, 8))
-        mms(('r',), 0, range(0, 2))
-        mms(('r',), 0, range(2, 4))
-        mms(('r',), 0, range(4, 6))
-        mms(('r',), 0, range(6, 8))
+        b_cols = psum.tile([P, P], F32, name="bank")
+        nc.tensor.transpose(b_cols[:], b_rows[:], ident_pe[:])
+        nc.scalar.activation(bias[:], b_cols[:, 0:TILES], IDENT)
+        load_w(0, 1)
+        load_w(1, 1)
+        by_kind(("q", "r"), 0, range(TILES))
+
         gather_words(0)
         part_words(0)
-        prep_w(0, 0)
-        load("x1", placed)
-        mms((0,), 0, range(0, 2))
-        mms((0,), 0, range(2, 4))
+        quantize_w(0, 0)
+        load_x(1)
+        by_kind((0,), 0, lower)
         gather_words(1)
-        prep_w(1, 0)
-        load("x2", placed)
+        quantize_w(1, 0)
+        load_x(2)
         part_words(1)
-        prep_w(0, 1)
-        load("x3", placed)
-        mms((1,), 0, range(0, 2))
-        mms((1,), 0, range(2, 4))
-        mms((0,), 0, range(4, 6))
-        mms((0,), 0, range(6, 8))
-        prep_w(1, 1)
+        quantize_w(0, 1)
+        load_x(3)
+        by_kind((1,), 0, lower)
+        by_kind((0,), 0, upper)
+        quantize_w(1, 1)
         first_tier(1)
-        mms((0,), 1, range(0, 2))
-        mms((1,), 1, range(0, 2))
-        mms((1,), 0, range(4, 6))
-        mms((1,), 0, range(6, 8))
-        mms((0,), 1, range(2, 4))
-        mms((1,), 1, range(2, 4))
-        residual(1, (0, 1))
-        residual(1, (2, 3))
+        by_kind((0, 1), 1, lower)
+        by_kind((1,), 0, upper)
         second_tier(1)
         gather_scales(1)
-        gather_words(2)
-        part_words(2)
-        first_tier(2)
-        mms(('q',), 1, range(0, 2))
-        mms(('q',), 1, range(2, 4))
-        mms(('r',), 1, range(0, 2))
-        mms(('r',), 1, range(2, 4))
-        mms((0,), 1, range(4, 6))
-        mms((1,), 1, range(4, 6))
-        mms(('q',), 1, range(4, 6))
-        mms(('r',), 1, range(4, 6))
-        residual(2, (0, 1))
-        residual(2, (2, 3))
-        second_tier(2)
-        mms((0,), 1, range(6, 8))
-        mms((1,), 1, range(6, 8))
-        mms(('q',), 1, range(6, 8))
-        mms(('r',), 1, range(6, 8))
-        mms((0,), 2, range(0, 2))
-        mms((0,), 2, range(2, 4))
-        mms((1,), 2, range(0, 2))
-        mms((1,), 2, range(2, 4))
-        gather_words(3)
-        part_words(3)
-        first_tier(3)
-        mms(('q',), 2, range(0, 2))
-        mms(('q',), 2, range(2, 4))
-        mms(('r',), 2, range(0, 2))
-        mms(('r',), 2, range(2, 4))
-        mms((0,), 2, range(4, 6))
-        mms((1,), 2, range(4, 6))
-        mms(('q',), 2, range(4, 6))
-        mms(('r',), 2, range(4, 6))
-        residual(3, (0, 1))
-        residual(3, (2, 3))
-        second_tier(3)
-        mms((0,), 2, range(6, 8))
-        mms((1,), 2, range(6, 8))
-        mms(('q',), 2, range(6, 8))
-        mms(('r',), 2, range(6, 8))
-        mms((0,), 3, range(0, 2))
-        mms((0,), 3, range(2, 4))
-        mms((1,), 3, range(0, 2))
-        mms((1,), 3, range(2, 4))
-        mms(('q',), 3, range(0, 2))
-        mms(('q',), 3, range(2, 4))
-        mms(('r',), 3, range(0, 2))
-        mms(('r',), 3, range(2, 4))
-        mms((0,), 3, range(4, 6))
-        mms((1,), 3, range(4, 6))
-        mms(('q',), 3, range(4, 6))
-        mms(('r',), 3, range(4, 6))
-        groups((0, 1, 'q', 'r'), 3, range(6, 8))
+
+        for c in range(1, CHUNKS):
+            more = c + 1 < CHUNKS
+            if c > 1:
+                by_kind((0, 1), c, lower)
+            if more:
+                first_tier(c + 1)
+                gather_words(c + 1)
+                part_words(c + 1)
+            by_kind(("q", "r"), c, lower)
+            by_kind(all_kinds, c, third_pair)
+            if more:
+                second_tier(c + 1)
+                by_kind(all_kinds, c, last_pair)
+            else:
+                for m in last_pair:
+                    by_kind(all_kinds, c, (m,))

@@ -22,66 +22,63 @@ PACK = 4
 W = 512
 CHUNKS = J // W
 TILES = N // P
-HALF = W // P
+HALF = TILES // 2
+PARTS = W // P
+PIECE = W // 2
+KINDS = 4
 RUN = 4
 LIST_ROWS = 16
 QUADRANT = 32
 SCALE_ROWS = 4
 BLOCKS = 16
 LIFT = 16
-PAIR = 2
 BANKS = 8
-STAGES = 4
+RESULTS = 2 * TILES
 ALIGN = 64
 KIB = 1024
 
-V_SHARE = {"x0": 384, "w00": 192, "w10": 128, "w01": 320, "w11": 512, "x1": 320, "x2": 256, "x3": 320}
+V_COLS = 176
 
-V_EMPTIES = ((2, 0), (2, 2), (2, 4), (2, 6), (3, 2), (3, 6))
+W_BLOCKS = tuple((a, n0) for n0 in range(0, N, PIECE) for a in range(2))
 
-FIRST_HOME = {
-    "raw_w00": 0,
-    "sel_in": 7 * KIB + KIB // 2,
-    "scales0": 8 * KIB,
-    "low_s": 9 * KIB,
-    "staged_x0": 11 * KIB,
-    "raw_w10": 11 * KIB,
-    "raw_w11": 19 * KIB,
-    "rest0": 25 * KIB,
-    "raw_w01": 27 * KIB,
-    "tab_s": 35 * KIB,
-    "raw_x0": 39 * KIB,
-    "blank": 39 * KIB,
-    "raw_tab": 47 * KIB,
-    "ident": 63 * KIB - KIB // 4,
-    "wx_s": 63 * KIB,
-    "words0": 64 * KIB,
-    "staged_w00": 66 * KIB,
-    "staged_w10": 70 * KIB,
-    "staged_w01": 74 * KIB,
-    "staged_w11": 82 * KIB,
-    "staged_x1": 86 * KIB,
-    "rest1": 90 * KIB,
-    "rest2": 94 * KIB,
-    "rest3": 98 * KIB,
+S_GROUPS = ((0, 2), (2, 1), (3, 1))
+
+HOME = {
+    "sel_in": 0,
+    "staged_x0a": 1 * KIB,
+    "staged_x0b": 4 * KIB - ALIGN,
+    "scales0": 0,
+    "staged_w0": 3 * KIB,
+    "staged_w1": 5 * KIB,
+    "words0": 1 * KIB,
+    "w_c2": 1 * KIB,
+    "words1": 5 * KIB,
+    "w_c3": 5 * KIB,
+    "raw_w1": 8 * KIB,
+    "staged_w2": 8 * KIB,
+    "staged_w3": 10 * KIB,
+    "staged_w5": 10 * KIB,
+    "staged_w7": 10 * KIB,
+    "xq_c1": 10 * KIB,
+    "bias0": 27 * KIB,
+    "staged_w4": 27 * KIB,
+    "staged_w6": 27 * KIB,
+    "staged_x1b": 27 * KIB,
+    "bias1": 12 * KIB,
+    "staged_x1a": 12 * KIB,
+    "raw_x1a": 15 * KIB,
+    "staged_x2": 15 * KIB,
+    "words2": 15 * KIB,
+    "scales1": 17 * KIB,
+    "rest1": 19 * KIB,
+    "xq_c2": 19 * KIB,
+    "rest2": 29 * KIB,
+    "xq_c3": 29 * KIB,
+    "bias2": 33 * KIB,
+    "staged_x3": 33 * KIB,
+    "words3": 33 * KIB,
+    "scales2": 35 * KIB,
 }
-
-TAKES_OVER = {
-    "raw_x1": "raw_w00",
-    "raw_x2": "raw_w10",
-    "raw_x3": "staged_w01",
-    "staged_x2": "raw_x1",
-    "staged_x3": "raw_x2",
-    "words1": "staged_w00",
-    "words2": "staged_x2",
-    "words3": "rest2",
-    "scales1": "rest1",
-    "done21": "staged_x3",
-}
-
-
-def home(name):
-    return home(TAKES_OVER[name]) if name in TAKES_OVER else FIRST_HOME[name]
 
 
 def tile_list_tiert_bias_kernel(
@@ -90,43 +87,55 @@ def tile_list_tiert_bias_kernel(
     nc = tc.nc
     with ExitStack() as ctx:
         keep = ctx.enter_context(tc.tile_pool(name="keep", bufs=1))
-        outp = ctx.enter_context(tc.tile_pool(name="outp", bufs=STAGES))
-        psum = ctx.enter_context(tc.psum_pool(name="psum", bufs=BANKS))
+        outp = ctx.enter_context(tc.tile_pool(name="outp", bufs=RESULTS))
+        psum = ctx.enter_context(tc.psum_pool(name="psum", bufs=1))
         shared = ctx.enter_context(tc.tile_pool(name="shared", bufs=1))
 
         def kept(shape, dtype, name):
             return keep.tile(shape, dtype, name=name, align_bytes=ALIGN)
 
         def placed(shape, dtype, name):
-            return shared.tile(shape, dtype, name=name, align_bytes=ALIGN, offset=home(name))
+            if name in HOME:
+                return shared.tile(shape, dtype, name=name, align_bytes=ALIGN, offset=HOME[name])
+            return kept(shape, dtype, name)
+
+        def bank(shape, number):
+            return psum.tile(shape, F32, name="bank%d" % number)
 
         offsets = keep.tile([P, J // LIST_ROWS], U16, name="offsets")
-        tab_s = placed([P, T // 4], I32, "tab_s")
+        tab_s = kept([P, T // 4], I32, "tab_s")
         wx_w = kept([P, N // 2], I32, "wx_w")
         b_rows = kept([P, P], F32, "b_rows")
-        ident_pe = kept([P, P], F32, "ident_pe")
         bias = kept([P, TILES], F32, "bias")
+        sel_in = placed([P, PACK, P, PACK], BF16, "sel_in")
         sel_c = kept([P, PACK * P], U32, "sel_c")
         sel_s = kept([P, PACK * P], U8, "sel_s")
-        halves = [(a, h) for a in range(2) for h in range(2)]
-        w_c = {k: kept([P, W], U32, "w_c%d%d" % k) for k in halves}
-        w_s = {k: kept([P, W], U8, "w_s%d%d" % k) for k in halves}
-        xq_c = [kept([P, W], U32, "xq_c%d" % c) for c in range(CHUNKS)]
+        w_c = {}
+        w_s = [kept([P, PIECE], U8, "w_s%d" % k) for k in range(len(W_BLOCKS))]
+        xq_c = {}
         xq_s = [kept([P, W], U8, "xq_s%d" % c) for c in range(CHUNKS)]
         xr_c = [kept([P, W], U32, "xr_c%d" % c) for c in range(CHUNKS)]
         xr_s = [kept([P, W], U8, "xr_s%d" % c) for c in range(CHUNKS)]
         t_c = [kept([P, 2, 2 * W], U8, "t_c%d" % c) for c in range(CHUNKS)]
+        low_s = [kept([P, n * W // 4], I32, "low_s%d" % g) for g, (c0, n) in enumerate(S_GROUPS)]
         raw = {}
 
         def load_block(key, rows):
-            raw[key] = placed([P, PACK, W], F32, "raw_" + key)
+            raw[key] = placed([P, PACK, rows.shape[1]], F32, "raw_" + key)
             nc.sync.dma_start(raw[key][:], rows.rearrange("(p i) j -> p i j", i=PACK))
 
-        def load_x(c):
-            load_block("x%d" % c, x[:, c * W : (c + 1) * W])
+        def x_pieces(c):
+            if c < 2:
+                return [("x%da" % c, 0, PIECE), ("x%db" % c, PIECE, PIECE)]
+            return [("x%d" % c, 0, W)]
 
-        def load_w(a, h):
-            load_block("w%d%d" % (a, h), wt[a * W : (a + 1) * W, h * W : (h + 1) * W])
+        def load_x(c):
+            for key, j0, cols in x_pieces(c):
+                load_block(key, x[:, c * W + j0 : c * W + j0 + cols])
+
+        def load_w(k):
+            a, n0 = W_BLOCKS[k]
+            load_block("w%d" % k, wt[a * W : (a + 1) * W, n0 : n0 + PIECE])
 
         nc.vector.memset(tab_s[:], 0)
         nc.sync.dma_start(offsets[:], offs)
@@ -134,62 +143,65 @@ def tile_list_tiert_bias_kernel(
         for r in range(SCALE_ROWS):
             rows = tab_scales[:, r:BLOCKS:SCALE_ROWS, :].bitcast(I32).rearrange("a q t -> q a t")
             nc.sync.dma_start(tab_s[r:P:LIFT, :], rows)
-
-        blank = placed([P, P], F32, "blank")
-        ident = placed([P, P], F32, "ident")
-        nc.gpsimd.memset(blank[:], 0.0)
-        make_identity(nc, ident[:])
-        nc.vector.tensor_copy(b_rows[:], blank[:])
-        nc.scalar.activation(ident_pe[:], ident[:], IDENT)
         load_x(0)
+        wx_s = placed([P, N // 4], I32, "wx_s")
+        nc.vector.memset(wx_s[:], 0)
+        nc.vector.memset(b_rows[:], 0.0)
+        for r in range(SCALE_ROWS):
+            nc.sync.dma_start(wx_s[r:P:QUADRANT, :], wx_scales[0, r:BLOCKS:SCALE_ROWS, :].bitcast(I32))
         nc.sync.dma_start(b_rows[0:TILES, :], b.rearrange("(m p) -> m p", p=P))
+        raw_tab = placed([P, T], I32, "raw_tab")
+        nc.sync.dma_start(raw_tab[:], tab_words[0].rearrange("p t y -> p (t y)").bitcast(I32))
+        load_w(0)
+        load_w(1)
+        ident = kept([P, P], F32, "ident")[:]
+        make_identity(nc, ident)
+        ident_pe = kept([P, P], F32, "ident_pe")
+        nc.scalar.activation(ident_pe[:], ident, IDENT)
 
-        sel_in = placed([P, PACK, P, PACK], BF16, "sel_in")
         sel_flat = sel_in[:].rearrange("p t m i -> p (t m i)")
         nc.vector.memset(sel_flat.bitcast(I32), 0)
         for t in range(PACK):
-            nc.vector.tensor_copy(sel_in[:, t, :, t], ident[:])
-        raw_tab = placed([P, T], I32, "raw_tab")
-        nc.sync.dma_start(raw_tab[:], tab_words[0].rearrange("p t y -> p (t y)").bitcast(I32))
-        wx_s = placed([P, N // 4], I32, "wx_s")
-        nc.vector.memset(wx_s[:], 0)
-        for r in range(SCALE_ROWS):
-            nc.sync.dma_start(wx_s[r:P:QUADRANT, :], wx_scales[0, r:BLOCKS:SCALE_ROWS, :].bitcast(I32))
+            nc.vector.tensor_copy(sel_in[:, t, :, t], ident)
         nc.vector.quantize_mx(sel_c[:].bitcast(FP8X4), sel_s[:], sel_flat)
 
-        low_s = placed([P, CHUNKS // PAIR, PAIR * W // 4], I32, "low_s")
-        nc.gpsimd.memset(low_s[P - QUADRANT : P, :, :], 0)
+        for g in range(len(S_GROUPS)):
+            nc.gpsimd.memset(low_s[g][P - QUADRANT : P, :], 0)
 
-        def runs_out(staged, lo, hi):
-            return staged[:, lo:hi, :].rearrange("p (c r) i -> p c i r", r=RUN)
+        def runs_out(ap, lo, hi):
+            return ap[:, lo:hi, :].rearrange("p (c r) i -> p c i r", r=RUN)
 
         def runs_in(ap):
             return ap.rearrange("p i (c r) -> p c i r", r=RUN)
 
-        def stage(key):
-            staged = placed([P, W, PACK], BF16, "staged_" + key)
-            v = V_SHARE[key]
-            nc.vector.tensor_copy(runs_out(staged, 0, v), runs_in(raw[key][:, :, 0:v]))
-            if v < W:
-                nc.scalar.activation(runs_out(staged, v, W), runs_in(raw[key][:, :, v:W]), IDENT)
-            return staged
+        staged = {}
 
-        def quantize(staged, codes, scales):
-            nc.vector.quantize_mx(codes[:].bitcast(FP8X4), scales[:], staged[:].rearrange("p j i -> p (j i)"))
+        def stage(key, v):
+            cols = raw[key].shape[2]
+            staged[key] = placed([P, cols, PACK], BF16, "staged_" + key)[:]
+            if v > 0:
+                nc.vector.tensor_copy(runs_out(staged[key], 0, v), runs_in(raw[key][:, :, 0:v]))
+            if v < cols:
+                nc.scalar.activation(runs_out(staged[key], v, cols), runs_in(raw[key][:, :, v:cols]), IDENT)
+
+        def quantize(src, codes, scales):
+            nc.vector.quantize_mx(codes.bitcast(FP8X4), scales, src.rearrange("p j i -> p (j i)"))
 
         def listed(first, count):
             return offsets[:, first * W // LIST_ROWS : (first + count) * W // LIST_ROWS]
 
-        words = {}
         t_s = {}
 
         def gather_scales(g):
-            both = placed([P, PAIR * W], U8, "scales%d" % g)
-            nc.vector.tensor_copy(both[:], tab_s[:].bitcast(U8).indirect(listed(PAIR * g, PAIR)))
-            nc.sync.dma_start(low_s[0 : P - LIFT, g, :], both[LIFT:P, :].bitcast(I32))
-            for d in range(PAIR):
-                t_s[PAIR * g + d, 0] = both[:, d * W : (d + 1) * W]
-                t_s[PAIR * g + d, 1] = low_s[:, g, :].bitcast(U8)[:, d * W : (d + 1) * W]
+            c0, n = S_GROUPS[g]
+            both = placed([P, n * W], U8, "scales%d" % g)
+            nc.vector.tensor_copy(both[:], tab_s[:].bitcast(U8).indirect(listed(c0, n)))
+            nc.sync.dma_start(low_s[g][0 : P - LIFT, :], both[LIFT:P, :].bitcast(I32))
+            for d in range(n):
+                t_s[c0 + d, 0] = both[:, d * W : (d + 1) * W]
+                t_s[c0 + d, 1] = low_s[g][:].bitcast(U8)[:, d * W : (d + 1) * W]
+
+        words = {}
 
         def gather_words(c):
             words[c] = placed([P, W], U32, "words%d" % c)
@@ -200,127 +212,172 @@ def tile_list_tiert_bias_kernel(
                 t_c[c][:].bitcast(U16), words[c][:].bitcast(U16).rearrange("p (j a) -> p a j", a=2)
             )
 
-        def quantize_w(a, h):
-            quantize(stage("w%d%d" % (a, h)), w_c[a, h], w_s[a, h])
+        def quantize_w(k):
+            w_c[k] = placed([P, PIECE], U32, "w_c%d" % k)
+            quantize(staged["w%d" % k], w_c[k][:], w_s[k][:])
 
-        def first_tier(c):
-            quantize(stage("x%d" % c), xq_c[c], xq_s[c])
+        def first_tier(c, v):
+            for key, j0, cols in x_pieces(c):
+                if key not in staged:
+                    stage(key, v)
+                if j0 == 0:
+                    xq_c[c] = placed([P, W], U32, "xq_c%d" % c)
+                quantize(staged[key], xq_c[c][:, j0 : j0 + cols], xq_s[c][:, j0 : j0 + cols])
 
-        def second_tier(c):
-            rest = placed([P, W, PACK], BF16, "rest%d" % c)
-            for s in range(HALF):
-                cols = slice(s * P, (s + 1) * P)
-                values = psum.tile([P, PACK, P], F32, name="bank")
-                for t in range(PACK):
-                    sel = slice(t * P, (t + 1) * P)
-                    nc.tensor.matmul_mx(
-                        values[:, t, :],
-                        lhsT=sel_c[:, sel].bitcast(FP8X4),
-                        lhsT_scale=sel_s[:, sel],
-                        rhs=xq_c[c][:, cols].bitcast(FP8X4),
-                        rhs_scale=xq_s[c][:, cols],
-                        start=True,
-                        stop=True,
-                    )
-                nc.vector.tensor_tensor(
-                    runs_out(rest, s * P, (s + 1) * P), runs_in(raw["x%d" % c][:, :, cols]), runs_in(values[:]), SUB
+        rest = {}
+
+        def residual(c, s, number):
+            if s == 0:
+                rest[c] = placed([P, W, PACK], BF16, "rest%d" % c)
+            cols = slice(s * P, (s + 1) * P)
+            values = bank([P, PACK, P], number)
+            for t in range(PACK):
+                sel = slice(t * P, (t + 1) * P)
+                nc.tensor.matmul_mx(
+                    values[:, t, :],
+                    lhsT=sel_c[:, sel].bitcast(FP8X4),
+                    lhsT_scale=sel_s[:, sel],
+                    rhs=xq_c[c][:, cols].bitcast(FP8X4),
+                    rhs_scale=xq_s[c][:, cols],
+                    start=True,
+                    stop=True,
                 )
-            quantize(rest, xr_c[c], xr_s[c])
+            key, j0, n = [pc for pc in x_pieces(c) if pc[1] <= s * P < pc[1] + pc[2]][0]
+            given = raw[key][:, :, s * P - j0 : (s + 1) * P - j0]
+            nc.vector.tensor_tensor(runs_out(rest[c], s * P, (s + 1) * P), runs_in(given), runs_in(values[:]), SUB)
+            if s == PARTS - 1:
+                quantize(rest[c][:], xr_c[c][:], xr_s[c][:])
 
         acc = {}
         passes_done = {}
-        done = {}
-        all_kinds = (0, 1, "q", "r")
 
-        def finish(c, m):
-            h = m // HALF
-            if (c, h) not in done:
-                name = "done%d%d" % (c, h)
-                if name in TAKES_OVER:
-                    done[c, h] = placed([P, HALF, W], F32, name)
-                else:
-                    done[c, h] = outp.tile([P, HALF, W], F32, name="done")
-            res = done[c, h][:, m % HALF, :]
-            if (c, m) in V_EMPTIES:
-                nc.vector.tensor_scalar_add(res, acc[c, m][:], bias[:, m : m + 1])
+        def bank_of(c, m):
+            return (m + HALF) % BANKS if c == 2 else m
+
+        def groups_of(c, m):
+            if (c, m) == (CHUNKS - 1, TILES - 1):
+                return [(s * P, P, s) for s in range(PARTS)]
+            return [(0, W, bank_of(c, m))]
+
+        def bias_of(c, m):
+            if c == 0 and m < HALF:
+                return pair_bias[m // 2][:, m % 2 : m % 2 + 1]
+            return (chunk1_bias if c == 1 else bias)[:, m : m + 1]
+
+        def finish(c, m, j0, n):
+            res = outp.tile([P, n], F32, name="done")
+            if c == CHUNKS - 1 and (m % 2 == 0 or j0 == W - P):
+                nc.vector.tensor_scalar_add(res[:], acc[c, m, j0][:], bias_of(c, m))
             else:
-                nc.scalar.activation(res, acc[c, m][:], IDENT, bias=bias[:, m : m + 1])
-            nc.sync.dma_start(out[m * P : (m + 1) * P, c * W : (c + 1) * W], res)
+                nc.scalar.activation(res[:], acc[c, m, j0][:], IDENT, bias=bias_of(c, m))
+            nc.sync.dma_start(out[m * P : (m + 1) * P, c * W + j0 : c * W + j0 + n], res[:])
 
-        def one_pass(kind, c, m):
-            if (c, m) not in acc:
-                acc[c, m] = psum.tile([P, W], F32, name="bank")
-                passes_done[c, m] = 0
-            first, last = passes_done[c, m] == 0, passes_done[c, m] == len(all_kinds) - 1
-            passes_done[c, m] = passes_done[c, m] + 1
+        def one_pass(kind, c, m, j0, n, number):
+            if (c, m, j0) not in acc:
+                acc[c, m, j0] = bank([P, n], number)
+                passes_done[c, m, j0] = 0
+            first, last = passes_done[c, m, j0] == 0, passes_done[c, m, j0] == KINDS - 1
+            passes_done[c, m, j0] = passes_done[c, m, j0] + 1
             if kind in ("q", "r"):
                 codes, scales = (xq_c, xq_s) if kind == "q" else (xr_c, xr_s)
                 lhsT = wx_w[:, m * P // 2 : (m + 1) * P // 2].bitcast(FP4X4)
                 lhsT_s = wx_s[:, m * P // 4 : (m + 1) * P // 4].bitcast(U8)
-                rhs, rhs_s = codes[c][:].bitcast(FP8X4), scales[c][:]
+                rhs, rhs_s = codes[c][:, j0 : j0 + n].bitcast(FP8X4), scales[c][:, j0 : j0 + n]
             else:
-                h, cols = m // HALF, slice((m % HALF) * P, (m % HALF + 1) * P)
-                lhsT, lhsT_s = w_c[kind, h][:, cols].bitcast(FP8X4), w_s[kind, h][:, cols]
-                rhs, rhs_s = t_c[c][:, kind, :].bitcast(FP4X4), t_s[c, kind]
+                n0 = m * P // PIECE * PIECE
+                k = W_BLOCKS.index((kind, n0))
+                cols = slice(m * P - n0, (m + 1) * P - n0)
+                lhsT, lhsT_s = w_c[k][:, cols].bitcast(FP8X4), w_s[k][:, cols]
+                rhs, rhs_s = t_c[c][:, kind, 2 * j0 : 2 * (j0 + n)].bitcast(FP4X4), t_s[c, kind][:, j0 : j0 + n]
             nc.tensor.matmul_mx(
-                acc[c, m][:], lhsT=lhsT, lhsT_scale=lhsT_s, rhs=rhs, rhs_scale=rhs_s, start=first, stop=last
+                acc[c, m, j0][:], lhsT=lhsT, lhsT_scale=lhsT_s, rhs=rhs, rhs_scale=rhs_s, start=first, stop=last
             )
             if last:
-                finish(c, m)
+                finish(c, m, j0, n)
 
         def by_kind(kinds, c, tiles):
             for kind in kinds:
                 for m in tiles:
-                    one_pass(kind, c, m)
+                    for group in groups_of(c, m):
+                        one_pass(kind, c, m, *group)
 
+        def by_tile(kinds, c, tiles):
+            for m in tiles:
+                for group in groups_of(c, m):
+                    for kind in kinds:
+                        one_pass(kind, c, m, *group)
+
+        table, own = (0, 1), ("q", "r")
         lower, upper = range(0, HALF), range(HALF, TILES)
-        third_pair, last_pair = upper[:2], upper[2:]
+        pairs = [(m, m + 1) for m in range(0, TILES, 2)]
 
-        load_w(0, 0)
         gather_scales(0)
-        first_tier(0)
-        load_w(1, 0)
-        second_tier(0)
-        b_cols = psum.tile([P, P], F32, name="bank")
+        first_tier(0, V_COLS)
+        b_cols = bank([P, P], 0)
         nc.tensor.transpose(b_cols[:], b_rows[:], ident_pe[:])
         nc.scalar.activation(bias[:], b_cols[:, 0:TILES], IDENT)
-        load_w(0, 1)
-        load_w(1, 1)
-        by_kind(("q", "r"), 0, range(TILES))
-
-        gather_words(0)
-        part_words(0)
-        quantize_w(0, 0)
-        load_x(1)
-        by_kind((0,), 0, lower)
-        gather_words(1)
-        quantize_w(1, 0)
-        load_x(2)
-        part_words(1)
-        quantize_w(0, 1)
-        load_x(3)
-        by_kind((1,), 0, lower)
-        by_kind((0,), 0, upper)
-        quantize_w(1, 1)
-        first_tier(1)
-        by_kind((0, 1), 1, lower)
-        by_kind((1,), 0, upper)
-        second_tier(1)
-        gather_scales(1)
-
+        pair_bias = [placed([P, 2], F32, "bias%d" % u) for u in range(2)]
+        for u in range(2):
+            nc.scalar.activation(pair_bias[u][:], b_cols[:, 2 * u : 2 * u + 2], IDENT)
+        chunk1_bias = placed([P, TILES], F32, "bias2")
+        nc.scalar.activation(chunk1_bias[:], b_cols[:, 0:TILES], IDENT)
+        for k in range(2, len(W_BLOCKS)):
+            load_w(k)
         for c in range(1, CHUNKS):
-            more = c + 1 < CHUNKS
-            if c > 1:
-                by_kind((0, 1), c, lower)
-            if more:
-                first_tier(c + 1)
+            load_x(c)
+        for s in range(PARTS):
+            residual(0, s, HALF + s)
+        by_kind(own, 0, range(TILES))
+
+        for k in range(4):
+            stage("w%d" % k, 0)
+        gather_words(0)
+        quantize_w(0)
+        part_words(0)
+        quantize_w(1)
+        by_kind(table, 0, pairs[0])
+        stage("w4", 0)
+        gather_words(1)
+        quantize_w(2)
+        part_words(1)
+        quantize_w(3)
+        by_tile(table, 1, pairs[0])
+        by_kind(table, 0, pairs[1])
+        stage("x1a", 0)
+        stage("w5", PIECE)
+        quantize_w(4)
+        quantize_w(5)
+        by_kind(table, 0, pairs[2])
+        by_tile(table, 1, pairs[1])
+        stage("w6", PIECE)
+        stage("w7", PIECE)
+        quantize_w(6)
+        quantize_w(7)
+        by_kind(table, 0, pairs[3])
+        first_tier(1, PIECE)
+
+        residual(1, 0, HALF)
+        residual(1, 1, HALF + 1)
+        by_kind(("q",), 1, lower)
+        residual(1, 2, HALF + 2)
+        residual(1, 3, HALF + 3)
+        first_tier(2, 0)
+        gather_scales(1)
+        gather_words(2)
+        part_words(2)
+        by_tile(table, 1, upper)
+        by_kind(("r",), 1, lower)
+        by_tile(own, 1, upper)
+        stage("x3", 0)
+
+        for c in range(2, CHUNKS):
+            for s in range(PARTS):
+                residual(c, s, bank_of(c, HALF + s))
+            if c + 1 < CHUNKS:
+                first_tier(c + 1, 0)
+                gather_scales(c)
                 gather_words(c + 1)
                 part_words(c + 1)
-            by_kind(("q", "r"), c, lower)
-            by_kind(all_kinds, c, third_pair)
-            if more:
-                second_tier(c + 1)
-                by_kind(all_kinds, c, last_pair)
-            else:
-                for m in last_pair:
-                    by_kind(all_kinds, c, (m,))
+            by_tile(table, c, lower)
+            by_kind(own, c, lower)
+            by_tile(own + table, c, upper)

@@ -32,52 +32,68 @@ QUADRANT = 32
 SCALE_ROWS = 4
 BLOCKS = 16
 LIFT = 16
-BANKS = 8
 RESULTS = 2 * TILES
+LATE_BANKS = (4, 5, 0, 1, 2, 3, 6, 7)
+HELD = ((0, 0), (0, 1), (1, 4), (1, 5))
 ALIGN = 64
 KIB = 1024
 
-V_COLS = 176
-
 W_BLOCKS = tuple((a, n0) for n0 in range(0, N, PIECE) for a in range(2))
 
-S_GROUPS = ((0, 2), (2, 1), (3, 1))
+S_GROUPS = ((0, 1), (1, 1), (2, 1), (3, 1))
 
 HOME = {
-    "sel_in": 0,
-    "staged_x0a": 1 * KIB,
-    "staged_x0b": 4 * KIB - ALIGN,
-    "scales0": 0,
-    "staged_w0": 3 * KIB,
-    "staged_w1": 5 * KIB,
-    "words0": 1 * KIB,
-    "w_c2": 1 * KIB,
-    "words1": 5 * KIB,
-    "w_c3": 5 * KIB,
-    "raw_w1": 8 * KIB,
-    "staged_w2": 8 * KIB,
-    "staged_w3": 10 * KIB,
-    "staged_w5": 10 * KIB,
-    "staged_w7": 10 * KIB,
-    "xq_c1": 10 * KIB,
-    "bias0": 27 * KIB,
-    "staged_w4": 27 * KIB,
-    "staged_w6": 27 * KIB,
-    "staged_x1b": 27 * KIB,
-    "bias1": 12 * KIB,
-    "staged_x1a": 12 * KIB,
-    "raw_x1a": 15 * KIB,
-    "staged_x2": 15 * KIB,
-    "words2": 15 * KIB,
-    "scales1": 17 * KIB,
-    "rest1": 19 * KIB,
-    "xq_c2": 19 * KIB,
-    "rest2": 29 * KIB,
-    "xq_c3": 29 * KIB,
-    "bias2": 33 * KIB,
-    "staged_x3": 33 * KIB,
-    "words3": 33 * KIB,
-    "scales2": 35 * KIB,
+    "sel_in": 0 * KIB,
+    "staged_x0a": 0 * KIB,
+    "scales0": 0 * KIB,
+    "staged_x0b": 4 * KIB,
+    "rest0": 4 * KIB,
+    "staged_x1b": 11 * KIB,
+    "rest1": 8 * KIB,
+    "xr_c0": 12 * KIB,
+    "raw_x0b": 14 * KIB,
+    "xq_c1": 14 * KIB,
+    "raw_x1a": 18 * KIB,
+    "w_c0": 18 * KIB,
+    "bias2": 19 * KIB,
+    "staged_w6": 19 * KIB,
+    "raw_x1b": 22 * KIB,
+    "w_c1": 22 * KIB,
+    "raw_w0": 26 * KIB,
+    "staged_w1": 26 * KIB,
+    "words0": 26 * KIB,
+    "w_c2": 26 * KIB,
+    "raw_w1": 30 * KIB,
+    "staged_w2": 30 * KIB,
+    "w_c3": 30 * KIB,
+    "scales1": 31 * KIB,
+    "bias": 32 * KIB,
+    "bias1": 33 * KIB,
+    "staged_x2": 33 * KIB,
+    "raw_w2": 37 * KIB,
+    "staged_w3": 37 * KIB,
+    "words1": 37 * KIB,
+    "staged_w4": 37 * KIB,
+    "w_c5": 37 * KIB,
+    "xq_c2": 38 * KIB,
+    "raw_w3": 41 * KIB,
+    "done0": 41 * KIB,
+    "done1": 43 * KIB,
+    "raw_w4": 45 * KIB,
+    "staged_w5": 45 * KIB,
+    "words2": 45 * KIB,
+    "scales2": 45 * KIB,
+    "raw_w5": 49 * KIB,
+    "w_c4": 49 * KIB,
+    "raw_w6": 53 * KIB,
+    "staged_w7": 53 * KIB,
+    "raw_w7": 57 * KIB,
+    "done2": 57 * KIB,
+    "done3": 59 * KIB,
+    "rest2": 63 * KIB,
+    "words3": 63 * KIB,
+    "scales3": 65 * KIB,
+    "staged_x3": 61 * KIB,
 }
 
 
@@ -106,7 +122,6 @@ def tile_list_tiert_bias_kernel(
         tab_s = kept([P, T // 4], I32, "tab_s")
         wx_w = kept([P, N // 2], I32, "wx_w")
         b_rows = kept([P, P], F32, "b_rows")
-        bias = kept([P, TILES], F32, "bias")
         sel_in = placed([P, PACK, P, PACK], BF16, "sel_in")
         sel_c = kept([P, PACK * P], U32, "sel_c")
         sel_s = kept([P, PACK * P], U8, "sel_s")
@@ -114,9 +129,9 @@ def tile_list_tiert_bias_kernel(
         w_s = [kept([P, PIECE], U8, "w_s%d" % k) for k in range(len(W_BLOCKS))]
         xq_c = {}
         xq_s = [kept([P, W], U8, "xq_s%d" % c) for c in range(CHUNKS)]
-        xr_c = [kept([P, W], U32, "xr_c%d" % c) for c in range(CHUNKS)]
+        xr_c = {}
         xr_s = [kept([P, W], U8, "xr_s%d" % c) for c in range(CHUNKS)]
-        t_c = [kept([P, 2, 2 * W], U8, "t_c%d" % c) for c in range(CHUNKS)]
+        t_c = {}
         low_s = [kept([P, n * W // 4], I32, "low_s%d" % g) for g, (c0, n) in enumerate(S_GROUPS)]
         raw = {}
 
@@ -129,50 +144,61 @@ def tile_list_tiert_bias_kernel(
                 return [("x%da" % c, 0, PIECE), ("x%db" % c, PIECE, PIECE)]
             return [("x%d" % c, 0, W)]
 
+        def piece(key):
+            c = int(key[1])
+            return [(c, j0, cols) for name, j0, cols in x_pieces(c) if name == key][0]
+
+        def load_piece(key):
+            c, j0, cols = piece(key)
+            load_block(key, x[:, c * W + j0 : c * W + j0 + cols])
+
         def load_x(c):
             for key, j0, cols in x_pieces(c):
-                load_block(key, x[:, c * W + j0 : c * W + j0 + cols])
+                load_piece(key)
 
         def load_w(k):
             a, n0 = W_BLOCKS[k]
             load_block("w%d" % k, wt[a * W : (a + 1) * W, n0 : n0 + PIECE])
-
-        nc.vector.memset(tab_s[:], 0)
-        nc.sync.dma_start(offsets[:], offs)
-        nc.sync.dma_start(wx_w[:], wx_words[0].bitcast(I32))
-        for r in range(SCALE_ROWS):
-            rows = tab_scales[:, r:BLOCKS:SCALE_ROWS, :].bitcast(I32).rearrange("a q t -> q a t")
-            nc.sync.dma_start(tab_s[r:P:LIFT, :], rows)
-        load_x(0)
-        wx_s = placed([P, N // 4], I32, "wx_s")
-        nc.vector.memset(wx_s[:], 0)
-        nc.vector.memset(b_rows[:], 0.0)
-        for r in range(SCALE_ROWS):
-            nc.sync.dma_start(wx_s[r:P:QUADRANT, :], wx_scales[0, r:BLOCKS:SCALE_ROWS, :].bitcast(I32))
-        nc.sync.dma_start(b_rows[0:TILES, :], b.rearrange("(m p) -> m p", p=P))
-        raw_tab = placed([P, T], I32, "raw_tab")
-        nc.sync.dma_start(raw_tab[:], tab_words[0].rearrange("p t y -> p (t y)").bitcast(I32))
-        load_w(0)
-        load_w(1)
-        ident = kept([P, P], F32, "ident")[:]
-        make_identity(nc, ident)
-        ident_pe = kept([P, P], F32, "ident_pe")
-        nc.scalar.activation(ident_pe[:], ident, IDENT)
-
-        sel_flat = sel_in[:].rearrange("p t m i -> p (t m i)")
-        nc.vector.memset(sel_flat.bitcast(I32), 0)
-        for t in range(PACK):
-            nc.vector.tensor_copy(sel_in[:, t, :, t], ident)
-        nc.vector.quantize_mx(sel_c[:].bitcast(FP8X4), sel_s[:], sel_flat)
-
-        for g in range(len(S_GROUPS)):
-            nc.gpsimd.memset(low_s[g][P - QUADRANT : P, :], 0)
 
         def runs_out(ap, lo, hi):
             return ap[:, lo:hi, :].rearrange("p (c r) i -> p c i r", r=RUN)
 
         def runs_in(ap):
             return ap.rearrange("p i (c r) -> p c i r", r=RUN)
+
+        wx_s = placed([P, N // 4], I32, "wx_s")
+        nc.vector.memset(tab_s[:], 0)
+        planes = kept([P, 2 * PACK - 1, P], BF16, "planes")
+        nc.gpsimd.memset(planes[:].rearrange("p u m -> p (u m)").bitcast(I32), 0)
+        ident = planes[:, PACK - 1, :]
+        make_identity(nc, ident, nomemset=True)
+        nc.gpsimd.memset(wx_s[:], 0)
+        nc.gpsimd.memset(b_rows[:], 0.0)
+        nc.sync.dma_start(offsets[:], offs)
+        load_piece("x0a")
+        for r in range(SCALE_ROWS):
+            rows = tab_scales[:, r:BLOCKS:SCALE_ROWS, :].bitcast(I32).rearrange("a q t -> q a t")
+            nc.sync.dma_start(tab_s[r:P:LIFT, :], rows)
+        load_piece("x0b")
+        nc.sync.dma_start(wx_w[:], wx_words[0].bitcast(I32))
+        for r in range(SCALE_ROWS):
+            nc.sync.dma_start(wx_s[r:P:QUADRANT, :], wx_scales[0, r:BLOCKS:SCALE_ROWS, :].bitcast(I32))
+        load_x(1)
+        nc.sync.dma_start(b_rows[0:TILES, :], b.rearrange("(m p) -> m p", p=P))
+        load_w(0)
+        load_w(1)
+        raw_tab = placed([P, T], I32, "raw_tab")
+        nc.sync.dma_start(raw_tab[:], tab_words[0].rearrange("p t y -> p (t y)").bitcast(I32))
+        ident_pe = kept([P, P], F32, "ident_pe")
+        nc.scalar.activation(ident_pe[:], ident, IDENT)
+
+        for t in range(PACK):
+            around = planes[:, PACK - 1 - t : 2 * PACK - 1 - t, :]
+            nc.vector.tensor_copy(runs_out(sel_in[:, t, :, :], 0, P), runs_in(around))
+        nc.vector.quantize_mx(sel_c[:].bitcast(FP8X4), sel_s[:], sel_in[:].rearrange("p t m i -> p (t m i)"))
+
+        for g in range(len(S_GROUPS)):
+            nc.gpsimd.memset(low_s[g][P - QUADRANT : P, :], 0)
 
         staged = {}
 
@@ -208,6 +234,7 @@ def tile_list_tiert_bias_kernel(
             nc.vector.tensor_copy(words[c][:], raw_tab[:].bitcast(U32).indirect(listed(c, 1)))
 
         def part_words(c):
+            t_c[c] = placed([P, 2, 2 * W], U8, "t_c%d" % c)
             nc.vector.tensor_copy(
                 t_c[c][:].bitcast(U16), words[c][:].bitcast(U16).rearrange("p (j a) -> p a j", a=2)
             )
@@ -216,13 +243,11 @@ def tile_list_tiert_bias_kernel(
             w_c[k] = placed([P, PIECE], U32, "w_c%d" % k)
             quantize(staged["w%d" % k], w_c[k][:], w_s[k][:])
 
-        def first_tier(c, v):
-            for key, j0, cols in x_pieces(c):
-                if key not in staged:
-                    stage(key, v)
-                if j0 == 0:
-                    xq_c[c] = placed([P, W], U32, "xq_c%d" % c)
-                quantize(staged[key], xq_c[c][:, j0 : j0 + cols], xq_s[c][:, j0 : j0 + cols])
+        def first_tier(key):
+            c, j0, cols = piece(key)
+            if j0 == 0:
+                xq_c[c] = placed([P, W], U32, "xq_c%d" % c)
+            quantize(staged[key], xq_c[c][:, j0 : j0 + cols], xq_s[c][:, j0 : j0 + cols])
 
         rest = {}
 
@@ -245,31 +270,32 @@ def tile_list_tiert_bias_kernel(
             key, j0, n = [pc for pc in x_pieces(c) if pc[1] <= s * P < pc[1] + pc[2]][0]
             given = raw[key][:, :, s * P - j0 : (s + 1) * P - j0]
             nc.vector.tensor_tensor(runs_out(rest[c], s * P, (s + 1) * P), runs_in(given), runs_in(values[:]), SUB)
-            if s == PARTS - 1:
-                quantize(rest[c][:], xr_c[c][:], xr_s[c][:])
+
+        def second_tier(c):
+            xr_c[c] = placed([P, W], U32, "xr_c%d" % c)
+            quantize(rest[c][:], xr_c[c][:], xr_s[c][:])
 
         acc = {}
         passes_done = {}
 
         def bank_of(c, m):
-            return (m + HALF) % BANKS if c == 2 else m
+            return HALF * c + m % HALF if c < 2 else LATE_BANKS[m]
 
         def groups_of(c, m):
             if (c, m) == (CHUNKS - 1, TILES - 1):
-                return [(s * P, P, s) for s in range(PARTS)]
+                return [(s * P, P, LATE_BANKS[s]) for s in range(PARTS)]
             return [(0, W, bank_of(c, m))]
 
-        def bias_of(c, m):
-            if c == 0 and m < HALF:
-                return pair_bias[m // 2][:, m % 2 : m % 2 + 1]
-            return (chunk1_bias if c == 1 else bias)[:, m : m + 1]
-
         def finish(c, m, j0, n):
-            res = outp.tile([P, n], F32, name="done")
-            if c == CHUNKS - 1 and (m % 2 == 0 or j0 == W - P):
-                nc.vector.tensor_scalar_add(res[:], acc[c, m, j0][:], bias_of(c, m))
+            if (c, m) in HELD:
+                res = placed([P, n], F32, "done%d" % HELD.index((c, m)))
             else:
-                nc.scalar.activation(res[:], acc[c, m, j0][:], IDENT, bias=bias_of(c, m))
+                res = outp.tile([P, n], F32, name="done")
+            col = pair_bias[m // 2][:, m % 2 : m % 2 + 1] if c == 0 and m // 2 in pair_bias else bias[:, m : m + 1]
+            if c == CHUNKS - 1 and (m % 2 == 0 or j0 == W - P):
+                nc.vector.tensor_scalar_add(res[:], acc[c, m, j0][:], col)
+            else:
+                nc.scalar.activation(res[:], acc[c, m, j0][:], IDENT, bias=col)
             nc.sync.dma_start(out[m * P : (m + 1) * P, c * W + j0 : c * W + j0 + n], res[:])
 
         def one_pass(kind, c, m, j0, n, number):
@@ -308,76 +334,97 @@ def tile_list_tiert_bias_kernel(
                         one_pass(kind, c, m, *group)
 
         table, own = (0, 1), ("q", "r")
-        lower, upper = range(0, HALF), range(HALF, TILES)
+        lower = range(0, HALF)
         pairs = [(m, m + 1) for m in range(0, TILES, 2)]
 
+        stage("x0a", PIECE)
+        first_tier("x0a")
         gather_scales(0)
-        first_tier(0, V_COLS)
-        b_cols = bank([P, P], 0)
-        nc.tensor.transpose(b_cols[:], b_rows[:], ident_pe[:])
-        nc.scalar.activation(bias[:], b_cols[:, 0:TILES], IDENT)
-        pair_bias = [placed([P, 2], F32, "bias%d" % u) for u in range(2)]
-        for u in range(2):
-            nc.scalar.activation(pair_bias[u][:], b_cols[:, 2 * u : 2 * u + 2], IDENT)
-        chunk1_bias = placed([P, TILES], F32, "bias2")
-        nc.scalar.activation(chunk1_bias[:], b_cols[:, 0:TILES], IDENT)
-        for k in range(2, len(W_BLOCKS)):
+        for k in range(2, 6):
             load_w(k)
-        for c in range(1, CHUNKS):
-            load_x(c)
+        load_x(2)
+        stage("x0b", 0)
+        first_tier("x0b")
         for s in range(PARTS):
             residual(0, s, HALF + s)
-        by_kind(own, 0, range(TILES))
-
-        for k in range(4):
-            stage("w%d" % k, 0)
-        gather_words(0)
-        quantize_w(0)
-        part_words(0)
-        quantize_w(1)
-        by_kind(table, 0, pairs[0])
-        stage("w4", 0)
-        gather_words(1)
-        quantize_w(2)
-        part_words(1)
-        quantize_w(3)
-        by_tile(table, 1, pairs[0])
-        by_kind(table, 0, pairs[1])
         stage("x1a", 0)
+        stage("x1b", 0)
+        by_kind(("q",), 0, lower)
+        first_tier("x1a")
+        first_tier("x1b")
+        second_tier(0)
+        for s in range(PARTS):
+            residual(1, s, HALF + s)
+        by_kind(("r",), 0, lower)
+        stage("w0", 0)
+        stage("w1", 0)
+        b_cols = bank([P, P], 2 * HALF - 1)
+        nc.tensor.transpose(b_cols[:], b_rows[:], ident_pe[:])
+        bias = placed([P, TILES], F32, "bias")
+        nc.scalar.activation(bias[:], b_cols[:, 0:TILES], IDENT)
+        pair_bias = {}
+        for u in (1, 2):
+            pair_bias[u] = placed([P, 2], F32, "bias%d" % u)
+            nc.scalar.activation(pair_bias[u][:], b_cols[:, 2 * u : 2 * u + 2], IDENT)
+        stage("w2", 0)
+        stage("w3", 0)
+        quantize_w(0)
+        quantize_w(1)
+        second_tier(1)
+        by_kind(own, 1, lower)
+
+        gather_words(0)
+        part_words(0)
+        quantize_w(2)
+        gather_scales(1)
+        load_w(6)
+        load_w(7)
+        load_x(3)
+        quantize_w(3)
+        gather_words(1)
+        part_words(1)
+        by_tile(table, 0, pairs[0])
+        by_kind(table, 0, pairs[1])
+        by_tile(own, 0, pairs[2])
+        stage("x2", 0)
+        by_tile(own, 0, pairs[3])
+        by_tile(table, 1, pairs[0])
+        stage("w4", PIECE)
         stage("w5", PIECE)
         quantize_w(4)
         quantize_w(5)
-        by_kind(table, 0, pairs[2])
-        by_tile(table, 1, pairs[1])
-        stage("w6", PIECE)
-        stage("w7", PIECE)
-        quantize_w(6)
-        quantize_w(7)
-        by_kind(table, 0, pairs[3])
-        first_tier(1, PIECE)
-
-        residual(1, 0, HALF)
-        residual(1, 1, HALF + 1)
-        by_kind(("q",), 1, lower)
-        residual(1, 2, HALF + 2)
-        residual(1, 3, HALF + 3)
-        first_tier(2, 0)
-        gather_scales(1)
         gather_words(2)
         part_words(2)
-        by_tile(table, 1, upper)
-        by_kind(("r",), 1, lower)
-        by_tile(own, 1, upper)
-        stage("x3", 0)
+        gather_scales(2)
+        first_tier("x2")
+        by_tile(table, 1, pairs[1])
+        by_tile(table, 0, pairs[2])
+        stage("w6", 0)
+        stage("w7", 0)
+        by_tile(own, 1, pairs[2])
+        by_tile(own, 1, pairs[3])
+        residual(2, 0, 0)
+        residual(2, 1, 1)
+        quantize_w(6)
+        by_tile(table, 1, pairs[2])
+        residual(2, 2, 0)
+        quantize_w(7)
+        residual(2, 3, 1)
+        second_tier(2)
+        by_kind(table, 0, pairs[3])
+        by_tile(table, 1, pairs[3])
 
-        for c in range(2, CHUNKS):
-            for s in range(PARTS):
-                residual(c, s, bank_of(c, HALF + s))
-            if c + 1 < CHUNKS:
-                first_tier(c + 1, 0)
-                gather_scales(c)
-                gather_words(c + 1)
-                part_words(c + 1)
-            by_tile(table, c, lower)
-            by_kind(own, c, lower)
-            by_tile(own + table, c, upper)
+        gather_words(3)
+        gather_scales(3)
+        part_words(3)
+        stage("x3", W)
+        first_tier("x3")
+        by_tile(table + own, 2, range(HALF + 1))
+        residual(3, 0, LATE_BANKS[0])
+        residual(3, 1, LATE_BANKS[1])
+        by_tile(table + own, 2, (HALF + 1,))
+        residual(3, 2, LATE_BANKS[2])
+        residual(3, 3, LATE_BANKS[3])
+        second_tier(3)
+        by_tile(table + own, 2, range(HALF + 2, TILES))
+        by_tile(table + own, 3, range(TILES))

@@ -16,6 +16,7 @@ FP8X4 = mybir.dt.float8_e4m3fn_x4
 FP4X4 = mybir.dt.float4_e2m1fn_x4
 IDENT = mybir.ActivationFunctionType.Identity
 SUB = mybir.AluOpType.subtract
+ADD = mybir.AluOpType.add
 
 P = 128
 PACK = 4
@@ -34,7 +35,8 @@ BLOCKS = 16
 LIFT = 16
 RESULTS = 2 * TILES
 LATE_BANKS = (4, 5, 0, 1, 2, 3, 6, 7)
-HELD = ((0, 0), (0, 1), (1, 4), (1, 5))
+HELD = ()
+SPLIT = ((0, 4), (0, 5), (0, 6), (0, 7))
 ALIGN = 64
 KIB = 1024
 
@@ -45,55 +47,39 @@ S_GROUPS = ((0, 1), (1, 1), (2, 1), (3, 1))
 HOME = {
     "sel_in": 0 * KIB,
     "staged_x0a": 0 * KIB,
-    "scales0": 0 * KIB,
-    "staged_x0b": 4 * KIB,
-    "rest0": 4 * KIB,
-    "staged_x1b": 11 * KIB,
-    "rest1": 8 * KIB,
-    "xr_c0": 12 * KIB,
-    "raw_x0b": 14 * KIB,
-    "xq_c1": 14 * KIB,
-    "raw_x1a": 18 * KIB,
-    "w_c0": 18 * KIB,
-    "bias2": 19 * KIB,
-    "staged_w6": 19 * KIB,
-    "raw_x1b": 22 * KIB,
-    "w_c1": 22 * KIB,
-    "raw_w0": 26 * KIB,
-    "staged_w1": 26 * KIB,
-    "words0": 26 * KIB,
-    "w_c2": 26 * KIB,
-    "raw_w1": 30 * KIB,
-    "staged_w2": 30 * KIB,
-    "w_c3": 30 * KIB,
-    "scales1": 31 * KIB,
-    "bias": 32 * KIB,
-    "bias1": 33 * KIB,
-    "staged_x2": 33 * KIB,
-    "raw_w2": 37 * KIB,
-    "staged_w3": 37 * KIB,
-    "words1": 37 * KIB,
-    "staged_w4": 37 * KIB,
-    "w_c5": 37 * KIB,
-    "xq_c2": 38 * KIB,
-    "raw_w3": 41 * KIB,
-    "done0": 41 * KIB,
-    "done1": 43 * KIB,
-    "raw_w4": 45 * KIB,
-    "staged_w5": 45 * KIB,
-    "words2": 45 * KIB,
-    "scales2": 45 * KIB,
-    "raw_w5": 49 * KIB,
-    "w_c4": 49 * KIB,
-    "raw_w6": 53 * KIB,
-    "staged_w7": 53 * KIB,
-    "raw_w7": 57 * KIB,
-    "done2": 57 * KIB,
-    "done3": 59 * KIB,
-    "rest2": 63 * KIB,
-    "words3": 63 * KIB,
-    "scales3": 65 * KIB,
-    "staged_x3": 61 * KIB,
+    "scales0": 2 * KIB,
+    "staged_x1b": 7 * KIB,
+    "rest1": 4 * KIB,
+    "xr_c0": 8 * KIB,
+    "raw_x0a": 10 * KIB,
+    "xq_c1": 10 * KIB,
+    "raw_x1a": 14 * KIB,
+    "w_c0": 14 * KIB,
+    "raw_x1b": 18 * KIB,
+    "w_c1": 18 * KIB,
+    "staged_w1": 22 * KIB,
+    "scales1": 22 * KIB,
+    "words0": 24 * KIB,
+    "words1": 24 * KIB,
+    "staged_w2": 26 * KIB,
+    "t_c1": 26 * KIB,
+    "raw_w5": 28 * KIB,
+    "late_bias": 28 * KIB,
+    "staged_w4": 32 * KIB,
+    "words2": 32 * KIB,
+    "bias1_2": 34 * KIB,
+    "staged_x2": 34 * KIB,
+    "staged_w5": 38 * KIB,
+    "scales2": 38 * KIB,
+    "staged_w6": 39 * KIB,
+    "raw_x3": 39 * KIB,
+    "raw_x2": 47 * KIB,
+    "xq_c3": 47 * KIB,
+    "rest2": 55 * KIB,
+    "scales3": 55 * KIB,
+    "words3": 56 * KIB,
+    "bias1_6": 59 * KIB,
+    "staged_x3": 59 * KIB,
 }
 
 
@@ -160,6 +146,10 @@ def tile_list_tiert_bias_kernel(
             a, n0 = W_BLOCKS[k]
             load_block("w%d" % k, wt[a * W : (a + 1) * W, n0 : n0 + PIECE])
 
+        def load_table():
+            raw["tab"] = placed([P, T], I32, "raw_tab")
+            nc.sync.dma_start(raw["tab"][:], tab_words[0].rearrange("p t y -> p (t y)").bitcast(I32))
+
         def runs_out(ap, lo, hi):
             return ap[:, lo:hi, :].rearrange("p (c r) i -> p c i r", r=RUN)
 
@@ -172,23 +162,22 @@ def tile_list_tiert_bias_kernel(
         nc.gpsimd.memset(planes[:].rearrange("p u m -> p (u m)").bitcast(I32), 0)
         ident = planes[:, PACK - 1, :]
         make_identity(nc, ident, nomemset=True)
-        nc.gpsimd.memset(wx_s[:], 0)
         nc.gpsimd.memset(b_rows[:], 0.0)
+        nc.gpsimd.memset(wx_s[:], 0)
         nc.sync.dma_start(offsets[:], offs)
         load_piece("x0a")
         for r in range(SCALE_ROWS):
             rows = tab_scales[:, r:BLOCKS:SCALE_ROWS, :].bitcast(I32).rearrange("a q t -> q a t")
             nc.sync.dma_start(tab_s[r:P:LIFT, :], rows)
+        nc.sync.dma_start(b_rows[0:TILES, :], b.rearrange("(m p) -> m p", p=P))
         load_piece("x0b")
         nc.sync.dma_start(wx_w[:], wx_words[0].bitcast(I32))
         for r in range(SCALE_ROWS):
             nc.sync.dma_start(wx_s[r:P:QUADRANT, :], wx_scales[0, r:BLOCKS:SCALE_ROWS, :].bitcast(I32))
         load_x(1)
-        nc.sync.dma_start(b_rows[0:TILES, :], b.rearrange("(m p) -> m p", p=P))
         load_w(0)
         load_w(1)
-        raw_tab = placed([P, T], I32, "raw_tab")
-        nc.sync.dma_start(raw_tab[:], tab_words[0].rearrange("p t y -> p (t y)").bitcast(I32))
+        load_table()
         ident_pe = kept([P, P], F32, "ident_pe")
         nc.scalar.activation(ident_pe[:], ident, IDENT)
 
@@ -231,7 +220,7 @@ def tile_list_tiert_bias_kernel(
 
         def gather_words(c):
             words[c] = placed([P, W], U32, "words%d" % c)
-            nc.vector.tensor_copy(words[c][:], raw_tab[:].bitcast(U32).indirect(listed(c, 1)))
+            nc.vector.tensor_copy(words[c][:], raw["tab"][:].bitcast(U32).indirect(listed(c, 1)))
 
         def part_words(c):
             t_c[c] = placed([P, 2, 2 * W], U8, "t_c%d" % c)
@@ -275,35 +264,42 @@ def tile_list_tiert_bias_kernel(
             xr_c[c] = placed([P, W], U32, "xr_c%d" % c)
             quantize(rest[c][:], xr_c[c][:], xr_s[c][:])
 
+        table, own = (0, 1), ("q", "r")
+        bias = kept([P, TILES], F32, "bias")
+        own_bias = {}
+        late = {}
         acc = {}
         passes_done = {}
 
-        def bank_of(c, m):
-            return HALF * c + m % HALF if c < 2 else LATE_BANKS[m]
+        own_sum = {}
 
-        def groups_of(c, m):
-            if (c, m) == (CHUNKS - 1, TILES - 1):
-                return [(s * P, P, LATE_BANKS[s]) for s in range(PARTS)]
-            return [(0, W, bank_of(c, m))]
-
-        def finish(c, m, j0, n):
+        def finish(c, m, j0, n, part, on_vector):
+            psum_sum = acc[c, m, j0, part][:]
+            col = own_bias[c, m][:] if (c, m) in own_bias else (bias if part == "own" else late.get("bias"))[:, m : m + 1]
+            if part == "own":
+                own_sum[c, m] = placed([P, n], F32, "own%d_%d" % (c, m))
+                nc.scalar.activation(own_sum[c, m][:], psum_sum, IDENT, bias=col)
+                return
             if (c, m) in HELD:
                 res = placed([P, n], F32, "done%d" % HELD.index((c, m)))
             else:
                 res = outp.tile([P, n], F32, name="done")
-            col = pair_bias[m // 2][:, m % 2 : m % 2 + 1] if c == 0 and m // 2 in pair_bias else bias[:, m : m + 1]
-            if c == CHUNKS - 1 and (m % 2 == 0 or j0 == W - P):
-                nc.vector.tensor_scalar_add(res[:], acc[c, m, j0][:], col)
+            if part == "table":
+                nc.vector.tensor_tensor(res[:], psum_sum, own_sum[c, m][:], ADD)
+            elif on_vector:
+                nc.vector.tensor_scalar_add(res[:], psum_sum, col)
             else:
-                nc.scalar.activation(res[:], acc[c, m, j0][:], IDENT, bias=col)
+                nc.scalar.activation(res[:], psum_sum, IDENT, bias=col)
             nc.sync.dma_start(out[m * P : (m + 1) * P, c * W + j0 : c * W + j0 + n], res[:])
 
-        def one_pass(kind, c, m, j0, n, number):
-            if (c, m, j0) not in acc:
-                acc[c, m, j0] = bank([P, n], number)
-                passes_done[c, m, j0] = 0
-            first, last = passes_done[c, m, j0] == 0, passes_done[c, m, j0] == KINDS - 1
-            passes_done[c, m, j0] = passes_done[c, m, j0] + 1
+        def one_pass(kind, c, m, number, j0=0, n=W, on_vector=False):
+            part = ("own" if kind in own else "table") if (c, m) in SPLIT else "all"
+            key = (c, m, j0, part)
+            if key not in acc:
+                acc[key] = bank([P, n], number)
+                passes_done[key] = 0
+            first, last = passes_done[key] == 0, passes_done[key] == (KINDS if part == "all" else KINDS // 2) - 1
+            passes_done[key] = passes_done[key] + 1
             if kind in ("q", "r"):
                 codes, scales = (xq_c, xq_s) if kind == "q" else (xr_c, xr_s)
                 lhsT = wx_w[:, m * P // 2 : (m + 1) * P // 2].bitcast(FP4X4)
@@ -316,115 +312,132 @@ def tile_list_tiert_bias_kernel(
                 lhsT, lhsT_s = w_c[k][:, cols].bitcast(FP8X4), w_s[k][:, cols]
                 rhs, rhs_s = t_c[c][:, kind, 2 * j0 : 2 * (j0 + n)].bitcast(FP4X4), t_s[c, kind][:, j0 : j0 + n]
             nc.tensor.matmul_mx(
-                acc[c, m, j0][:], lhsT=lhsT, lhsT_scale=lhsT_s, rhs=rhs, rhs_scale=rhs_s, start=first, stop=last
+                acc[key][:], lhsT=lhsT, lhsT_scale=lhsT_s, rhs=rhs, rhs_scale=rhs_s, start=first, stop=last
             )
             if last:
-                finish(c, m, j0, n)
+                finish(c, m, j0, n, part, on_vector)
 
-        def by_kind(kinds, c, tiles):
+        def by_kind(kinds, c, tiles, banks):
             for kind in kinds:
-                for m in tiles:
-                    for group in groups_of(c, m):
-                        one_pass(kind, c, m, *group)
+                for m, number in zip(tiles, banks):
+                    one_pass(kind, c, m, number)
 
-        def by_tile(kinds, c, tiles):
-            for m in tiles:
-                for group in groups_of(c, m):
-                    for kind in kinds:
-                        one_pass(kind, c, m, *group)
+        def by_tile(kinds, c, tiles, banks):
+            for m, number in zip(tiles, banks):
+                for kind in kinds:
+                    one_pass(kind, c, m, number)
 
-        table, own = (0, 1), ("q", "r")
-        lower = range(0, HALF)
-        pairs = [(m, m + 1) for m in range(0, TILES, 2)]
+        def last_chunk(banks):
+            c = CHUNKS - 1
+            for kind in table + own:
+                for m in range(HALF):
+                    one_pass(kind, c, m, banks[m], on_vector=m % 2 == 0)
+            for m in range(HALF, TILES - 1):
+                for kind in table + own:
+                    one_pass(kind, c, m, banks[m], on_vector=m % 2 == 0)
+            for s in range(PARTS):
+                for kind in table + own:
+                    one_pass(kind, c, TILES - 1, banks[s], s * P, P, s == PARTS - 1)
 
+        def copy_bias():
+            late["bias"] = placed([P, TILES], F32, "late_bias")
+            nc.scalar.activation(late["bias"][:], bias[:], IDENT)
+
+        def make_bias(number, pairs):
+            b_cols = bank([P, P], number)
+            nc.tensor.transpose(b_cols[:], b_rows[:], ident_pe[:])
+            nc.scalar.activation(bias[:], b_cols[:, 0:TILES], IDENT)
+            for c, m in pairs:
+                own_bias[c, m] = placed([P, 1], F32, "bias%d_%d" % (c, m))
+                nc.scalar.activation(own_bias[c, m][:], b_cols[:, m : m + 1], IDENT)
+
+        make_bias(3, ((1, 2), (1, 6)))
         stage("x0a", PIECE)
-        first_tier("x0a")
         gather_scales(0)
-        for k in range(2, 6):
-            load_w(k)
-        load_x(2)
+        first_tier("x0a")
+        load_w(2)
+        load_w(3)
+        load_w(4)
+        load_w(5)
         stage("x0b", 0)
         first_tier("x0b")
         for s in range(PARTS):
             residual(0, s, HALF + s)
         stage("x1a", 0)
         stage("x1b", 0)
-        by_kind(("q",), 0, lower)
+        by_kind(("q",), 0, (4, 5, 6, 7), (0, 1, 2, 3))
         first_tier("x1a")
         first_tier("x1b")
         second_tier(0)
-        for s in range(PARTS):
-            residual(1, s, HALF + s)
-        by_kind(("r",), 0, lower)
+        residual(1, 0, 4)
+        residual(1, 1, 5)
+        residual(1, 2, 6)
+        residual(1, 3, 7)
         stage("w0", 0)
         stage("w1", 0)
-        b_cols = bank([P, P], 2 * HALF - 1)
-        nc.tensor.transpose(b_cols[:], b_rows[:], ident_pe[:])
-        bias = placed([P, TILES], F32, "bias")
-        nc.scalar.activation(bias[:], b_cols[:, 0:TILES], IDENT)
-        pair_bias = {}
-        for u in (1, 2):
-            pair_bias[u] = placed([P, 2], F32, "bias%d" % u)
-            nc.scalar.activation(pair_bias[u][:], b_cols[:, 2 * u : 2 * u + 2], IDENT)
-        stage("w2", 0)
-        stage("w3", 0)
+        by_kind(("r",), 0, (4, 5, 6, 7), (0, 1, 2, 3))
         quantize_w(0)
         quantize_w(1)
         second_tier(1)
-        by_kind(own, 1, lower)
-
-        gather_words(0)
-        part_words(0)
-        quantize_w(2)
         gather_scales(1)
         load_w(6)
         load_w(7)
-        load_x(3)
-        quantize_w(3)
+        load_x(2)
+        by_kind(("q",), 1, (0, 1, 2, 3), (4, 5, 6, 7))
+        by_tile(own, 0, (0, 1), (0, 1))
+        by_kind(("r",), 1, (0, 1, 2, 3), (4, 5, 6, 7))
+        by_tile(own, 0, (2, 3), (2, 3))
+        stage("w2", 0)
+        stage("w3", 0)
+        stage("w4", 0)
+        stage("w5", 0)
+        copy_bias()
+        gather_words(0)
+        part_words(0)
         gather_words(1)
+        quantize_w(2)
         part_words(1)
-        by_tile(table, 0, pairs[0])
-        by_kind(table, 0, pairs[1])
-        by_tile(own, 0, pairs[2])
-        stage("x2", 0)
-        by_tile(own, 0, pairs[3])
-        by_tile(table, 1, pairs[0])
-        stage("w4", PIECE)
-        stage("w5", PIECE)
+        quantize_w(3)
+        by_tile(table, 0, (0, 1), (0, 1))
+        by_kind((0,), 0, (2, 3), (2, 3))
+        by_tile(table, 1, (0, 1), (4, 5))
         quantize_w(4)
-        quantize_w(5)
         gather_words(2)
+        quantize_w(5)
         part_words(2)
+        by_kind((1,), 0, (2, 3), (2, 3))
+        by_tile(table, 1, (2, 3), (6, 7))
+        by_tile(own, 1, (4, 5), (4, 5))
+        stage("w6", PIECE)
+        stage("w7", PIECE)
+        stage("x2", 0)
         gather_scales(2)
+        quantize_w(6)
+        load_x(3)
+        quantize_w(7)
+        by_tile(table, 0, (4, 5), (0, 1))
         first_tier("x2")
-        by_tile(table, 1, pairs[1])
-        by_tile(table, 0, pairs[2])
-        stage("w6", 0)
-        stage("w7", 0)
-        by_tile(own, 1, pairs[2])
-        by_tile(own, 1, pairs[3])
+        by_tile(own, 1, (6, 7), (6, 7))
+        by_tile(table, 1, (4, 5), (4, 5))
+        by_tile(table, 0, (6, 7), (2, 3))
+        by_tile(table, 1, (6, 7), (6, 7))
+        stage("x3", 0)
         residual(2, 0, 0)
         residual(2, 1, 1)
-        quantize_w(6)
-        by_tile(table, 1, pairs[2])
-        residual(2, 2, 0)
-        quantize_w(7)
-        residual(2, 3, 1)
+        residual(2, 2, 4)
+        residual(2, 3, 5)
         second_tier(2)
-        by_kind(table, 0, pairs[3])
-        by_tile(table, 1, pairs[3])
-
-        gather_words(3)
         gather_scales(3)
-        part_words(3)
-        stage("x3", W)
+        gather_words(3)
         first_tier("x3")
-        by_tile(table + own, 2, range(HALF + 1))
-        residual(3, 0, LATE_BANKS[0])
-        residual(3, 1, LATE_BANKS[1])
-        by_tile(table + own, 2, (HALF + 1,))
-        residual(3, 2, LATE_BANKS[2])
-        residual(3, 3, LATE_BANKS[3])
+        part_words(3)
+        by_tile((0, "q", 1), 2, range(6), (2, 3, 6, 7, 0, 1))
+        by_kind(("r",), 2, range(6), (2, 3, 6, 7, 0, 1))
+        by_tile(table + own, 2, (6,), (4,))
+        residual(3, 0, 2)
+        residual(3, 1, 3)
+        residual(3, 2, 6)
+        residual(3, 3, 7)
         second_tier(3)
-        by_tile(table + own, 2, range(HALF + 2, TILES))
-        by_tile(table + own, 3, range(TILES))
+        by_tile(table + own, 2, (7,), (5,))
+        last_chunk((0, 1, 4, 2, 3, 6, 7, 5))

@@ -17,69 +17,60 @@ FP4X4 = mybir.dt.float4_e2m1fn_x4
 IDENT = mybir.ActivationFunctionType.Identity
 SUB = mybir.AluOpType.subtract
 ADD = mybir.AluOpType.add
+MULT = mybir.AluOpType.mult
 
 P = 128
 PACK = 4
 W = 512
 CHUNKS = J // W
 TILES = N // P
-HALF = TILES // 2
 PARTS = W // P
 PIECE = W // 2
-KINDS = 4
 RUN = 4
 LIST_ROWS = 16
 QUADRANT = 32
 SCALE_ROWS = 4
 BLOCKS = 16
 LIFT = 16
-RESULTS = 2 * TILES
-LATE_BANKS = (4, 5, 0, 1, 2, 3, 6, 7)
-HELD = ()
-SPLIT = ((0, 4), (0, 5), (0, 6), (0, 7))
+RESULTS = 20
+PAD = 16
 ALIGN = 64
 KIB = 1024
 
-W_BLOCKS = tuple((a, n0) for n0 in range(0, N, PIECE) for a in range(2))
-
+X_PIECES = {"x0a": (0, 0, 256), "x0b": (0, 256, 256), "x1a": (1, 0, 256), "x1b": (1, 256, 256), "x2a": (2, 0, 256), "x2b": (2, 256, 256), "x3": (3, 0, 512)}
+W_BLOCKS = {"w%d" % (2 * u + a): (a, u * PIECE, PIECE) for u in range(4) for a in range(2)}
 S_GROUPS = ((0, 1), (1, 1), (2, 1), (3, 1))
-
+SPLIT = ((0, 2), (0, 3), (0, 4), (0, 5), (0, 6), (0, 7))
+STAGED_TOGETHER = [("w1", "w2"), ("w4", "w5"), ("x2a", "x2b"), ("x1a", "x1b")]
+WORDS_TOGETHER = {0: 2}
 HOME = {
-    "sel_in": 0 * KIB,
-    "staged_x0a": 0 * KIB,
-    "scales0": 2 * KIB,
-    "staged_x1b": 7 * KIB,
-    "rest1": 4 * KIB,
-    "xr_c0": 8 * KIB,
-    "raw_x0a": 10 * KIB,
-    "xq_c1": 10 * KIB,
-    "raw_x1a": 14 * KIB,
-    "w_c0": 14 * KIB,
-    "raw_x1b": 18 * KIB,
-    "w_c1": 18 * KIB,
-    "staged_w1": 22 * KIB,
-    "scales1": 22 * KIB,
-    "words0": 24 * KIB,
-    "words1": 24 * KIB,
-    "staged_w2": 26 * KIB,
-    "t_c1": 26 * KIB,
-    "raw_w5": 28 * KIB,
-    "late_bias": 28 * KIB,
-    "staged_w4": 32 * KIB,
-    "words2": 32 * KIB,
-    "bias1_2": 34 * KIB,
-    "staged_x2": 34 * KIB,
-    "staged_w5": 38 * KIB,
-    "scales2": 38 * KIB,
-    "staged_w6": 39 * KIB,
-    "raw_x3": 39 * KIB,
-    "raw_x2": 47 * KIB,
-    "xq_c3": 47 * KIB,
-    "rest2": 55 * KIB,
-    "scales3": 55 * KIB,
-    "words3": 56 * KIB,
-    "bias1_6": 59 * KIB,
-    "staged_x3": 59 * KIB,
+    "sel_in": 2 * KIB,
+    "staged_x0a": 2 * KIB,
+    "staged_x0b": 0 * KIB + 64,
+    "scales0": 2 * KIB + 64,
+    "staged_x1a": 3 * KIB,
+    "bias": 6 * KIB + 512,
+    "raw_x0a": 7 * KIB,
+    "scales1": 7 * KIB,
+    "raw_x1a": 11 * KIB,
+    "c_w0": 11 * KIB,
+    "rest1": 18 * KIB + 960,
+    "words0": 15 * KIB,
+    "staged_w3": 19 * KIB,
+    "staged_w1": 21 * KIB,
+    "scales2": 24 * KIB + 512,
+    "staged_w4": 17 * KIB,
+    "staged_w6": 15 * KIB + 512,
+    "words2": 15 * KIB,
+    "own0_2": 25 * KIB,
+    "staged_w7": 25 * KIB,
+    "staged_x2a": 26 * KIB,
+    "staged_x3": 26 * KIB,
+    "raw_x2b": 30 * KIB,
+    "scales3": 30 * KIB,
+    "words3": 31 * KIB,
+    "raw_w3": 34 * KIB,
+    "late_bias": 34 * KIB,
 }
 
 
@@ -93,62 +84,53 @@ def tile_list_tiert_bias_kernel(
         psum = ctx.enter_context(tc.psum_pool(name="psum", bufs=1))
         shared = ctx.enter_context(tc.tile_pool(name="shared", bufs=1))
 
-        def kept(shape, dtype, name):
-            return keep.tile(shape, dtype, name=name, align_bytes=ALIGN)
-
         def placed(shape, dtype, name):
             if name in HOME:
                 return shared.tile(shape, dtype, name=name, align_bytes=ALIGN, offset=HOME[name])
-            return kept(shape, dtype, name)
+            return keep.tile(shape, dtype, name=name, align_bytes=ALIGN)
 
         def bank(shape, number):
             return psum.tile(shape, F32, name="bank%d" % number)
 
         offsets = keep.tile([P, J // LIST_ROWS], U16, name="offsets")
-        tab_s = kept([P, T // 4], I32, "tab_s")
-        wx_w = kept([P, N // 2], I32, "wx_w")
-        b_rows = kept([P, P], F32, "b_rows")
-        sel_in = placed([P, PACK, P, PACK], BF16, "sel_in")
-        sel_c = kept([P, PACK * P], U32, "sel_c")
-        sel_s = kept([P, PACK * P], U8, "sel_s")
-        w_c = {}
-        w_s = [kept([P, PIECE], U8, "w_s%d" % k) for k in range(len(W_BLOCKS))]
-        xq_c = {}
-        xq_s = [kept([P, W], U8, "xq_s%d" % c) for c in range(CHUNKS)]
-        xr_c = {}
-        xr_s = [kept([P, W], U8, "xr_s%d" % c) for c in range(CHUNKS)]
-        t_c = {}
-        low_s = [kept([P, n * W // 4], I32, "low_s%d" % g) for g, (c0, n) in enumerate(S_GROUPS)]
-        raw = {}
+        tab_s = placed([P, T // 4], I32, "tab_s")
+        wx_w = placed([P, N // 2], I32, "wx_w")
+        wx_s = placed([P, N // 4], I32, "wx_s")
+        sel_c = placed([P, PAD + PACK * P], U32, "sel_c")
+        sel_s = placed([P, 2 * P], U8, "sel_s")
+        low_all = placed([P, J // 4], I32, "low_all")
+        low_s = [low_all[:, c0 * W // 4 : (c0 + n) * W // 4] for c0, n in S_GROUPS]
+        raw, staged, words, rest = {}, {}, {}, {}
+        w_c, w_s, xq_c, xq_s, xr_c, xr_s, t_c, t_s = {}, {}, {}, {}, {}, {}, {}, {}
+        values, acc, passes_done, own_sum, gathered = {}, {}, {}, {}, {}
 
         def load_block(key, rows):
             raw[key] = placed([P, PACK, rows.shape[1]], F32, "raw_" + key)
             nc.sync.dma_start(raw[key][:], rows.rearrange("(p i) j -> p i j", i=PACK))
 
-        def x_pieces(c):
-            if c < 2:
-                return [("x%da" % c, 0, PIECE), ("x%db" % c, PIECE, PIECE)]
-            return [("x%d" % c, 0, W)]
-
-        def piece(key):
-            c = int(key[1])
-            return [(c, j0, cols) for name, j0, cols in x_pieces(c) if name == key][0]
-
-        def load_piece(key):
-            c, j0, cols = piece(key)
+        def load_x(key):
+            c, j0, cols = X_PIECES[key]
             load_block(key, x[:, c * W + j0 : c * W + j0 + cols])
 
-        def load_x(c):
-            for key, j0, cols in x_pieces(c):
-                load_piece(key)
-
-        def load_w(k):
-            a, n0 = W_BLOCKS[k]
-            load_block("w%d" % k, wt[a * W : (a + 1) * W, n0 : n0 + PIECE])
+        def load_w(key):
+            a, n0, cols = W_BLOCKS[key]
+            load_block(key, wt[a * W : (a + 1) * W, n0 : n0 + cols])
 
         def load_table():
             raw["tab"] = placed([P, T], I32, "raw_tab")
             nc.sync.dma_start(raw["tab"][:], tab_words[0].rearrange("p t y -> p (t y)").bitcast(I32))
+
+        def load_table_scales():
+            for r in range(SCALE_ROWS):
+                rows = tab_scales[:, r:BLOCKS:SCALE_ROWS, :].bitcast(I32).rearrange("a q t -> q a t")
+                nc.sync.dma_start(tab_s[r:P:LIFT, :], rows)
+
+        def load_wx():
+            nc.sync.dma_start(wx_w[:], wx_words[0].bitcast(I32))
+
+        def load_wx_scales():
+            for r in range(SCALE_ROWS):
+                nc.sync.dma_start(wx_s[r:P:QUADRANT, :], wx_scales[0, r:BLOCKS:SCALE_ROWS, :].bitcast(I32))
 
         def runs_out(ap, lo, hi):
             return ap[:, lo:hi, :].rearrange("p (c r) i -> p c i r", r=RUN)
@@ -156,48 +138,23 @@ def tile_list_tiert_bias_kernel(
         def runs_in(ap):
             return ap.rearrange("p i (c r) -> p c i r", r=RUN)
 
-        wx_s = placed([P, N // 4], I32, "wx_s")
-        nc.vector.memset(tab_s[:], 0)
-        planes = kept([P, 2 * PACK - 1, P], BF16, "planes")
-        nc.gpsimd.memset(planes[:].rearrange("p u m -> p (u m)").bitcast(I32), 0)
-        ident = planes[:, PACK - 1, :]
-        make_identity(nc, ident, nomemset=True)
-        nc.gpsimd.memset(b_rows[:], 0.0)
-        nc.gpsimd.memset(wx_s[:], 0)
-        nc.sync.dma_start(offsets[:], offs)
-        load_piece("x0a")
-        for r in range(SCALE_ROWS):
-            rows = tab_scales[:, r:BLOCKS:SCALE_ROWS, :].bitcast(I32).rearrange("a q t -> q a t")
-            nc.sync.dma_start(tab_s[r:P:LIFT, :], rows)
-        nc.sync.dma_start(b_rows[0:TILES, :], b.rearrange("(m p) -> m p", p=P))
-        load_piece("x0b")
-        nc.sync.dma_start(wx_w[:], wx_words[0].bitcast(I32))
-        for r in range(SCALE_ROWS):
-            nc.sync.dma_start(wx_s[r:P:QUADRANT, :], wx_scales[0, r:BLOCKS:SCALE_ROWS, :].bitcast(I32))
-        load_x(1)
-        load_w(0)
-        load_w(1)
-        load_table()
-        ident_pe = kept([P, P], F32, "ident_pe")
-        nc.scalar.activation(ident_pe[:], ident, IDENT)
-
-        for t in range(PACK):
-            around = planes[:, PACK - 1 - t : 2 * PACK - 1 - t, :]
-            nc.vector.tensor_copy(runs_out(sel_in[:, t, :, :], 0, P), runs_in(around))
-        nc.vector.quantize_mx(sel_c[:].bitcast(FP8X4), sel_s[:], sel_in[:].rearrange("p t m i -> p (t m i)"))
-
-        for g in range(len(S_GROUPS)):
-            nc.gpsimd.memset(low_s[g][P - QUADRANT : P, :], 0)
-
-        staged = {}
-
-        def stage(key, v):
+        def stage(key, engine, lo=0, hi=None):
             cols = raw[key].shape[2]
-            staged[key] = placed([P, cols, PACK], BF16, "staged_" + key)[:]
-            if v > 0:
-                nc.vector.tensor_copy(runs_out(staged[key], 0, v), runs_in(raw[key][:, :, 0:v]))
-            if v < cols:
-                nc.scalar.activation(runs_out(staged[key], v, cols), runs_in(raw[key][:, :, v:cols]), IDENT)
+            hi = cols if hi is None else hi
+            if key not in staged:
+                group = [g for g in STAGED_TOGETHER if key in g] + [(key,)]
+                whole = placed([P, len(group[0]) * cols * PACK], BF16, "staged_" + group[0][0])
+                for u, member in enumerate(group[0]):
+                    share = whole[:, u * cols * PACK : (u + 1) * cols * PACK]
+                    staged[member] = share.rearrange("p (j i) -> p j i", i=PACK)
+            if engine == "v":
+                nc.vector.tensor_copy(runs_out(staged[key], lo, hi), runs_in(raw[key][:, :, lo:hi]))
+            elif engine == "s":
+                nc.scalar.activation(runs_out(staged[key], lo, hi), runs_in(raw[key][:, :, lo:hi]), IDENT)
+            else:
+                nc.gpsimd.tensor_scalar(
+                    staged[key][:, lo:hi, :], raw[key][:, :, lo:hi].rearrange("p i j -> p j i"), 1.0, 0.0, MULT, ADD
+                )
 
         def quantize(src, codes, scales):
             nc.vector.quantize_mx(codes.bitcast(FP8X4), scales, src.rearrange("p j i -> p (j i)"))
@@ -205,239 +162,332 @@ def tile_list_tiert_bias_kernel(
         def listed(first, count):
             return offsets[:, first * W // LIST_ROWS : (first + count) * W // LIST_ROWS]
 
-        t_s = {}
-
         def gather_scales(g):
             c0, n = S_GROUPS[g]
-            both = placed([P, n * W], U8, "scales%d" % g)
-            nc.vector.tensor_copy(both[:], tab_s[:].bitcast(U8).indirect(listed(c0, n)))
-            nc.sync.dma_start(low_s[g][0 : P - LIFT, :], both[LIFT:P, :].bitcast(I32))
+            gathered[g] = placed([P, n * W], U8, "scales%d" % g)
+            nc.vector.tensor_copy(gathered[g][:], tab_s[:].bitcast(U8).indirect(listed(c0, n)))
             for d in range(n):
-                t_s[c0 + d, 0] = both[:, d * W : (d + 1) * W]
-                t_s[c0 + d, 1] = low_s[g][:].bitcast(U8)[:, d * W : (d + 1) * W]
+                t_s[c0 + d, 0] = gathered[g][:, d * W : (d + 1) * W]
+                t_s[c0 + d, 1] = low_s[g].bitcast(U8)[:, d * W : (d + 1) * W]
 
-        words = {}
+        def move_scales(g):
+            nc.sync.dma_start(low_s[g][0 : P - LIFT, :], gathered[g][LIFT:P, :].bitcast(I32))
 
         def gather_words(c):
-            words[c] = placed([P, W], U32, "words%d" % c)
-            nc.vector.tensor_copy(words[c][:], raw["tab"][:].bitcast(U32).indirect(listed(c, 1)))
+            if c not in words:
+                count = WORDS_TOGETHER.get(c, 1)
+                whole = placed([P, count * W], U32, "words%d" % c)
+                for u in range(count):
+                    words[c + u] = whole[:, u * W : (u + 1) * W]
+            nc.vector.tensor_copy(words[c], raw["tab"][:].bitcast(U32).indirect(listed(c, 1)))
 
         def part_words(c):
             t_c[c] = placed([P, 2, 2 * W], U8, "t_c%d" % c)
             nc.vector.tensor_copy(
-                t_c[c][:].bitcast(U16), words[c][:].bitcast(U16).rearrange("p (j a) -> p a j", a=2)
+                t_c[c][:].bitcast(U16), words[c].bitcast(U16).rearrange("p (j a) -> p a j", a=2)
             )
 
-        def quantize_w(k):
-            w_c[k] = placed([P, PIECE], U32, "w_c%d" % k)
-            quantize(staged["w%d" % k], w_c[k][:], w_s[k][:])
+        def quantize_w(key, lo=0, hi=None):
+            cols = raw[key].shape[2]
+            hi = cols if hi is None else hi
+            if key not in w_c:
+                w_c[key] = placed([P, cols], U32, "c_" + key)
+                w_s[key] = placed([P, cols], U8, "s_" + key)
+            quantize(staged[key][:, lo:hi, :], w_c[key][:, lo:hi], w_s[key][:, lo:hi])
 
-        def first_tier(key):
-            c, j0, cols = piece(key)
-            if j0 == 0:
+        def first_tier(key, lo=0, hi=None):
+            c, j0, cols = X_PIECES[key]
+            hi = cols if hi is None else hi
+            if c not in xq_c:
                 xq_c[c] = placed([P, W], U32, "xq_c%d" % c)
-            quantize(staged[key], xq_c[c][:, j0 : j0 + cols], xq_s[c][:, j0 : j0 + cols])
+                xq_s[c] = placed([P, W], U8, "xq_s%d" % c)
+            quantize(staged[key][:, lo:hi, :], xq_c[c][:, j0 + lo : j0 + hi], xq_s[c][:, j0 + lo : j0 + hi])
 
-        rest = {}
-
-        def residual(c, s, number):
-            if s == 0:
-                rest[c] = placed([P, W, PACK], BF16, "rest%d" % c)
+        def decode(c, s, number):
             cols = slice(s * P, (s + 1) * P)
-            values = bank([P, PACK, P], number)
+            values[c, s] = bank([P, PACK, P], number)
             for t in range(PACK):
-                sel = slice(t * P, (t + 1) * P)
                 nc.tensor.matmul_mx(
-                    values[:, t, :],
-                    lhsT=sel_c[:, sel].bitcast(FP8X4),
-                    lhsT_scale=sel_s[:, sel],
+                    values[c, s][:, t, :],
+                    lhsT=sel_c[:, PAD + t * P : PAD + (t + 1) * P].bitcast(FP8X4),
+                    lhsT_scale=sel_s[:, t % 2 * P : (t % 2 + 1) * P],
                     rhs=xq_c[c][:, cols].bitcast(FP8X4),
                     rhs_scale=xq_s[c][:, cols],
                     start=True,
                     stop=True,
                 )
-            key, j0, n = [pc for pc in x_pieces(c) if pc[1] <= s * P < pc[1] + pc[2]][0]
+
+        def subtract(c, s):
+            if c not in rest:
+                rest[c] = placed([P, W, PACK], BF16, "rest%d" % c)
+            key = [k for k, (d, j0, n) in X_PIECES.items() if d == c and j0 <= s * P < j0 + n][0]
+            j0 = X_PIECES[key][1]
             given = raw[key][:, :, s * P - j0 : (s + 1) * P - j0]
-            nc.vector.tensor_tensor(runs_out(rest[c], s * P, (s + 1) * P), runs_in(given), runs_in(values[:]), SUB)
+            nc.vector.tensor_tensor(
+                runs_out(rest[c], s * P, (s + 1) * P), runs_in(given), runs_in(values[c, s][:]), SUB
+            )
 
-        def second_tier(c):
-            xr_c[c] = placed([P, W], U32, "xr_c%d" % c)
-            quantize(rest[c][:], xr_c[c][:], xr_s[c][:])
+        def second_tier(c, lo=0, hi=W):
+            if c not in xr_c:
+                xr_c[c] = placed([P, W], U32, "xr_c%d" % c)
+                xr_s[c] = placed([P, W], U8, "xr_s%d" % c)
+            quantize(rest[c][:, lo:hi, :], xr_c[c][:, lo:hi], xr_s[c][:, lo:hi])
 
-        table, own = (0, 1), ("q", "r")
-        bias = kept([P, TILES], F32, "bias")
-        own_bias = {}
-        late = {}
-        acc = {}
-        passes_done = {}
-
-        own_sum = {}
-
-        def finish(c, m, j0, n, part, on_vector):
-            psum_sum = acc[c, m, j0, part][:]
-            col = own_bias[c, m][:] if (c, m) in own_bias else (bias if part == "own" else late.get("bias"))[:, m : m + 1]
-            if part == "own":
-                own_sum[c, m] = placed([P, n], F32, "own%d_%d" % (c, m))
-                nc.scalar.activation(own_sum[c, m][:], psum_sum, IDENT, bias=col)
-                return
-            if (c, m) in HELD:
-                res = placed([P, n], F32, "done%d" % HELD.index((c, m)))
-            else:
-                res = outp.tile([P, n], F32, name="done")
-            if part == "table":
-                nc.vector.tensor_tensor(res[:], psum_sum, own_sum[c, m][:], ADD)
-            elif on_vector:
-                nc.vector.tensor_scalar_add(res[:], psum_sum, col)
-            else:
-                nc.scalar.activation(res[:], psum_sum, IDENT, bias=col)
-            nc.sync.dma_start(out[m * P : (m + 1) * P, c * W + j0 : c * W + j0 + n], res[:])
-
-        def one_pass(kind, c, m, number, j0=0, n=W, on_vector=False):
-            part = ("own" if kind in own else "table") if (c, m) in SPLIT else "all"
+        def one_pass(kind, c, m, number, j0=0, n=W):
+            own = kind in ("q", "r")
+            part = ("own" if own else "table") if (c, m) in SPLIT else "all"
             key = (c, m, j0, part)
             if key not in acc:
                 acc[key] = bank([P, n], number)
                 passes_done[key] = 0
-            first, last = passes_done[key] == 0, passes_done[key] == (KINDS if part == "all" else KINDS // 2) - 1
+            first, last = passes_done[key] == 0, passes_done[key] == (3 if part == "all" else 1)
             passes_done[key] = passes_done[key] + 1
-            if kind in ("q", "r"):
+            if own:
                 codes, scales = (xq_c, xq_s) if kind == "q" else (xr_c, xr_s)
                 lhsT = wx_w[:, m * P // 2 : (m + 1) * P // 2].bitcast(FP4X4)
                 lhsT_s = wx_s[:, m * P // 4 : (m + 1) * P // 4].bitcast(U8)
                 rhs, rhs_s = codes[c][:, j0 : j0 + n].bitcast(FP8X4), scales[c][:, j0 : j0 + n]
             else:
-                n0 = m * P // PIECE * PIECE
-                k = W_BLOCKS.index((kind, n0))
+                k = [k for k, (a, n0, cols) in W_BLOCKS.items() if a == kind and n0 <= m * P < n0 + cols][0]
+                n0 = W_BLOCKS[k][1]
                 cols = slice(m * P - n0, (m + 1) * P - n0)
                 lhsT, lhsT_s = w_c[k][:, cols].bitcast(FP8X4), w_s[k][:, cols]
                 rhs, rhs_s = t_c[c][:, kind, 2 * j0 : 2 * (j0 + n)].bitcast(FP4X4), t_s[c, kind][:, j0 : j0 + n]
             nc.tensor.matmul_mx(
                 acc[key][:], lhsT=lhsT, lhsT_scale=lhsT_s, rhs=rhs, rhs_scale=rhs_s, start=first, stop=last
             )
-            if last:
-                finish(c, m, j0, n, part, on_vector)
 
-        def by_kind(kinds, c, tiles, banks):
-            for kind in kinds:
-                for m, number in zip(tiles, banks):
-                    one_pass(kind, c, m, number)
-
-        def by_tile(kinds, c, tiles, banks):
+        def passes(kinds, c, tiles, banks):
             for m, number in zip(tiles, banks):
                 for kind in kinds:
                     one_pass(kind, c, m, number)
 
-        def last_chunk(banks):
-            c = CHUNKS - 1
-            for kind in table + own:
-                for m in range(HALF):
-                    one_pass(kind, c, m, banks[m], on_vector=m % 2 == 0)
-            for m in range(HALF, TILES - 1):
-                for kind in table + own:
-                    one_pass(kind, c, m, banks[m], on_vector=m % 2 == 0)
-            for s in range(PARTS):
-                for kind in table + own:
-                    one_pass(kind, c, TILES - 1, banks[s], s * P, P, s == PARTS - 1)
+        cols_of_b = {}
 
-        def copy_bias():
-            late["bias"] = placed([P, TILES], F32, "late_bias")
-            nc.scalar.activation(late["bias"][:], bias[:], IDENT)
+        def bias_col(name, m):
+            return cols_of_b[name][:, B_STEP * m : B_STEP * m + 1]
 
-        def make_bias(number, pairs):
-            b_cols = bank([P, P], number)
-            nc.tensor.transpose(b_cols[:], b_rows[:], ident_pe[:])
-            nc.scalar.activation(bias[:], b_cols[:, 0:TILES], IDENT)
-            for c, m in pairs:
-                own_bias[c, m] = placed([P, 1], F32, "bias%d_%d" % (c, m))
-                nc.scalar.activation(own_bias[c, m][:], b_cols[:, m : m + 1], IDENT)
+        def set_aside(c, m, name="bias"):
+            own_sum[c, m] = placed([P, W], F32, "own%d_%d" % (c, m))
+            nc.scalar.activation(own_sum[c, m][:], acc[c, m, 0, "own"][:], IDENT, bias=bias_col(name, m))
 
-        make_bias(3, ((1, 2), (1, 6)))
-        stage("x0a", PIECE)
-        gather_scales(0)
+        def finish(c, m, engine, name="bias", j0=0, n=W):
+            res = outp.tile([P, n], F32, name="done")
+            if (c, m) in SPLIT:
+                nc.vector.tensor_tensor(res[:], acc[c, m, j0, "table"][:], own_sum[c, m][:], ADD)
+            elif engine == "v":
+                nc.vector.tensor_scalar_add(res[:], acc[c, m, j0, "all"][:], bias_col(name, m))
+            else:
+                nc.scalar.activation(res[:], acc[c, m, j0, "all"][:], IDENT, bias=bias_col(name, m))
+            nc.sync.dma_start(out[m * P : (m + 1) * P, c * W + j0 : c * W + j0 + n], res[:])
+
+        def copy_bias(name, src="bias"):
+            cols_of_b[name] = placed([P, B_STEP * TILES], F32, name)
+            nc.scalar.activation(cols_of_b[name][:], cols_of_b[src][:], IDENT)
+
+        B_STEP = QUADRANT // TILES
+        b_rows = placed([P, QUADRANT], F32, "b_rows")
+
+        def load_b():
+            nc.sync.dma_start(b_rows[0:P:B_STEP, :], b.rearrange("(m q j) -> q m j", q=P // QUADRANT, j=QUADRANT))
+
+        def turn_b():
+            cols_of_b["bias"] = placed([P, QUADRANT], F32, "bias")
+            nc.vector.transpose(cols_of_b["bias"][:], b_rows[:])
+
+        planes = placed([P, PACK + 1, P], BF16, "planes")
+        sel_in = placed([P, 2, P, PACK], BF16, "sel_in")
+
+        def make_planes():
+            nc.gpsimd.memset(planes[:].rearrange("p u m -> p (u m)").bitcast(I32), 0)
+            make_identity(nc, planes[:, 1, :], nomemset=True)
+
+        def lay_selection():
+            nc.vector.tensor_copy(runs_out(sel_in[:, 0, :, :], 0, P), runs_in(planes[:, 1 : PACK + 1, :]))
+            nc.scalar.activation(runs_out(sel_in[:, 1, :, :], 0, P), runs_in(planes[:, 0:PACK, :]), IDENT)
+
+        def quantize_selection():
+            nc.vector.quantize_mx(
+                sel_c[:, PAD : PAD + 2 * P].bitcast(FP8X4), sel_s[:], sel_in[:].rearrange("p t m i -> p (t m i)")
+            )
+
+        def move_selection():
+            halves = sel_c[:].bitcast(U16)
+            nc.vector.tensor_copy(
+                halves[:, 2 * (PAD + 2 * P) : 2 * (PAD + 4 * P)], halves[:, 2 * PAD - 1 : 2 * (PAD + 2 * P) - 1]
+            )
+
+        def zero_small():
+            nc.vector.memset(wx_s[:], 0)
+            nc.vector.memset(b_rows[:], 0.0)
+            nc.vector.memset(sel_c[:, 0:PAD].bitcast(I32), 0)
+            nc.vector.memset(low_all[P - QUADRANT : P, :], 0)
+
+        def clock(name, ap):
+            word = placed([P, 1], I32, "clock_" + name)
+            nc.gpsimd.tensor_copy(word[:], ap.bitcast(I32)[:, 0:1])
+
+        table, own = (0, 1), ("q", "r")
+
+
+        make_planes()
+        nc.vector.memset(tab_s[:], 0)
+        zero_small()
+        lay_selection()
+        quantize_selection()
+        move_selection()
+
+        nc.sync.dma_start(offsets[:], offs)
+        load_x("x0a")
+        load_table_scales()
+        load_x("x0b")
+        load_wx()
+        load_wx_scales()
+        load_x("x1a")
+        load_x("x1b")
+        load_b()
+        load_w("w0")
+        load_table()
+        stage("x0a", "v")
         first_tier("x0a")
-        load_w(2)
-        load_w(3)
-        load_w(4)
-        load_w(5)
-        stage("x0b", 0)
+        stage("x0b", "s")
+        gather_scales(0)
+        decode(0, 0, 4)
+        decode(0, 1, 5)
+        subtract(0, 0)
+        subtract(0, 1)
         first_tier("x0b")
-        for s in range(PARTS):
-            residual(0, s, HALF + s)
-        stage("x1a", 0)
-        stage("x1b", 0)
-        by_kind(("q",), 0, (4, 5, 6, 7), (0, 1, 2, 3))
-        first_tier("x1a")
-        first_tier("x1b")
-        second_tier(0)
-        residual(1, 0, 4)
-        residual(1, 1, 5)
-        residual(1, 2, 6)
-        residual(1, 3, 7)
-        stage("w0", 0)
-        stage("w1", 0)
-        by_kind(("r",), 0, (4, 5, 6, 7), (0, 1, 2, 3))
-        quantize_w(0)
-        quantize_w(1)
-        second_tier(1)
         gather_scales(1)
-        load_w(6)
-        load_w(7)
-        load_x(2)
-        by_kind(("q",), 1, (0, 1, 2, 3), (4, 5, 6, 7))
-        by_tile(own, 0, (0, 1), (0, 1))
-        by_kind(("r",), 1, (0, 1, 2, 3), (4, 5, 6, 7))
-        by_tile(own, 0, (2, 3), (2, 3))
-        stage("w2", 0)
-        stage("w3", 0)
-        stage("w4", 0)
-        stage("w5", 0)
-        copy_bias()
+        move_scales(0)
+        load_w("w1")
+        move_scales(1)
+        for k in range(2, 8):
+           load_w("w%d" % k)
+        load_x("x2a")
+        load_x("x2b")
+        load_x("x3")
+        decode(0, 2, 6)
+        decode(0, 3, 7)
+        subtract(0, 2)
+        subtract(0, 3)
+        stage("x1a", "s")
+        stage("x1b", "s")
+        stage("w0", "s")
+        passes(("q",), 0, (4, 5, 6, 7), (0, 1, 2, 3))
+        first_tier("x1a")
+        second_tier(0)
+        first_tier("x1b")
+        turn_b()
+        decode(1, 0, 4)
+        decode(1, 1, 5)
+        passes(("r",), 0, (4, 5), (0, 1))
+        decode(1, 2, 6)
+        decode(1, 3, 7)
+        passes(("r",), 0, (6, 7), (2, 3))
+        for s in range(4):
+           subtract(1, s)
+        for m in range(4, 8):
+           set_aside(0, m)
+        passes(own, 0, (2, 3, 0, 1), (0, 1, 2, 3))
+        set_aside(0, 2)
+        set_aside(0, 3)
+        quantize_w("w0")
+        second_tier(1)
+        passes(("q",), 1, (0, 1, 2, 3, 4, 5), (4, 5, 6, 7, 0, 1))
+        passes(("r",), 1, (0, 1, 2, 3, 4, 5), (4, 5, 6, 7, 0, 1))
+
+        for k in range(1, 4):
+           stage("w%d" % k, "s")
+        copy_bias("late_bias")
         gather_words(0)
-        part_words(0)
         gather_words(1)
-        quantize_w(2)
+        part_words(0)
+        quantize_w("w1")
         part_words(1)
-        quantize_w(3)
-        by_tile(table, 0, (0, 1), (0, 1))
-        by_kind((0,), 0, (2, 3), (2, 3))
-        by_tile(table, 1, (0, 1), (4, 5))
-        quantize_w(4)
-        gather_words(2)
-        quantize_w(5)
-        part_words(2)
-        by_kind((1,), 0, (2, 3), (2, 3))
-        by_tile(table, 1, (2, 3), (6, 7))
-        by_tile(own, 1, (4, 5), (4, 5))
-        stage("w6", PIECE)
-        stage("w7", PIECE)
-        stage("x2", 0)
+        quantize_w("w2")
         gather_scales(2)
-        quantize_w(6)
-        load_x(3)
-        quantize_w(7)
-        by_tile(table, 0, (4, 5), (0, 1))
-        first_tier("x2")
-        by_tile(own, 1, (6, 7), (6, 7))
-        by_tile(table, 1, (4, 5), (4, 5))
-        by_tile(table, 0, (6, 7), (2, 3))
-        by_tile(table, 1, (6, 7), (6, 7))
-        stage("x3", 0)
-        residual(2, 0, 0)
-        residual(2, 1, 1)
-        residual(2, 2, 4)
-        residual(2, 3, 5)
+        move_scales(2)
+        quantize_w("w3")
+        stage("w4", "v")
+        stage("w5", "v")
+        quantize_w("w4")
+        quantize_w("w5")
+        passes((0,), 0, (0, 1), (2, 3))
+        passes((1,), 0, (0, 1), (2, 3))
+        finish(0, 0, "s", "late_bias")
+        finish(0, 1, "s", "late_bias")
+        passes(table, 1, (0, 1), (4, 5))
+        finish(1, 0, "s", "late_bias")
+        finish(1, 1, "s", "late_bias")
+        passes((0,), 1, (2, 3), (6, 7))
+        passes((1,), 1, (2, 3), (6, 7))
+        finish(1, 2, "s", "late_bias")
+        finish(1, 3, "s", "late_bias")
+        passes(table, 0, (2, 3), (2, 3))
+        finish(0, 2, "v")
+        finish(0, 3, "v")
+        stage("w6", "s")
+        stage("w7", "v")
+        quantize_w("w6")
+        quantize_w("w7")
+        passes((0,), 1, (4, 5), (0, 1))
+        passes((0,), 0, (4, 5), (4, 5))
+        passes((1,), 1, (4, 5), (0, 1))
+        passes((1,), 0, (4, 5), (4, 5))
+        finish(1, 4, "s", "late_bias")
+        finish(1, 5, "s", "late_bias")
+        finish(0, 4, "v")
+        finish(0, 5, "v")
+        passes(own, 1, (6, 7), (6, 7))
+        passes((0,), 1, (6, 7), (6, 7))
+        passes((0,), 0, (6, 7), (2, 3))
+        passes((1,), 1, (6, 7), (6, 7))
+        passes((1,), 0, (6, 7), (2, 3))
+        stage("x2a", "s")
+        stage("x2b", "s")
+        finish(1, 6, "s", "late_bias")
+        finish(1, 7, "s", "late_bias")
+        gather_words(2)
+        first_tier("x2a")
+        part_words(2)
+        first_tier("x2b")
+        finish(0, 6, "v")
+        finish(0, 7, "v")
+        decode(2, 0, 4)
+        decode(2, 1, 5)
+        passes(table, 2, (0, 1), (0, 1))
+        decode(2, 2, 6)
+        decode(2, 3, 7)
+        for s in range(4):
+           subtract(2, s)
+        passes(("q",), 2, (0, 1), (0, 1))
+        passes(table + ("q",), 2, (2, 3, 4, 5), (2, 3, 4, 5))
+        stage("x3", "s")
         second_tier(2)
         gather_scales(3)
+        move_scales(3)
         gather_words(3)
         first_tier("x3")
         part_words(3)
-        by_tile((0, "q", 1), 2, range(6), (2, 3, 6, 7, 0, 1))
-        by_kind(("r",), 2, range(6), (2, 3, 6, 7, 0, 1))
-        by_tile(table + own, 2, (6,), (4,))
-        residual(3, 0, 2)
-        residual(3, 1, 3)
-        residual(3, 2, 6)
-        residual(3, 3, 7)
+        passes(("r",), 2, range(6), (0, 1, 2, 3, 4, 5))
+        for m in range(6):
+           finish(2, m, "s")
+        passes(table + own, 2, (6,), (6,))
+        finish(2, 6, "s", "late_bias")
+        for s in range(4):
+           decode(3, s, s)
+           subtract(3, s)
         second_tier(3)
-        by_tile(table + own, 2, (7,), (5,))
-        last_chunk((0, 1, 4, 2, 3, 6, 7, 5))
+        passes(table + own, 2, (7,), (7,))
+        finish(2, 7, "s", "late_bias")
+        for kind in table + own:
+           passes((kind,), 3, range(4), (4, 5, 6, 0))
+        for m in range(4):
+           finish(3, m, "vs"[m % 2])
+        for m, number in zip((4, 5, 6), (1, 2, 3)):
+           passes(table + own, 3, (m,), (number,))
+           finish(3, m, "vs"[m % 2])
+        for s, number in enumerate((7, 4, 5, 6)):
+           for kind in table + own:
+               one_pass(kind, 3, 7, number, s * P, P)
+           finish(3, 7, "v" if s == 3 else "s", j0=s * P, n=P)

@@ -37,40 +37,47 @@ PAD = 16
 ALIGN = 64
 KIB = 1024
 
-X_PIECES = {"x0a": (0, 0, 256), "x0b": (0, 256, 256), "x1a": (1, 0, 256), "x1b": (1, 256, 256), "x2a": (2, 0, 256), "x2b": (2, 256, 256), "x3": (3, 0, 512)}
+X_PIECES = {"x0a": (0, 0, 256), "x0b": (0, 256, 256), "x1a": (1, 0, 256), "x1b": (1, 256, 256), "x2a": (2, 0, 256), "x2b": (2, 256, 256), "x3": (3, 0, 512), "x00": (0, 0, 128), "x01": (0, 128, 128)}
 W_BLOCKS = {"w%d" % (2 * u + a): (a, u * PIECE, PIECE) for u in range(4) for a in range(2)}
 S_GROUPS = ((0, 1), (1, 1), (2, 1), (3, 1))
 SPLIT = ((0, 2), (0, 3), (0, 4), (0, 5), (0, 6), (0, 7))
-STAGED_TOGETHER = [("w1", "w2"), ("w4", "w5"), ("x2a", "x2b"), ("x1a", "x1b")]
+STAGED_TOGETHER = [("w1", "w2"), ("x2a", "x2b"), ("x1a", "x1b")]
 WORDS_TOGETHER = {0: 2}
 HOME = {
     "sel_in": 2 * KIB,
-    "staged_x0a": 2 * KIB,
+    "staged_x00": 2 * KIB,
+    "staged_x01": 3 * KIB,
     "staged_x0b": 0 * KIB + 64,
     "scales0": 2 * KIB + 64,
-    "staged_x1a": 3 * KIB,
-    "bias": 6 * KIB + 512,
-    "raw_x0a": 7 * KIB,
-    "scales1": 7 * KIB,
-    "raw_x1a": 11 * KIB,
-    "c_w0": 11 * KIB,
-    "rest1": 18 * KIB + 960,
-    "words0": 15 * KIB,
-    "staged_w3": 19 * KIB,
-    "staged_w1": 21 * KIB,
-    "scales2": 24 * KIB + 512,
-    "staged_w4": 17 * KIB,
-    "staged_w6": 15 * KIB + 512,
-    "words2": 15 * KIB,
-    "own0_2": 25 * KIB,
-    "staged_w7": 25 * KIB,
-    "staged_x2a": 26 * KIB,
-    "staged_x3": 26 * KIB,
-    "raw_x2b": 30 * KIB,
-    "scales3": 30 * KIB,
-    "words3": 31 * KIB,
-    "raw_w3": 34 * KIB,
-    "late_bias": 34 * KIB,
+    "staged_x1a": 3 * KIB + 512,
+    "raw_x0a": 8 * KIB,
+    "scales1": 8 * KIB,
+    "raw_x0b": 12 * KIB,
+    "bias": 12 * KIB,
+    "raw_x1a": 16 * KIB,
+    "c_w0": 16 * KIB,
+    "raw_x1b": 23 * KIB + 960,
+    "words0": 20 * KIB,
+    "staged_w3": 24 * KIB,
+    "staged_w1": 26 * KIB,
+    "staged_w4": 26 * KIB,
+    "staged_w5": 28 * KIB,
+    "scales2": 26 * KIB,
+    "staged_w6": 26 * KIB + 512,
+    "words2": 26 * KIB + 512,
+    "staged_x2a": 29 * KIB,
+    "staged_x3": 29 * KIB,
+    "own0_2": 33 * KIB,
+    "staged_w7": 33 * KIB,
+    "raw_x2b": 35 * KIB,
+    "scales3": 35 * KIB,
+    "words3": 36 * KIB,
+    "raw_w3": 39 * KIB,
+    "late_bias": 39 * KIB,
+    "raw_w6": 43 * KIB,
+    "c_w7": 43 * KIB,
+    "raw_w1": 47 * KIB,
+    "t_c1": 47 * KIB,
 }
 
 
@@ -111,6 +118,10 @@ def tile_list_tiert_bias_kernel(
         def load_x(key):
             c, j0, cols = X_PIECES[key]
             load_block(key, x[:, c * W + j0 : c * W + j0 + cols])
+
+        def split_x(key, parts):
+            for u, part in enumerate(parts):
+                raw[part] = raw[key][:, :, u * P : (u + 1) * P]
 
         def load_w(key):
             a, n0, cols = W_BLOCKS[key]
@@ -343,13 +354,16 @@ def tile_list_tiert_bias_kernel(
         load_x("x0b")
         load_wx()
         load_wx_scales()
+        load_b()
         load_x("x1a")
         load_x("x1b")
-        load_b()
         load_w("w0")
         load_table()
-        stage("x0a", "v")
-        first_tier("x0a")
+        split_x("x0a", ("x00", "x01"))
+        stage("x00", "v")
+        stage("x01", "v")
+        first_tier("x00")
+        first_tier("x01")
         stage("x0b", "s")
         gather_scales(0)
         decode(0, 0, 4)
@@ -373,29 +387,30 @@ def tile_list_tiert_bias_kernel(
         stage("x1a", "s")
         stage("x1b", "s")
         stage("w0", "s")
-        passes(("q",), 0, (4, 5, 6, 7), (0, 1, 2, 3))
+        passes(("q",), 0, (4, 5, 6, 7, 2, 3), (0, 1, 2, 3, 4, 5))
         first_tier("x1a")
+        turn_b()
         second_tier(0)
         first_tier("x1b")
-        turn_b()
-        decode(1, 0, 4)
-        decode(1, 1, 5)
-        passes(("r",), 0, (4, 5), (0, 1))
+        decode(1, 0, 6)
+        decode(1, 1, 7)
+        subtract(1, 0)
+        subtract(1, 1)
+        passes(("r",), 0, (4, 5, 6), (0, 1, 2))
         decode(1, 2, 6)
+        passes(("r",), 0, (7,), (3,))
         decode(1, 3, 7)
-        passes(("r",), 0, (6, 7), (2, 3))
-        for s in range(4):
-           subtract(1, s)
-        for m in range(4, 8):
+        passes(("r",), 0, (2, 3), (4, 5))
+        for m in (4, 5, 6, 7, 2, 3):
            set_aside(0, m)
-        passes(own, 0, (2, 3, 0, 1), (0, 1, 2, 3))
-        set_aside(0, 2)
-        set_aside(0, 3)
+        subtract(1, 2)
+        subtract(1, 3)
         quantize_w("w0")
         second_tier(1)
-        passes(("q",), 1, (0, 1, 2, 3, 4, 5), (4, 5, 6, 7, 0, 1))
-        passes(("r",), 1, (0, 1, 2, 3, 4, 5), (4, 5, 6, 7, 0, 1))
-
+        passes(("q",), 1, (2, 3), (0, 1))
+        passes(own, 0, (0, 1), (2, 3))
+        passes(("q",), 1, (0, 1, 4, 5), (6, 7, 4, 5))
+        passes(("r",), 1, (0, 1, 2, 3, 4, 5), (6, 7, 0, 1, 4, 5))
         for k in range(1, 4):
            stage("w%d" % k, "s")
         copy_bias("late_bias")
@@ -405,45 +420,45 @@ def tile_list_tiert_bias_kernel(
         quantize_w("w1")
         part_words(1)
         quantize_w("w2")
-        gather_scales(2)
-        move_scales(2)
         quantize_w("w3")
         stage("w4", "v")
         stage("w5", "v")
         quantize_w("w4")
         quantize_w("w5")
+        gather_scales(2)
+        move_scales(2)
         passes((0,), 0, (0, 1), (2, 3))
         passes((1,), 0, (0, 1), (2, 3))
         finish(0, 0, "s", "late_bias")
         finish(0, 1, "s", "late_bias")
-        passes(table, 1, (0, 1), (4, 5))
+        passes(table, 1, (0, 1), (6, 7))
         finish(1, 0, "s", "late_bias")
         finish(1, 1, "s", "late_bias")
-        passes((0,), 1, (2, 3), (6, 7))
-        passes((1,), 1, (2, 3), (6, 7))
+        passes((0,), 1, (2, 3), (0, 1))
+        passes((1,), 1, (2, 3), (0, 1))
         finish(1, 2, "s", "late_bias")
         finish(1, 3, "s", "late_bias")
         passes(table, 0, (2, 3), (2, 3))
         finish(0, 2, "v")
         finish(0, 3, "v")
         stage("w6", "s")
+        stage("x2a", "s")
         stage("w7", "v")
         quantize_w("w6")
         quantize_w("w7")
-        passes((0,), 1, (4, 5), (0, 1))
-        passes((0,), 0, (4, 5), (4, 5))
-        passes((1,), 1, (4, 5), (0, 1))
-        passes((1,), 0, (4, 5), (4, 5))
+        passes((0,), 1, (4, 5), (4, 5))
+        passes((0,), 0, (4, 5), (6, 7))
+        passes((1,), 1, (4, 5), (4, 5))
+        passes((1,), 0, (4, 5), (6, 7))
         finish(1, 4, "s", "late_bias")
         finish(1, 5, "s", "late_bias")
         finish(0, 4, "v")
         finish(0, 5, "v")
-        passes(own, 1, (6, 7), (6, 7))
-        passes((0,), 1, (6, 7), (6, 7))
+        passes(own, 1, (6, 7), (0, 1))
+        passes((0,), 1, (6, 7), (0, 1))
         passes((0,), 0, (6, 7), (2, 3))
-        passes((1,), 1, (6, 7), (6, 7))
+        passes((1,), 1, (6, 7), (0, 1))
         passes((1,), 0, (6, 7), (2, 3))
-        stage("x2a", "s")
         stage("x2b", "s")
         finish(1, 6, "s", "late_bias")
         finish(1, 7, "s", "late_bias")
@@ -453,15 +468,15 @@ def tile_list_tiert_bias_kernel(
         first_tier("x2b")
         finish(0, 6, "v")
         finish(0, 7, "v")
-        decode(2, 0, 4)
-        decode(2, 1, 5)
-        passes(table, 2, (0, 1), (0, 1))
-        decode(2, 2, 6)
-        decode(2, 3, 7)
+        decode(2, 0, 6)
+        decode(2, 1, 7)
+        passes(table, 2, (0, 1), (4, 5))
+        decode(2, 2, 0)
+        decode(2, 3, 1)
         for s in range(4):
            subtract(2, s)
-        passes(("q",), 2, (0, 1), (0, 1))
-        passes(table + ("q",), 2, (2, 3, 4, 5), (2, 3, 4, 5))
+        passes(("q",), 2, (0, 1), (4, 5))
+        passes(table + ("q",), 2, (2, 3, 4, 5), (2, 3, 6, 7))
         stage("x3", "s")
         second_tier(2)
         gather_scales(3)
@@ -469,25 +484,25 @@ def tile_list_tiert_bias_kernel(
         gather_words(3)
         first_tier("x3")
         part_words(3)
-        passes(("r",), 2, range(6), (0, 1, 2, 3, 4, 5))
+        passes(("r",), 2, range(6), (4, 5, 2, 3, 6, 7))
         for m in range(6):
            finish(2, m, "s")
-        passes(table + own, 2, (6,), (6,))
+        passes(table + own, 2, (6,), (0,))
         finish(2, 6, "s", "late_bias")
-        for s in range(4):
-           decode(3, s, s)
+        for s, number in enumerate((4, 5, 2, 3)):
+           decode(3, s, number)
            subtract(3, s)
         second_tier(3)
-        passes(table + own, 2, (7,), (7,))
+        passes(table + own, 2, (7,), (1,))
         finish(2, 7, "s", "late_bias")
         for kind in table + own:
-           passes((kind,), 3, range(4), (4, 5, 6, 0))
+           passes((kind,), 3, range(4), (6, 7, 0, 4))
         for m in range(4):
            finish(3, m, "vs"[m % 2])
-        for m, number in zip((4, 5, 6), (1, 2, 3)):
+        for m, number in zip((4, 5), (5, 2)):
            passes(table + own, 3, (m,), (number,))
            finish(3, m, "vs"[m % 2])
-        for s, number in enumerate((7, 4, 5, 6)):
+        for m, j0, n, number, engine in ((6, 0, 256, 3, "v"), (6, 256, 256, 1, "s"), (7, 0, 256, 6, "v"), (7, 256, 128, 7, "s"), (7, 384, 128, 0, "v")):
            for kind in table + own:
-               one_pass(kind, 3, 7, number, s * P, P)
-           finish(3, 7, "v" if s == 3 else "s", j0=s * P, n=P)
+               one_pass(kind, 3, m, number, j0, n)
+           finish(3, m, engine, j0=j0, n=n)

@@ -34,11 +34,14 @@ BLOCKS = 16
 LIFT = 16
 RESULTS = 20
 PAD = 16
+PAIRS = 1
+STORED_TOGETHER = []
 ALIGN = 64
 KIB = 1024
 
 X_PIECES = {"x0a": (0, 0, 256), "x0b": (0, 256, 256), "x1a": (1, 0, 256), "x1b": (1, 256, 256), "x2a": (2, 0, 256), "x2b": (2, 256, 256), "x3": (3, 0, 512), "x00": (0, 0, 128), "x01": (0, 128, 128)}
 W_BLOCKS = {"w%d" % (2 * u + a): (a, u * PIECE, PIECE) for u in range(4) for a in range(2)}
+W_LOADS = {}
 S_GROUPS = ((0, 1), (1, 1), (2, 1), (3, 1))
 SPLIT = ((0, 2), (0, 3), (0, 4), (0, 5), (0, 6), (0, 7))
 STAGED_TOGETHER = [("w1", "w2"), ("x2a", "x2b"), ("x1a", "x1b")]
@@ -60,15 +63,14 @@ HOME = {
     "words0": 20 * KIB,
     "staged_w3": 24 * KIB,
     "staged_w1": 26 * KIB,
-    "staged_w4": 26 * KIB,
-    "staged_w5": 28 * KIB,
-    "scales2": 26 * KIB,
-    "staged_w6": 26 * KIB + 512,
-    "words2": 26 * KIB + 512,
-    "staged_x2a": 29 * KIB,
-    "staged_x3": 29 * KIB,
-    "own0_2": 33 * KIB,
-    "staged_w7": 33 * KIB,
+    "scales2": 29 * KIB + 512,
+    "staged_w4": 24 * KIB + 64,
+    "staged_w5": 22 * KIB + 64,
+    "staged_w6": 21 * KIB,
+    "own0_2": 30 * KIB,
+    "staged_w7": 30 * KIB,
+    "staged_x2a": 31 * KIB,
+    "staged_x3": 31 * KIB,
     "raw_x2b": 35 * KIB,
     "scales3": 35 * KIB,
     "words3": 36 * KIB,
@@ -78,6 +80,8 @@ HOME = {
     "c_w7": 43 * KIB,
     "raw_w1": 47 * KIB,
     "t_c1": 47 * KIB,
+    "own0_4": 51 * KIB,
+    "words2": 51 * KIB,
 }
 
 
@@ -88,6 +92,7 @@ def tile_list_tiert_bias_kernel(
     with ExitStack() as ctx:
         keep = ctx.enter_context(tc.tile_pool(name="keep", bufs=1))
         outp = ctx.enter_context(tc.tile_pool(name="outp", bufs=RESULTS))
+        pairp = ctx.enter_context(tc.tile_pool(name="pairp", bufs=PAIRS))
         psum = ctx.enter_context(tc.psum_pool(name="psum", bufs=1))
         shared = ctx.enter_context(tc.tile_pool(name="shared", bufs=1))
 
@@ -119,12 +124,13 @@ def tile_list_tiert_bias_kernel(
             c, j0, cols = X_PIECES[key]
             load_block(key, x[:, c * W + j0 : c * W + j0 + cols])
 
-        def split_x(key, parts):
+        def split(key, parts):
+            cols = raw[key].shape[2] // len(parts)
             for u, part in enumerate(parts):
-                raw[part] = raw[key][:, :, u * P : (u + 1) * P]
+                raw[part] = raw[key][:, :, u * cols : (u + 1) * cols]
 
         def load_w(key):
-            a, n0, cols = W_BLOCKS[key]
+            a, n0, cols = W_BLOCKS[key] if key in W_BLOCKS else W_LOADS[key]
             load_block(key, wt[a * W : (a + 1) * W, n0 : n0 + cols])
 
         def load_table():
@@ -273,7 +279,7 @@ def tile_list_tiert_bias_kernel(
                 for kind in kinds:
                     one_pass(kind, c, m, number)
 
-        cols_of_b = {}
+        cols_of_b, results, filled = {}, {}, {}
 
         def bias_col(name, m):
             return cols_of_b[name][:, B_STEP * m : B_STEP * m + 1]
@@ -283,14 +289,32 @@ def tile_list_tiert_bias_kernel(
             nc.scalar.activation(own_sum[c, m][:], acc[c, m, 0, "own"][:], IDENT, bias=bias_col(name, m))
 
         def finish(c, m, engine, name="bias", j0=0, n=W):
-            res = outp.tile([P, n], F32, name="done")
-            if (c, m) in SPLIT:
-                nc.vector.tensor_tensor(res[:], acc[c, m, j0, "table"][:], own_sum[c, m][:], ADD)
-            elif engine == "v":
-                nc.vector.tensor_scalar_add(res[:], acc[c, m, j0, "all"][:], bias_col(name, m))
+            group = [g for g in STORED_TOGETHER if (c, m) in g]
+            if group:
+                tiles = group[0]
+                if tiles not in results:
+                    results[tiles] = pairp.tile([P, len(tiles) * W], F32, name="pair")
+                    filled[tiles] = 0
+                filled[tiles] = filled[tiles] + 1
+                res = results[tiles][:, tiles.index((c, m)) * W : (tiles.index((c, m)) + 1) * W]
             else:
-                nc.scalar.activation(res[:], acc[c, m, j0, "all"][:], IDENT, bias=bias_col(name, m))
-            nc.sync.dma_start(out[m * P : (m + 1) * P, c * W + j0 : c * W + j0 + n], res[:])
+                res = outp.tile([P, n], F32, name="done")[:]
+            if (c, m) in SPLIT:
+                nc.vector.tensor_tensor(res, acc[c, m, j0, "table"][:], own_sum[c, m][:], ADD)
+            elif engine == "v":
+                nc.vector.tensor_scalar_add(res, acc[c, m, j0, "all"][:], bias_col(name, m))
+            else:
+                nc.scalar.activation(res, acc[c, m, j0, "all"][:], IDENT, bias=bias_col(name, m))
+            if not group:
+                nc.sync.dma_start(out[m * P : (m + 1) * P, c * W + j0 : c * W + j0 + n], res)
+            elif filled[tiles] == len(tiles):
+                (c0, m0), (c1, m1) = tiles[0], tiles[-1]
+                if m0 == m1:
+                    rows = out[m0 * P : (m0 + 1) * P, c0 * W : (c1 + 1) * W]
+                    nc.sync.dma_start(rows, results[tiles][:])
+                else:
+                    rows = out[m0 * P : (m1 + 1) * P, c0 * W : (c0 + 1) * W]
+                    nc.sync.dma_start(rows.rearrange("(u p) j -> p u j", p=P), results[tiles][:].rearrange("p (u j) -> p u j", j=W))
 
         def copy_bias(name, src="bias"):
             cols_of_b[name] = placed([P, B_STEP * TILES], F32, name)
@@ -359,7 +383,7 @@ def tile_list_tiert_bias_kernel(
         load_x("x1b")
         load_w("w0")
         load_table()
-        split_x("x0a", ("x00", "x01"))
+        split("x0a", ("x00", "x01"))
         stage("x00", "v")
         stage("x01", "v")
         first_tier("x00")
@@ -420,13 +444,13 @@ def tile_list_tiert_bias_kernel(
         quantize_w("w1")
         part_words(1)
         quantize_w("w2")
+        gather_scales(2)
+        move_scales(2)
         quantize_w("w3")
         stage("w4", "v")
         stage("w5", "v")
         quantize_w("w4")
         quantize_w("w5")
-        gather_scales(2)
-        move_scales(2)
         passes((0,), 0, (0, 1), (2, 3))
         passes((1,), 0, (0, 1), (2, 3))
         finish(0, 0, "s", "late_bias")
@@ -442,7 +466,6 @@ def tile_list_tiert_bias_kernel(
         finish(0, 2, "v")
         finish(0, 3, "v")
         stage("w6", "s")
-        stage("x2a", "s")
         stage("w7", "v")
         quantize_w("w6")
         quantize_w("w7")
@@ -459,6 +482,7 @@ def tile_list_tiert_bias_kernel(
         passes((0,), 0, (6, 7), (2, 3))
         passes((1,), 1, (6, 7), (0, 1))
         passes((1,), 0, (6, 7), (2, 3))
+        stage("x2a", "s")
         stage("x2b", "s")
         finish(1, 6, "s", "late_bias")
         finish(1, 7, "s", "late_bias")

@@ -63,25 +63,22 @@ HOME = {
     "words0": 20 * KIB,
     "staged_w3": 24 * KIB,
     "staged_w1": 26 * KIB,
-    "scales2": 29 * KIB + 512,
     "staged_w4": 24 * KIB + 64,
     "staged_w5": 22 * KIB + 64,
-    "staged_w6": 21 * KIB,
-    "own0_2": 30 * KIB,
-    "staged_w7": 30 * KIB,
-    "staged_x2a": 31 * KIB,
-    "staged_x3": 31 * KIB,
-    "raw_x2b": 35 * KIB,
-    "scales3": 35 * KIB,
-    "words3": 36 * KIB,
-    "raw_w3": 39 * KIB,
-    "late_bias": 39 * KIB,
-    "raw_w6": 43 * KIB,
-    "c_w7": 43 * KIB,
-    "raw_w1": 47 * KIB,
-    "t_c1": 47 * KIB,
-    "own0_4": 51 * KIB,
-    "words2": 51 * KIB,
+    "scales2": 20 * KIB,
+    "staged_w6": 22 * KIB + 576,
+    "staged_w7": 20 * KIB + 576,
+    "staged_x2a": 24 * KIB + 512,
+    "staged_x3": 24 * KIB + 512,
+    "raw_x2b": 30 * KIB,
+    "scales3": 30 * KIB,
+    "words3": 31 * KIB,
+    "raw_w3": 34 * KIB,
+    "late_bias": 34 * KIB,
+    "raw_w1": 38 * KIB,
+    "t_c1": 38 * KIB,
+    "own0_3": 42 * KIB,
+    "words2": 42 * KIB,
 }
 
 
@@ -378,9 +375,9 @@ def tile_list_tiert_bias_kernel(
         load_x("x0b")
         load_wx()
         load_wx_scales()
-        load_b()
         load_x("x1a")
         load_x("x1b")
+        load_b()
         load_w("w0")
         load_table()
         split("x0a", ("x00", "x01"))
@@ -403,7 +400,6 @@ def tile_list_tiert_bias_kernel(
            load_w("w%d" % k)
         load_x("x2a")
         load_x("x2b")
-        load_x("x3")
         decode(0, 2, 6)
         decode(0, 3, 7)
         subtract(0, 2)
@@ -443,9 +439,10 @@ def tile_list_tiert_bias_kernel(
         part_words(0)
         quantize_w("w1")
         part_words(1)
-        quantize_w("w2")
         gather_scales(2)
         move_scales(2)
+        load_x("x3")
+        quantize_w("w2")
         quantize_w("w3")
         stage("w4", "v")
         stage("w5", "v")
@@ -464,10 +461,11 @@ def tile_list_tiert_bias_kernel(
         finish(1, 3, "s", "late_bias")
         passes(table, 0, (2, 3), (2, 3))
         finish(0, 2, "v")
+        stage("w6", "v")
         finish(0, 3, "v")
-        stage("w6", "s")
-        stage("w7", "v")
+        stage("w7", "s")
         quantize_w("w6")
+        gather_words(2)
         quantize_w("w7")
         passes((0,), 1, (4, 5), (4, 5))
         passes((0,), 0, (4, 5), (6, 7))
@@ -476,6 +474,7 @@ def tile_list_tiert_bias_kernel(
         finish(1, 4, "s", "late_bias")
         finish(1, 5, "s", "late_bias")
         finish(0, 4, "v")
+        part_words(2)
         finish(0, 5, "v")
         passes(own, 1, (6, 7), (0, 1))
         passes((0,), 1, (6, 7), (0, 1))
@@ -486,15 +485,14 @@ def tile_list_tiert_bias_kernel(
         stage("x2b", "s")
         finish(1, 6, "s", "late_bias")
         finish(1, 7, "s", "late_bias")
-        gather_words(2)
         first_tier("x2a")
-        part_words(2)
         first_tier("x2b")
         finish(0, 6, "v")
         finish(0, 7, "v")
+        passes((0,), 2, (0, 1), (4, 5))
+        passes((1,), 2, (0, 1), (4, 5))
         decode(2, 0, 6)
         decode(2, 1, 7)
-        passes(table, 2, (0, 1), (4, 5))
         decode(2, 2, 0)
         decode(2, 3, 1)
         for s in range(4):

@@ -61,24 +61,27 @@ HOME = {
     "c_w0": 16 * KIB,
     "raw_x1b": 23 * KIB + 960,
     "words0": 20 * KIB,
-    "staged_w3": 24 * KIB,
-    "staged_w1": 26 * KIB,
-    "staged_w4": 24 * KIB + 64,
-    "staged_w5": 22 * KIB + 64,
-    "scales2": 20 * KIB,
-    "staged_w6": 22 * KIB + 576,
-    "staged_w7": 20 * KIB + 576,
-    "staged_x2a": 24 * KIB + 512,
-    "staged_x3": 24 * KIB + 512,
-    "raw_x2b": 30 * KIB,
-    "scales3": 30 * KIB,
-    "words3": 31 * KIB,
-    "raw_w3": 34 * KIB,
-    "late_bias": 34 * KIB,
-    "raw_w1": 38 * KIB,
-    "t_c1": 38 * KIB,
-    "own0_3": 42 * KIB,
-    "words2": 42 * KIB,
+    "staged_w1": 24 * KIB,
+    "raw_w1": 28 * KIB,
+    "t_c1": 28 * KIB,
+    "staged_w3": 30 * KIB,
+    "scales2": 30 * KIB,
+    "raw_w2": 32 * KIB,
+    "late_bias": 32 * KIB,
+    "raw_w3": 36 * KIB,
+    "staged_w4": 36 * KIB,
+    "raw_w4": 40 * KIB,
+    "staged_w5": 40 * KIB,
+    "staged_w7": 40 * KIB,
+    "own0_2": 44 * KIB,
+    "staged_w6": 44 * KIB,
+    "staged_x2a": 44 * KIB,
+    "staged_x3": 44 * KIB,
+    "own0_3": 48 * KIB,
+    "words2": 48 * KIB,
+    "raw_x2b": 50 * KIB,
+    "scales3": 50 * KIB,
+    "words3": 51 * KIB,
 }
 
 
@@ -134,17 +137,17 @@ def tile_list_tiert_bias_kernel(
             raw["tab"] = placed([P, T], I32, "raw_tab")
             nc.sync.dma_start(raw["tab"][:], tab_words[0].rearrange("p t y -> p (t y)").bitcast(I32))
 
-        def load_table_scales():
+        def load_table_scales(queue=nc.sync):
             for r in range(SCALE_ROWS):
                 rows = tab_scales[:, r:BLOCKS:SCALE_ROWS, :].bitcast(I32).rearrange("a q t -> q a t")
-                nc.sync.dma_start(tab_s[r:P:LIFT, :], rows)
+                queue.dma_start(tab_s[r:P:LIFT, :], rows)
 
         def load_wx():
             nc.sync.dma_start(wx_w[:], wx_words[0].bitcast(I32))
 
-        def load_wx_scales():
+        def load_wx_scales(queue=nc.sync):
             for r in range(SCALE_ROWS):
-                nc.sync.dma_start(wx_s[r:P:QUADRANT, :], wx_scales[0, r:BLOCKS:SCALE_ROWS, :].bitcast(I32))
+                queue.dma_start(wx_s[r:P:QUADRANT, :], wx_scales[0, r:BLOCKS:SCALE_ROWS, :].bitcast(I32))
 
         def runs_out(ap, lo, hi):
             return ap[:, lo:hi, :].rearrange("p (c r) i -> p c i r", r=RUN)
@@ -271,6 +274,19 @@ def tile_list_tiert_bias_kernel(
                 acc[key][:], lhsT=lhsT, lhsT_scale=lhsT_s, rhs=rhs, rhs_scale=rhs_s, start=first, stop=last
             )
 
+        def keep_warm(number, count):
+            spare = bank([P, 2 * P], number)
+            for u in range(count):
+                nc.tensor.matmul_mx(
+                    spare[:],
+                    lhsT=sel_c[:, PAD : PAD + P].bitcast(FP8X4),
+                    lhsT_scale=sel_s[:, 0:P],
+                    rhs=sel_c[:, PAD : PAD + 2 * P].bitcast(FP8X4),
+                    rhs_scale=sel_s[:],
+                    start=True,
+                    stop=True,
+                )
+
         def passes(kinds, c, tiles, banks):
             for m, number in zip(tiles, banks):
                 for kind in kinds:
@@ -320,8 +336,8 @@ def tile_list_tiert_bias_kernel(
         B_STEP = QUADRANT // TILES
         b_rows = placed([P, QUADRANT], F32, "b_rows")
 
-        def load_b():
-            nc.sync.dma_start(b_rows[0:P:B_STEP, :], b.rearrange("(m q j) -> q m j", q=P // QUADRANT, j=QUADRANT))
+        def load_b(queue=nc.sync):
+            queue.dma_start(b_rows[0:P:B_STEP, :], b.rearrange("(m q j) -> q m j", q=P // QUADRANT, j=QUADRANT))
 
         def turn_b():
             cols_of_b["bias"] = placed([P, QUADRANT], F32, "bias")
@@ -334,8 +350,11 @@ def tile_list_tiert_bias_kernel(
             nc.gpsimd.memset(planes[:].rearrange("p u m -> p (u m)").bitcast(I32), 0)
             make_identity(nc, planes[:, 1, :], nomemset=True)
 
-        def lay_selection():
-            nc.vector.tensor_copy(runs_out(sel_in[:, 0, :, :], 0, P), runs_in(planes[:, 1 : PACK + 1, :]))
+        def lay_selection(both=False):
+            if both:
+                nc.scalar.activation(runs_out(sel_in[:, 0, :, :], 0, P), runs_in(planes[:, 1 : PACK + 1, :]), IDENT)
+            else:
+                nc.vector.tensor_copy(runs_out(sel_in[:, 0, :, :], 0, P), runs_in(planes[:, 1 : PACK + 1, :]))
             nc.scalar.activation(runs_out(sel_in[:, 1, :, :], 0, P), runs_in(planes[:, 0:PACK, :]), IDENT)
 
         def quantize_selection():
@@ -431,7 +450,7 @@ def tile_list_tiert_bias_kernel(
         passes(own, 0, (0, 1), (2, 3))
         passes(("q",), 1, (0, 1, 4, 5), (6, 7, 4, 5))
         passes(("r",), 1, (0, 1, 2, 3, 4, 5), (6, 7, 0, 1, 4, 5))
-        for k in range(1, 4):
+        for k in range(1, 3):
            stage("w%d" % k, "s")
         copy_bias("late_bias")
         gather_words(0)
@@ -439,15 +458,14 @@ def tile_list_tiert_bias_kernel(
         part_words(0)
         quantize_w("w1")
         part_words(1)
-        gather_scales(2)
-        move_scales(2)
-        load_x("x3")
+        stage("w3", "v")
         quantize_w("w2")
         quantize_w("w3")
         stage("w4", "v")
-        stage("w5", "v")
+        gather_scales(2)
+        move_scales(2)
+        load_x("x3")
         quantize_w("w4")
-        quantize_w("w5")
         passes((0,), 0, (0, 1), (2, 3))
         passes((1,), 0, (0, 1), (2, 3))
         finish(0, 0, "s", "late_bias")
@@ -455,12 +473,14 @@ def tile_list_tiert_bias_kernel(
         passes(table, 1, (0, 1), (6, 7))
         finish(1, 0, "s", "late_bias")
         finish(1, 1, "s", "late_bias")
+        stage("w5", "s")
         passes((0,), 1, (2, 3), (0, 1))
         passes((1,), 1, (2, 3), (0, 1))
         finish(1, 2, "s", "late_bias")
         finish(1, 3, "s", "late_bias")
         passes(table, 0, (2, 3), (2, 3))
         finish(0, 2, "v")
+        quantize_w("w5")
         stage("w6", "v")
         finish(0, 3, "v")
         stage("w7", "s")

@@ -38,6 +38,20 @@ PAIRS = 1
 STORED_TOGETHER = []
 ALIGN = 64
 KIB = 1024
+LINE = 256
+PHASE = {
+    "xq_c": 0,
+    "xr_c": 0,
+    "t_c": 0,
+    "xq_s": 128,
+    "xr_s": 128,
+    "scales": 128,
+    "low_all": 128,
+    "wx_w": 64,
+    "c_w": 64,
+    "wx_s": 192,
+    "s_w": 192,
+}
 
 X_PIECES = {"x0a": (0, 0, 256), "x0b": (0, 256, 256), "x1a": (1, 0, 256), "x1b": (1, 256, 256), "x2a": (2, 0, 256), "x2b": (2, 256, 256), "x3": (3, 0, 512), "x00": (0, 0, 128), "x01": (0, 128, 128)}
 W_BLOCKS = {"w%d" % (2 * u + a): (a, u * PIECE, PIECE) for u in range(4) for a in range(2)}
@@ -97,8 +111,16 @@ def tile_list_tiert_bias_kernel(
         shared = ctx.enter_context(tc.tile_pool(name="shared", bufs=1))
 
         def placed(shape, dtype, name):
+            phase = [v for k, v in PHASE.items() if name.startswith(k)]
             if name in HOME:
-                return shared.tile(shape, dtype, name=name, align_bytes=ALIGN, offset=HOME[name])
+                at = HOME[name] // LINE * LINE + phase[0] if phase else HOME[name]
+                wide = LINE if at % LINE == 0 else ALIGN
+                return shared.tile(shape, dtype, name=name, align_bytes=wide, offset=at)
+            if phase:
+                size = {U8: 1, U32: 4, I32: 4}[dtype]
+                skip, cols = phase[0] // size, shape[-1] * (shape[1] if len(shape) == 3 else 1)
+                view = keep.tile([P, skip + cols], dtype, name=name, align_bytes=LINE)[:, skip : skip + cols]
+                return view.rearrange("p (a j) -> p a j", a=shape[1]) if len(shape) == 3 else view
             return keep.tile(shape, dtype, name=name, align_bytes=ALIGN)
 
         def bank(shape, number):
@@ -145,8 +167,8 @@ def tile_list_tiert_bias_kernel(
         def load_wx():
             nc.sync.dma_start(wx_w[:], wx_words[0].bitcast(I32))
 
-        def load_wx_scales(queue=nc.sync):
-            for r in range(SCALE_ROWS):
+        def load_wx_scales(queue=nc.sync, rows=range(SCALE_ROWS)):
+            for r in rows:
                 queue.dma_start(wx_s[r:P:QUADRANT, :], wx_scales[0, r:BLOCKS:SCALE_ROWS, :].bitcast(I32))
 
         def runs_out(ap, lo, hi):

from contextlib import ExitStack

import concourse.mybir as mybir
from concourse.masks import make_identity

K, L, N, T, J = 1024, 512, 1024, 4096, 2048
FLOPS = 2 * K * N * J + 2 * 2 * L * N * J + 2 * L * L * J

F32 = mybir.dt.float32
BF16 = mybir.dt.bfloat16
I32 = mybir.dt.int32
U32 = mybir.dt.uint32
U16 = mybir.dt.uint16
U8 = mybir.dt.uint8
FP8X4 = mybir.dt.float8_e4m3fn_x4
FP4X4 = mybir.dt.float4_e2m1fn_x4
IDENT = mybir.ActivationFunctionType.Identity
SUB = mybir.AluOpType.subtract
ADD = mybir.AluOpType.add
MULT = mybir.AluOpType.mult

P = 128
PACK = 4
W = 512
CHUNKS = J // W
TILES = N // P
PARTS = W // P
PIECE = W // 2
RUN = 4
LIST_ROWS = 16
QUADRANT = 32
SCALE_ROWS = 4
BLOCKS = 16
LIFT = 16
RESULTS = 20
PAD = 16
PAIRS = 1
STORED_TOGETHER = []
ALIGN = 64
KIB = 1024
LINE = 256
PHASE = {
    "xq_c": 0,
    "xr_c": 0,
    "t_c": 0,
    "xq_s": 128,
    "xr_s": 128,
    "scales": 128,
    "low_all": 128,
    "wx_w": 64,
    "c_w": 64,
    "wx_s": 192,
    "s_w": 192,
}

X_PIECES = {"x0a": (0, 0, 256), "x0b": (0, 256, 256), "x1a": (1, 0, 256), "x1b": (1, 256, 256), "x2a": (2, 0, 256), "x2b": (2, 256, 256), "x3": (3, 0, 512), "x00": (0, 0, 128), "x01": (0, 128, 128)}
W_BLOCKS = {"w%d" % (2 * u + a): (a, u * PIECE, PIECE) for u in range(4) for a in range(2)}
W_LOADS = {}
S_GROUPS = ((0, 1), (1, 1), (2, 1), (3, 1))
SPLIT = ((0, 2), (0, 3), (0, 4), (0, 5), (0, 6), (0, 7))
STAGED_TOGETHER = [("w1", "w2"), ("x2a", "x2b"), ("x1a", "x1b")]
WORDS_TOGETHER = {0: 2}
HOME = {
    "sel_in": 2 * KIB,
    "staged_x00": 2 * KIB,
    "staged_x01": 3 * KIB,
    "staged_x0b": 0 * KIB + 64,
    "scales0": 2 * KIB + 64,
    "staged_x1a": 3 * KIB + 512,
    "raw_x0a": 8 * KIB,
    "scales1": 8 * KIB,
    "raw_x0b": 12 * KIB,
    "bias": 12 * KIB,
    "raw_x1a": 16 * KIB,
    "c_w0": 16 * KIB,
    "raw_x1b": 23 * KIB + 960,
    "words0": 20 * KIB,
    "staged_w1": 24 * KIB,
    "raw_w1": 28 * KIB,
    "t_c1": 28 * KIB,
    "staged_w3": 30 * KIB,
    "scales2": 30 * KIB,
    "raw_w2": 32 * KIB,
    "late_bias": 32 * KIB,
    "raw_w3": 36 * KIB,
    "staged_w4": 36 * KIB,
    "raw_w4": 40 * KIB,
    "staged_w5": 40 * KIB,
    "staged_w7": 40 * KIB,
    "own0_2": 44 * KIB,
    "staged_w6": 44 * KIB,
    "staged_x2a": 44 * KIB,
    "staged_x3": 44 * KIB,
    "own0_3": 48 * KIB,
    "words2": 48 * KIB,
    "raw_x2b": 50 * KIB,
    "scales3": 50 * KIB,
    "words3": 51 * KIB,
}


def tile_list_tiert_bias_kernel(
    tc, tab_words, tab_scales, wt, x, wx_words, wx_scales, b, offs, out
):
    nc = tc.nc
    with ExitStack() as ctx:
        keep = ctx.enter_context(tc.tile_pool(name="keep", bufs=1))
        outp = ctx.enter_context(tc.tile_pool(name="outp", bufs=RESULTS))
        pairp = ctx.enter_context(tc.tile_pool(name="pairp", bufs=PAIRS))
        psum = ctx.enter_context(tc.psum_pool(name="psum", bufs=1))
        shared = ctx.enter_context(tc.tile_pool(name="shared", bufs=1))

        def placed(shape, dtype, name):
            phase = [v for k, v in PHASE.items() if name.startswith(k)]
            if name in HOME:
                at = HOME[name] // LINE * LINE + phase[0] if phase else HOME[name]
                wide = LINE if at % LINE == 0 else ALIGN
                return shared.tile(shape, dtype, name=name, align_bytes=wide, offset=at)
            if phase:
                size = {U8: 1, U32: 4, I32: 4}[dtype]
                skip, cols = phase[0] // size, shape[-1] * (shape[1] if len(shape) == 3 else 1)
                view = keep.tile([P, skip + cols], dtype, name=name, align_bytes=LINE)[:, skip : skip + cols]
                return view.rearrange("p (a j) -> p a j", a=shape[1]) if len(shape) == 3 else view
            return keep.tile(shape, dtype, name=name, align_bytes=ALIGN)

        def bank(shape, number):
            return psum.tile(shape, F32, name="bank%d" % number)

        offsets = keep.tile([P, J // LIST_ROWS], U16, name="offsets")
        tab_s = placed([P, T // 4], I32, "tab_s")
        wx_w = placed([P, N // 2], I32, "wx_w")
        wx_s = placed([P, N // 4], I32, "wx_s")
        sel_c = placed([P, PAD + PACK * P], U32, "sel_c")
        sel_s = placed([P, 2 * P], U8, "sel_s")
        low_all = placed([P, J // 4], I32, "low_all")
        low_s = [low_all[:, c0 * W // 4 : (c0 + n) * W // 4] for c0, n in S_GROUPS]
        raw, staged, words, rest = {}, {}, {}, {}
        w_c, w_s, xq_c, xq_s, xr_c, xr_s, t_c, t_s = {}, {}, {}, {}, {}, {}, {}, {}
        values, acc, passes_done, own_sum, gathered = {}, {}, {}, {}, {}

        def load_block(key, rows):
            raw[key] = placed([P, PACK, rows.shape[1]], F32, "raw_" + key)
            nc.sync.dma_start(raw[key][:], rows.rearrange("(p i) j -> p i j", i=PACK))

        def load_x(key):
            c, j0, cols = X_PIECES[key]
            load_block(key, x[:, c * W + j0 : c * W + j0 + cols])

        def split(key, parts):
            cols = raw[key].shape[2] // len(parts)
            for u, part in enumerate(parts):
                raw[part] = raw[key][:, :, u * cols : (u + 1) * cols]

        def load_w(key):
            a, n0, cols = W_BLOCKS[key] if key in W_BLOCKS else W_LOADS[key]
            load_block(key, wt[a * W : (a + 1) * W, n0 : n0 + cols])

        def load_table():
            raw["tab"] = placed([P, T], I32, "raw_tab")
            nc.sync.dma_start(raw["tab"][:], tab_words[0].rearrange("p t y -> p (t y)").bitcast(I32))

        def load_table_scales(queue=nc.sync):
            for r in range(SCALE_ROWS):
                rows = tab_scales[:, r:BLOCKS:SCALE_ROWS, :].bitcast(I32).rearrange("a q t -> q a t")
                queue.dma_start(tab_s[r:P:LIFT, :], rows)

        def load_wx():
            nc.sync.dma_start(wx_w[:], wx_words[0].bitcast(I32))

        def load_wx_scales(queue=nc.sync, rows=range(SCALE_ROWS)):
            for r in rows:
                queue.dma_start(wx_s[r:P:QUADRANT, :], wx_scales[0, r:BLOCKS:SCALE_ROWS, :].bitcast(I32))

        def runs_out(ap, lo, hi):
            return ap[:, lo:hi, :].rearrange("p (c r) i -> p c i r", r=RUN)

        def runs_in(ap):
            return ap.rearrange("p i (c r) -> p c i r", r=RUN)

        def stage(key, engine, lo=0, hi=None):
            cols = raw[key].shape[2]
            hi = cols if hi is None else hi
            if key not in staged:
                group = [g for g in STAGED_TOGETHER if key in g] + [(key,)]
                whole = placed([P, len(group[0]) * cols * PACK], BF16, "staged_" + group[0][0])
                for u, member in enumerate(group[0]):
                    share = whole[:, u * cols * PACK : (u + 1) * cols * PACK]
                    staged[member] = share.rearrange("p (j i) -> p j i", i=PACK)
            if engine == "v":
                nc.vector.tensor_copy(runs_out(staged[key], lo, hi), runs_in(raw[key][:, :, lo:hi]))
            elif engine == "s":
                nc.scalar.activation(runs_out(staged[key], lo, hi), runs_in(raw[key][:, :, lo:hi]), IDENT)
            else:
                nc.gpsimd.tensor_scalar(
                    staged[key][:, lo:hi, :], raw[key][:, :, lo:hi].rearrange("p i j -> p j i"), 1.0, 0.0, MULT, ADD
                )

        def quantize(src, codes, scales):
            nc.vector.quantize_mx(codes.bitcast(FP8X4), scales, src.rearrange("p j i -> p (j i)"))

        def listed(first, count):
            return offsets[:, first * W // LIST_ROWS : (first + count) * W // LIST_ROWS]

        def gather_scales(g):
            c0, n = S_GROUPS[g]
            gathered[g] = placed([P, n * W], U8, "scales%d" % g)
            nc.vector.tensor_copy(gathered[g][:], tab_s[:].bitcast(U8).indirect(listed(c0, n)))
            for d in range(n):
                t_s[c0 + d, 0] = gathered[g][:, d * W : (d + 1) * W]
                t_s[c0 + d, 1] = low_s[g].bitcast(U8)[:, d * W : (d + 1) * W]

        def move_scales(g):
            nc.sync.dma_start(low_s[g][0 : P - LIFT, :], gathered[g][LIFT:P, :].bitcast(I32))

        def gather_words(c):
            if c not in words:
                count = WORDS_TOGETHER.get(c, 1)
                whole = placed([P, count * W], U32, "words%d" % c)
                for u in range(count):
                    words[c + u] = whole[:, u * W : (u + 1) * W]
            nc.vector.tensor_copy(words[c], raw["tab"][:].bitcast(U32).indirect(listed(c, 1)))

        def part_words(c):
            t_c[c] = placed([P, 2, 2 * W], U8, "t_c%d" % c)
            nc.vector.tensor_copy(
                t_c[c][:].bitcast(U16), words[c].bitcast(U16).rearrange("p (j a) -> p a j", a=2)
            )

        def quantize_w(key, lo=0, hi=None):
            cols = raw[key].shape[2]
            hi = cols if hi is None else hi
            if key not in w_c:
                w_c[key] = placed([P, cols], U32, "c_" + key)
                w_s[key] = placed([P, cols], U8, "s_" + key)
            quantize(staged[key][:, lo:hi, :], w_c[key][:, lo:hi], w_s[key][:, lo:hi])

        def first_tier(key, lo=0, hi=None):
            c, j0, cols = X_PIECES[key]
            hi = cols if hi is None else hi
            if c not in xq_c:
                xq_c[c] = placed([P, W], U32, "xq_c%d" % c)
                xq_s[c] = placed([P, W], U8, "xq_s%d" % c)
            quantize(staged[key][:, lo:hi, :], xq_c[c][:, j0 + lo : j0 + hi], xq_s[c][:, j0 + lo : j0 + hi])

        def decode(c, s, number):
            cols = slice(s * P, (s + 1) * P)
            values[c, s] = bank([P, PACK, P], number)
            for t in range(PACK):
                nc.tensor.matmul_mx(
                    values[c, s][:, t, :],
                    lhsT=sel_c[:, PAD + t * P : PAD + (t + 1) * P].bitcast(FP8X4),
                    lhsT_scale=sel_s[:, t % 2 * P : (t % 2 + 1) * P],
                    rhs=xq_c[c][:, cols].bitcast(FP8X4),
                    rhs_scale=xq_s[c][:, cols],
                    start=True,
                    stop=True,
                )

        def subtract(c, s):
            if c not in rest:
                rest[c] = placed([P, W, PACK], BF16, "rest%d" % c)
            key = [k for k, (d, j0, n) in X_PIECES.items() if d == c and j0 <= s * P < j0 + n][0]
            j0 = X_PIECES[key][1]
            given = raw[key][:, :, s * P - j0 : (s + 1) * P - j0]
            nc.vector.tensor_tensor(
                runs_out(rest[c], s * P, (s + 1) * P), runs_in(given), runs_in(values[c, s][:]), SUB
            )

        def second_tier(c, lo=0, hi=W):
            if c not in xr_c:
                xr_c[c] = placed([P, W], U32, "xr_c%d" % c)
                xr_s[c] = placed([P, W], U8, "xr_s%d" % c)
            quantize(rest[c][:, lo:hi, :], xr_c[c][:, lo:hi], xr_s[c][:, lo:hi])

        def one_pass(kind, c, m, number, j0=0, n=W):
            own = kind in ("q", "r")
            part = ("own" if own else "table") if (c, m) in SPLIT else "all"
            key = (c, m, j0, part)
            if key not in acc:
                acc[key] = bank([P, n], number)
                passes_done[key] = 0
            first, last = passes_done[key] == 0, passes_done[key] == (3 if part == "all" else 1)
            passes_done[key] = passes_done[key] + 1
            if own:
                codes, scales = (xq_c, xq_s) if kind == "q" else (xr_c, xr_s)
                lhsT = wx_w[:, m * P // 2 : (m + 1) * P // 2].bitcast(FP4X4)
                lhsT_s = wx_s[:, m * P // 4 : (m + 1) * P // 4].bitcast(U8)
                rhs, rhs_s = codes[c][:, j0 : j0 + n].bitcast(FP8X4), scales[c][:, j0 : j0 + n]
            else:
                k = [k for k, (a, n0, cols) in W_BLOCKS.items() if a == kind and n0 <= m * P < n0 + cols][0]
                n0 = W_BLOCKS[k][1]
                cols = slice(m * P - n0, (m + 1) * P - n0)
                lhsT, lhsT_s = w_c[k][:, cols].bitcast(FP8X4), w_s[k][:, cols]
                rhs, rhs_s = t_c[c][:, kind, 2 * j0 : 2 * (j0 + n)].bitcast(FP4X4), t_s[c, kind][:, j0 : j0 + n]
            nc.tensor.matmul_mx(
                acc[key][:], lhsT=lhsT, lhsT_scale=lhsT_s, rhs=rhs, rhs_scale=rhs_s, start=first, stop=last
            )

        def keep_warm(number, count):
            spare = bank([P, 2 * P], number)
            for u in range(count):
                nc.tensor.matmul_mx(
                    spare[:],
                    lhsT=sel_c[:, PAD : PAD + P].bitcast(FP8X4),
                    lhsT_scale=sel_s[:, 0:P],
                    rhs=sel_c[:, PAD : PAD + 2 * P].bitcast(FP8X4),
                    rhs_scale=sel_s[:],
                    start=True,
                    stop=True,
                )

        def passes(kinds, c, tiles, banks):
            for m, number in zip(tiles, banks):
                for kind in kinds:
                    one_pass(kind, c, m, number)

        cols_of_b, results, filled = {}, {}, {}

        def bias_col(name, m):
            return cols_of_b[name][:, B_STEP * m : B_STEP * m + 1]

        def set_aside(c, m, name="bias"):
            own_sum[c, m] = placed([P, W], F32, "own%d_%d" % (c, m))
            nc.scalar.activation(own_sum[c, m][:], acc[c, m, 0, "own"][:], IDENT, bias=bias_col(name, m))

        def finish(c, m, engine, name="bias", j0=0, n=W):
            group = [g for g in STORED_TOGETHER if (c, m) in g]
            if group:
                tiles = group[0]
                if tiles not in results:
                    results[tiles] = pairp.tile([P, len(tiles) * W], F32, name="pair")
                    filled[tiles] = 0
                filled[tiles] = filled[tiles] + 1
                res = results[tiles][:, tiles.index((c, m)) * W : (tiles.index((c, m)) + 1) * W]
            else:
                res = outp.tile([P, n], F32, name="done")[:]
            if (c, m) in SPLIT:
                nc.vector.tensor_tensor(res, acc[c, m, j0, "table"][:], own_sum[c, m][:], ADD)
            elif engine == "v":
                nc.vector.tensor_scalar_add(res, acc[c, m, j0, "all"][:], bias_col(name, m))
            else:
                nc.scalar.activation(res, acc[c, m, j0, "all"][:], IDENT, bias=bias_col(name, m))
            if not group:
                nc.sync.dma_start(out[m * P : (m + 1) * P, c * W + j0 : c * W + j0 + n], res)
            elif filled[tiles] == len(tiles):
                (c0, m0), (c1, m1) = tiles[0], tiles[-1]
                if m0 == m1:
                    rows = out[m0 * P : (m0 + 1) * P, c0 * W : (c1 + 1) * W]
                    nc.sync.dma_start(rows, results[tiles][:])
                else:
                    rows = out[m0 * P : (m1 + 1) * P, c0 * W : (c0 + 1) * W]
                    nc.sync.dma_start(rows.rearrange("(u p) j -> p u j", p=P), results[tiles][:].rearrange("p (u j) -> p u j", j=W))

        def copy_bias(name, src="bias"):
            cols_of_b[name] = placed([P, B_STEP * TILES], F32, name)
            nc.scalar.activation(cols_of_b[name][:], cols_of_b[src][:], IDENT)

        B_STEP = QUADRANT // TILES
        b_rows = placed([P, QUADRANT], F32, "b_rows")

        def load_b(queue=nc.sync):
            queue.dma_start(b_rows[0:P:B_STEP, :], b.rearrange("(m q j) -> q m j", q=P // QUADRANT, j=QUADRANT))

        def turn_b():
            cols_of_b["bias"] = placed([P, QUADRANT], F32, "bias")
            nc.vector.transpose(cols_of_b["bias"][:], b_rows[:])

        planes = placed([P, PACK + 1, P], BF16, "planes")
        sel_in = placed([P, 2, P, PACK], BF16, "sel_in")

        def make_planes():
            nc.gpsimd.memset(planes[:].rearrange("p u m -> p (u m)").bitcast(I32), 0)
            make_identity(nc, planes[:, 1, :], nomemset=True)

        def lay_selection(both=False):
            if both:
                nc.scalar.activation(runs_out(sel_in[:, 0, :, :], 0, P), runs_in(planes[:, 1 : PACK + 1, :]), IDENT)
            else:
                nc.vector.tensor_copy(runs_out(sel_in[:, 0, :, :], 0, P), runs_in(planes[:, 1 : PACK + 1, :]))
            nc.scalar.activation(runs_out(sel_in[:, 1, :, :], 0, P), runs_in(planes[:, 0:PACK, :]), IDENT)

        def quantize_selection():
            nc.vector.quantize_mx(
                sel_c[:, PAD : PAD + 2 * P].bitcast(FP8X4), sel_s[:], sel_in[:].rearrange("p t m i -> p (t m i)")
            )

        def move_selection():
            halves = sel_c[:].bitcast(U16)
            nc.vector.tensor_copy(
                halves[:, 2 * (PAD + 2 * P) : 2 * (PAD + 4 * P)], halves[:, 2 * PAD - 1 : 2 * (PAD + 2 * P) - 1]
            )

        def zero_small():
            nc.vector.memset(wx_s[:], 0)
            nc.vector.memset(b_rows[:], 0.0)
            nc.vector.memset(sel_c[:, 0:PAD].bitcast(I32), 0)
            nc.vector.memset(low_all[P - QUADRANT : P, :], 0)

        def clock(name, ap):
            word = placed([P, 1], I32, "clock_" + name)
            nc.gpsimd.tensor_copy(word[:], ap.bitcast(I32)[:, 0:1])

        table, own = (0, 1), ("q", "r")


        make_planes()
        nc.vector.memset(tab_s[:], 0)
        zero_small()
        lay_selection()
        quantize_selection()
        move_selection()

        nc.sync.dma_start(offsets[:], offs)
        load_x("x0a")
        load_table_scales()
        load_x("x0b")
        load_wx()
        load_wx_scales()
        load_x("x1a")
        load_x("x1b")
        load_b()
        load_w("w0")
        load_table()
        split("x0a", ("x00", "x01"))
        stage("x00", "v")
        stage("x01", "v")
        first_tier("x00")
        first_tier("x01")
        stage("x0b", "s")
        gather_scales(0)
        decode(0, 0, 4)
        decode(0, 1, 5)
        subtract(0, 0)
        subtract(0, 1)
        first_tier("x0b")
        gather_scales(1)
        move_scales(0)
        load_w("w1")
        move_scales(1)
        for k in range(2, 8):
           load_w("w%d" % k)
        load_x("x2a")
        load_x("x2b")
        decode(0, 2, 6)
        decode(0, 3, 7)
        subtract(0, 2)
        subtract(0, 3)
        stage("x1a", "s")
        stage("x1b", "s")
        stage("w0", "s")
        passes(("q",), 0, (4, 5, 6, 7, 2, 3), (0, 1, 2, 3, 4, 5))
        first_tier("x1a")
        turn_b()
        second_tier(0)
        first_tier("x1b")
        decode(1, 0, 6)
        decode(1, 1, 7)
        subtract(1, 0)
        subtract(1, 1)
        passes(("r",), 0, (4, 5, 6), (0, 1, 2))
        decode(1, 2, 6)
        passes(("r",), 0, (7,), (3,))
        decode(1, 3, 7)
        passes(("r",), 0, (2, 3), (4, 5))
        for m in (4, 5, 6, 7, 2, 3):
           set_aside(0, m)
        subtract(1, 2)
        subtract(1, 3)
        quantize_w("w0")
        second_tier(1)
        passes(("q",), 1, (2, 3), (0, 1))
        passes(own, 0, (0, 1), (2, 3))
        passes(("q",), 1, (0, 1, 4, 5), (6, 7, 4, 5))
        passes(("r",), 1, (0, 1, 2, 3, 4, 5), (6, 7, 0, 1, 4, 5))
        for k in range(1, 3):
           stage("w%d" % k, "s")
        copy_bias("late_bias")
        gather_words(0)
        gather_words(1)
        part_words(0)
        quantize_w("w1")
        part_words(1)
        stage("w3", "v")
        quantize_w("w2")
        quantize_w("w3")
        stage("w4", "v")
        gather_scales(2)
        move_scales(2)
        load_x("x3")
        quantize_w("w4")
        passes((0,), 0, (0, 1), (2, 3))
        passes((1,), 0, (0, 1), (2, 3))
        finish(0, 0, "s", "late_bias")
        finish(0, 1, "s", "late_bias")
        passes(table, 1, (0, 1), (6, 7))
        finish(1, 0, "s", "late_bias")
        finish(1, 1, "s", "late_bias")
        stage("w5", "s")
        passes((0,), 1, (2, 3), (0, 1))
        passes((1,), 1, (2, 3), (0, 1))
        finish(1, 2, "s", "late_bias")
        finish(1, 3, "s", "late_bias")
        passes(table, 0, (2, 3), (2, 3))
        finish(0, 2, "v")
        quantize_w("w5")
        stage("w6", "v")
        finish(0, 3, "v")
        stage("w7", "s")
        quantize_w("w6")
        gather_words(2)
        quantize_w("w7")
        passes((0,), 1, (4, 5), (4, 5))
        passes((0,), 0, (4, 5), (6, 7))
        passes((1,), 1, (4, 5), (4, 5))
        passes((1,), 0, (4, 5), (6, 7))
        finish(1, 4, "s", "late_bias")
        finish(1, 5, "s", "late_bias")
        finish(0, 4, "v")
        part_words(2)
        finish(0, 5, "v")
        passes(own, 1, (6, 7), (0, 1))
        passes((0,), 1, (6, 7), (0, 1))
        passes((0,), 0, (6, 7), (2, 3))
        passes((1,), 1, (6, 7), (0, 1))
        passes((1,), 0, (6, 7), (2, 3))
        stage("x2a", "s")
        stage("x2b", "s")
        finish(1, 6, "s", "late_bias")
        finish(1, 7, "s", "late_bias")
        first_tier("x2a")
        first_tier("x2b")
        finish(0, 6, "v")
        finish(0, 7, "v")
        passes((0,), 2, (0, 1), (4, 5))
        passes((1,), 2, (0, 1), (4, 5))
        decode(2, 0, 6)
        decode(2, 1, 7)
        decode(2, 2, 0)
        decode(2, 3, 1)
        for s in range(4):
           subtract(2, s)
        passes(("q",), 2, (0, 1), (4, 5))
        passes(table + ("q",), 2, (2, 3, 4, 5), (2, 3, 6, 7))
        stage("x3", "s")
        second_tier(2)
        gather_scales(3)
        move_scales(3)
        gather_words(3)
        first_tier("x3")
        part_words(3)
        passes(("r",), 2, range(6), (4, 5, 2, 3, 6, 7))
        for m in range(6):
           finish(2, m, "s")
        passes(table + own, 2, (6,), (0,))
        finish(2, 6, "s", "late_bias")
        for s, number in enumerate((4, 5, 2, 3)):
           decode(3, s, number)
           subtract(3, s)
        second_tier(3)
        passes(table + own, 2, (7,), (1,))
        finish(2, 7, "s", "late_bias")
        for kind in table + own:
           passes((kind,), 3, range(4), (6, 7, 0, 4))
        for m in range(4):
           finish(3, m, "vs"[m % 2])
        for m, number in zip((4, 5), (5, 2)):
           passes(table + own, 3, (m,), (number,))
           finish(3, m, "vs"[m % 2])
        for m, j0, n, number, engine in ((6, 0, 256, 3, "v"), (6, 256, 256, 1, "s"), (7, 0, 256, 6, "v"), (7, 256, 128, 7, "s"), (7, 384, 128, 0, "v")):
           for kind in table + own:
               one_pass(kind, 3, m, number, j0, n)
           finish(3, m, engine, j0=j0, n=n)
